import numpy as np, ml_dtypes
CORES = [36,164,52,180,100,228,116,244]
N = 8
BF = ml_dtypes.bfloat16
def gentries(a):
    return np.ascontiguousarray(a.reshape(8, 16, -1).transpose(0, 2, 1)).reshape(8, -1)
def gtable(e):
    e = np.asarray(e); return np.ascontiguousarray(e.reshape(8, -1, 16).transpose(0, 2, 1)).reshape(128, -1).astype(np.int32)
W, L, M, RO = 2048, 256, 16, 4
def base(rng):
    x = rng.integers(0, 256, (N, 8, W, 16)); o = rng.permutation(W); h = W >> 3
    x[:, :, o[:h]] = x[:, :, o[h:2 * h]]
    ring = rng.integers(0, W, (N, 8, 16, L)); o = rng.permutation(L)
    ring[..., o[:4]] = ring[..., o[4:8]]
    return x, ring, rng.integers(0, 32, (N, 8, 16)), rng.integers(0, W >> 1, (N, 8, M))
def pack(x, ring, wt, kap):
    return {"x": np.ascontiguousarray(x.transpose(0, 1, 3, 2)).reshape(N, 128, W).astype(np.float32).astype(BF), "ring": np.ascontiguousarray(ring.reshape(N, 128, L)).astype(np.int32),
            "wt": np.ascontiguousarray(wt.reshape(N, 128, 1)).astype(np.int32), "kap": np.stack([gtable(a) for a in kap])}
def setup_inputs(rng):
    return pack(*base(rng))
def setup_inputs_spread(rng):
    x = np.minimum((np.exp2(8 * rng.random((N, 8, W, 1))) * rng.random((N, 8, W, 16)) * 1.25).astype(np.int64), 255) * (rng.random((N, 8, W, 1)) > 0.0625)
    low = np.minimum((W * rng.random((N, 8, 16, L)) ** 4).astype(np.int64), W - 1)
    ring = np.where(rng.random((N, 8, 1, L)) < 0.5, low, W - 1 - low)
    wt = np.minimum(np.exp2(5.2 * rng.random((N, 8, 16))).astype(np.int64), 31) * (rng.random((N, 8, 16)) > 0.125)
    kap = np.minimum(np.exp2(np.log2(W) * rng.random((N, 8, M))).astype(np.int64) - 1, W // 2 - 1)
    return pack(x, ring, wt, kap)
def setup_inputs_ends(rng):
    x = 255 * rng.integers(0, 2, (N, 8, W, 16)); q = rng.random((N, 8, W)); x[q < 0.25] = 0; x[q >= 0.75] = 255
    wt = 31 * rng.integers(0, 2, (N, 8, 16)); wt[:, 3] = 31; wt[:, 7] = 31; wt[:, 4] = 0
    kap = (W // 2 - 1) * rng.integers(0, 2, (N, 8, M))
    ring = (W - 1) * rng.integers(0, 2, (N, 8, 16, L)); mid = rng.random((N, 8, 16, L)) < 0.2
    for g in (0, 3, 7): mid[:, g] = False
    ring = np.where(mid, rng.integers(0, W, (N, 8, 16, L)), ring)
    c = (((W - 1) ** 2 >> 5) + kap * (W - 1) + (2 * np.arange(M) + 1) * (W - 1)) & (W - 1)
    for r in range(N):
        for g in (0, 3, 7):
            x[r, g, c[r, g]] = 0 if g == 0 else 255
            if g == 3: x[r, g, c[r, g, M - 1], int(rng.integers(0, 16))] = 254
            x[r, g, W - 1] = 0; x[r, g, 0] = 255
            for i in (2, 5, L - 1): ring[r, g, :2, i] = W - 1
            for i in (1, 8, L - 2): ring[r, g, :2, i] = 0
    return pack(x, ring, wt, kap)
def setup_inputs_corners(rng):
    x, ring, wt, kap = base(rng)
    for f_ in (0, 15): x[..., f_] = 32 * rng.integers(0, 8, (N, 8, W)) + rng.choice(np.array([0, 15, 16, 31, 1, 14, 17, 30]), (N, 8, W))
    for r in range(N):
        for g in range(8):
            k = (r + g) % 4; wt[r, g] = 31 if k == 2 else 0
            if k == 0: wt[r, g, 0] = 1
            if k == 3: wt[r, g, 15] = 1
            k = (r + g // 2) % 3; kap[r, g] = 0 if k == 0 else W // 2 - 1 if k == 1 else rng.choice(np.array([0, 1, W // 2 - 2, W // 2 - 1]), M)
    kind = rng.integers(0, 6, (N, 8, 1, L)); turn = (W - 1) * (np.arange(16) & 1)[None, None, :, None]
    ring = np.where(kind == 1, ring[:, :, :1], ring); ring = np.where(kind == 2, 0, ring); ring = np.where(kind == 3, W - 1, ring); ring = np.where(kind == 4, turn, ring)
    return pack(x, ring, wt, kap)
def setup_inputs_crowd(rng):
    x, ring, wt, kap = base(rng); wt[...] = 0; wt[..., 0] = 1; ring = np.minimum(ring, W - 2)
    i = int(rng.choice(np.array([0, L // 2, L - 1]))); sel = rng.integers(0, 4, L); o = 1 + rng.permutation(W - 2)
    for r in range(N):
        k = 3 if r == 3 else r % 3; up = 16 if k < 2 else 0
        x[r, ..., 0] = (x[r, ..., 0] & 3) + 2 if k == 3 else (x[r, ..., 0] & 239) + up
        for g in (0, 1): ring[r, g] = np.repeat(ring[r, g, :, :1].copy(), L, axis=1)
        ring[r, 1, :, i] = rng.integers(0, W - 1, 16)
        ring[r, 4] = ring[r, 4][:, sel]
        for g in (2, 3, 5, 7):
            v = int(rng.integers(1, W - 1)); x[r, g, v] = 0; x[r, g, v, 0] = 5 + up
            ring[r, g, 1] = v; ring[r, g, 5] = 0; kap[r, g] = 0
            if g in (3, 5): ring[r, g, 5, i] = int(rng.integers(1, W - 1))
        x[r, 6, :, 1] &= 127; x[r, 6, 0] = 0; x[r, 6, 0, 1] = 64; x[r, 6, o[0], 0] = 5 + up; x[r, 6, o[1], 0] = 6 + up
        ring[r, 6, 0] = o[0]; ring[r, 6, 1] = o[1]; ring[r, 6, 5] = 0; ring[r, 6, 6] = rng.permutation(o[2:])[:L]
        if k == 1: x[r, 6, W - 1, 0] = 5; ring[r, 6, 0, L - 1] = W - 1
        if k == 3: x[r, 4, W - 1, 0] = 16; ring[r, 4, 1, rng.permutation(L)[:int(rng.integers(1, 64))]] = W - 1
    return pack(x, ring, wt, kap)
def setup_inputs_ties(rng):
    x, ring, wt, kap = base(rng); pool = rng.integers(0, 256, (N, 8, 5, 16)); pool[:, :, 4] = (pool[:, :, 0] + pool[:, :, 1]) & 255
    pool[:, ::2, 3] = pool[:, ::2, 2] ^ 1
    x = np.take_along_axis(pool, rng.integers(0, 5, (N, 8, W, 1)), 2)
    for g in (1, 4, 7):
        ring[:, g] = rng.integers(0, 64, (N, 16, L))
        x[:, g, :64] = rng.integers(0, 4, (N, 64, 16)); x[:, g, 64:] = rng.integers(240, 256, (N, W - 64, 16))
    return pack(x, ring, wt, kap)
def check_inputs(d):
    bad = []
    for k, lo, hi in (("x", 0, 255), ("ring", 0, W - 1), ("wt", 0, 31), ("kap", 0, W // 2 - 1)):
        a = np.asarray(d[k]).astype(np.float32)
        if not (np.min(a) >= lo and np.max(a) <= hi): bad.append("range of " + k)
        elif np.any(a != np.floor(a)): bad.append("whole numbers of " + k)
    return bad
def pick(X, ix):
    return np.take_along_axis(X, ix[..., None], 2)
def reference(x, ring, wt, kap):
    X = np.ascontiguousarray(x.astype(np.float32).astype(np.int32).reshape(N, 8, 16, W).transpose(0, 1, 3, 2))
    R = ring.astype(np.int64).reshape(N, 8, 16, L); wts = wt.astype(np.int32).reshape(N, 8, 1, 16)
    kp = np.stack([gentries(a) for a in kap]).astype(np.int64)[:, :, None, :]; odd = 2 * np.arange(M) + 1
    A = np.zeros(N, np.int64)
    for t in range(RO):
        far = np.stack([R[(r + 1 + t % (N - 1)) % N] for r in range(N)])
        both = np.concatenate([R, far], axis=2)
        a = (np.add.reduce(pick(X, R[:, :, 0]) * wts, axis=3) & 31).astype(np.int64)
        b = (np.add.reduce(pick(X, R[:, :, 1]) * wts, axis=3) & 31).astype(np.int64)
        P = np.take_along_axis(both, a[:, :, None, :], 2)[:, :, 0]; Q = np.take_along_axis(both, b[:, :, None, :], 2)[:, :, 0]
        y = (pick(X, P) + pick(X, Q)) & 255
        c = (((P * Q) >> 5)[..., None] + kp * P[..., None] + odd * Q[..., None] + A[:, None, None, None]) & (W - 1)
        s = np.add.reduce(np.abs(pick(X, c.reshape(N, 8, L * M)).reshape(N, 8, L, M, 16) - y[:, :, :, None, :]), axis=4)
        m = np.argmin(s, axis=3)
        e = np.take_along_axis(c, m[..., None], 3)[..., 0]
        A = np.add.reduce(((a >= 16).astype(np.int64) + (b >= 16)).reshape(N, 8 * L), axis=1) & 63
        for r in range(N):
            for g in range(8):
                v, i = np.unique(e[r, g], return_index=True)
                X[r, g, v] = (X[r, g, v] + y[r, g, i]) >> 1
        R = np.concatenate([e[:, :, None, :], R[:, :, :15]], axis=2)
    return {"yx": np.ascontiguousarray(X.transpose(0, 1, 3, 2)).reshape(N, 128, W).astype(np.float32).astype(BF), "yr": R.reshape(N, 128, L).astype(np.float32)}

@@ -1,0 +1,492 @@
+from concourse.bass import DstId, RemoteDMATransfer
+from concourse.mybir import AluOpType as A, AxisListType, ActivationFunctionType as F
+
+N, RO = 8, 4
+KS = 4
+CA = 9
+BF, H, FL, I32, U16 = "bfloat16", "float16", "float32", "int32", "uint16"
+
+
+def _sb(n, d):
+    return ("sbuf", [128, n], d)
+
+
+SCRATCH = {
+    "X": _sb(2048 + 16 * KS, BF), "RI": _sb(256, I32), "WI": _sb(1, I32), "KI": _sb(1, I32),
+    "RF": _sb(272, FL), "TR": _sb(512, FL), "TL": _sb(16, U16),
+    "T0": _sb(560, FL), "T1": _sb(560, FL), "T2": _sb(560, FL), "T3": _sb(560, FL),
+    "CI": _sb(16, I32), "CF": _sb(32, FL), "AGE": _sb(16, I32),
+    "JL": _sb(256, BF), "IG": _sb(256, BF), "H2": _sb(64, BF), "J": _sb(192, BF), "Q4": _sb(64, BF), "KAQ": _sb(256, BF),
+    "SEL": _sb(576, BF), "ONES": _sb(128, BF), "C1024": _sb(16 * CA, BF),
+    "DM": _sb(256, BF), "NDM": _sb(256, BF), "QC": _sb(256, BF), "PEN": _sb(256, BF), "BON": _sb(128, BF),
+    "ID": _sb(18 * 128, BF), "KM": _sb(2048, H), "KD": _sb(16, H),
+    "HP": _sb(64, BF), "KB": _sb(64, BF), "KBQ": _sb(128, BF), "KT": _sb(128, BF),
+    "EU": _sb(96, U16), "G01": _sb(512, BF), "HS": _sb(64, I32), "HA": _sb(32, I32),
+    "OFF": _sb(32, U16), "FO": _sb(32, BF), "GP": _sb(256, H), "SP": _sb(256, H), "GQ": _sb(256, FL), "SQ": _sb(256, FL),
+    "OP": _sb(16, U16), "OQ": _sb(16, U16), "Q16": _sb(16, H), "PQ": _sb(16, I32), "FI": _sb(16, I32), "F16": _sb(16, H),
+    "XP": _sb(256, BF), "XQ": _sb(256, BF), "SG": _sb(256, BF), "Y": _sb(512, BF),
+    "CR": _sb(256, I32), "C32": _sb(256, I32), "CU": _sb(256, U16),
+    "D": _sb(4096, BF), "AB": _sb(4096, BF),
+    "R0": _sb(64, FL), "R1": _sb(64, FL), "R2": _sb(64, FL), "R3": _sb(32, FL), "R4": _sb(16, FL),
+    "L0": _sb(64, FL), "L1": _sb(64, FL), "L2": _sb(64, FL), "SC": _sb(64, I32),
+    "MA": _sb(16, I32), "OM": _sb(16, U16),
+    "GE": _sb(256, H), "SE": _sb(256, H), "EQ": _sb(256 * KS, BF), "LS": _sb(256, FL), "OF": _sb(16, FL), "OS": _sb(16, U16),
+    "B4K": _sb(128, BF), "DUI": _sb(16, I32), "DUT": _sb(16, FL),
+    "XE": _sb(256, BF), "N1": _sb(256, FL), "NX": _sb(256, BF), "EB": _sb(256, FL),
+}
+for _n in ("PH", "PC0", "PC1", "PY", "PD0", "PD1", "PK0", "PK1"):
+    SCRATCH[_n] = ("psum", [128, 512], FL)
+
+SEMAPHORES = (["v", "s", "p", "gp", "sent", "lr", "lx", "lw", "lk", "cp", "yr0", "yxa", "yxb"]
+              + ["arr%d" % k for k in range(RO)] + ["ce%d" % k for k in range(RO)] + ["ye%d" % k for k in range(RO)])
+
+MAGIC = 12582912.0
+
+
+def rank_program(g, core, T, topo):
+    rank = T.rank_of(core)
+    if rank is None:
+        return
+    Q = {"v": g.vector, "s": g.scalar, "p": g.tensor, "gp": g, "y": g.sync}
+    cnt = {}
+    waited = {}
+    lastw = {}
+    readers = {}
+
+    def need(q, sem, val):
+        if waited.get((q, sem), 0) < val:
+            Q[q].wait_ge(T.sem[sem], val)
+            waited[(q, sem)] = val
+
+    def deps(q, r, w, loose=False):
+        for k in r:
+            t = lastw.get(k)
+            if t and not (t[0] == q and (q == "p" or not t[3])):
+                need(q, t[1], t[2])
+        for k in w:
+            t = lastw.get(k)
+            if t and not (t[0] == q and (q == "p" or loose or not t[3])):
+                need(q, t[1], t[2])
+            for t in readers.get(k, []):
+                if not (t[0] == q == "p"):
+                    need(q, t[1], t[2])
+
+    def note(q, sem, val, r, w):
+        for k in r:
+            if k[:2] == "P:":
+                lastw[k] = (q, sem, val, False)
+            else:
+                readers.setdefault(k, []).append((q, sem, val))
+        for k in w:
+            lastw[k] = (q, sem, val, True)
+            readers[k] = []
+
+    def op(q, fn, r, w, loose=False):
+        deps(q, r, w, loose)
+        cnt[q] = cnt.get(q, 0) + 1
+        fn().then_inc(T.sem[q], 1)
+        note(q, q, cnt[q], r, w)
+
+    def dmas(q, sem, items):
+        for o, i, r, w in items:
+            deps(q, r, w)
+        for o, i, r, w in items:
+            Q[q].dma_start(o, i).then_inc(T.sem[sem], 16)
+        cnt[sem] = cnt.get(sem, 0) + 16 * len(items)
+        for o, i, r, w in items:
+            note("dma", sem, cnt[sem], r, w)
+
+    V, S, P = g.vector, g.scalar, g.tensor
+
+    def cp(o, i, r, w, loose=False):
+        op("v", lambda: V.tensor_copy(o, i), r, w, loose)
+
+    def ts(o, i, s1, o1, r, w, s2=None, o2=None):
+        if o2 is None:
+            op("v", lambda: V.tensor_scalar(o, i, s1, None, o1), r, w)
+        else:
+            op("v", lambda: V.tensor_scalar(o, i, s1, s2, o1, o2), r, w)
+
+    def tt(o, a, b, o1, r, w):
+        op("v", lambda: V.tensor_tensor(o, a, b, o1), r, w)
+
+    def scan(o, d0, d1, init, o0, o1, r, w):
+        op("v", lambda: V.tensor_tensor_scan(o, d0, d1, init, o0, o1), r, w)
+
+    def ms(o, c, w):
+        op("v", lambda: V.memset(o, c), [], w)
+
+    def act(o, i, f, r, w, bias=0.0, scale=1.0):
+        op("s", lambda: S.activation(o, i, f, bias=bias, scale=scale), r, w)
+
+    def mm(o, l, x, st, sp, r, w):
+        op("p", lambda: P.matmul(o, l, x, st, sp), r, w)
+
+    def iota(o, pat, base, cm, w, small=True):
+        if small:
+            op("gp", lambda: g.iota(o, pat, base, cm, allow_small_or_imprecise_dtypes=True), [], w)
+        else:
+            op("gp", lambda: g.iota(o, pat, base, cm), [], w)
+
+    TT = [T.T0, T.T1, T.T2, T.T3]
+    XW = T.X[:, 0:2048]
+
+    def ci(k):
+        return T.CI[:, k:k + 1]
+
+    def cf(k):
+        return T.CF[:, k:k + 1]
+
+    def idm(k):
+        return T.ID[:, 128 * k:128 * (k + 1)]
+
+    def sel(which, shift):
+        return T.SEL[:, 144 * which + shift:144 * which + shift + 128]
+
+    def peer(s):
+        return T.cores[(rank - 1 - s) % N]
+
+    def send(items, r):
+        for k in r:
+            t = lastw[k]
+            need("gp", t[1], t[2])
+        trs, tot = [], 0
+        for j, (s, src, dst) in enumerate(items):
+            d = peer(s)
+            eng = topo.engines(core, d)
+            n = share(len(items), len(eng))
+            mask = 0
+            for e in eng[j * n:(j + 1) * n]:
+                mask += 1 << e
+            rid, pid = topo.addr(d, core)
+            trs.append(RemoteDMATransfer(dst_ids=[DstId(rid=rid, pnc=pid)], dma_engine_mask=mask,
+                                         remote_sem=T.sem["arr%d" % s], src=src, dst=dst))
+            tot += n
+        g.remote_dma_fused(trs, local_sem=T.sem["sent"])
+        cnt["sent"] = cnt.get("sent", 0) + tot
+
+    def share(k, n):
+        m = 1
+        while 2 * m * k <= n:
+            m *= 2
+        return m
+
+    def arrivals(s):
+        n = len(topo.engines(T.cores[(rank + 1 + s) % N], core))
+        if s == 0:
+            return share(1, n)
+        return share(RO - 1, n) + share(1, n) + sum(share(RO - 2 - t, n) for t in range(s - 1))
+
+    dmas("y", "lr", [(T.RI[:], T.ring[:], [], ["RI"])])
+    dmas("y", "lx", [(XW, T.x[:], [], ["X"])])
+    dmas("s", "lw", [(T.WI[:], T.wt[:], [], ["WI"])])
+    dmas("s", "lk", [(T.KI[:], T.kap[:], [], ["KI"])])
+
+    iota(ci(0), [[0, 1]], 0, 1, ["q"], small=False)
+    iota(T.AGE[:], [[1, 16]], 0, 0, ["AGE"], small=False)
+    iota(T.JL[:], [[0, 16], [1, 16]], 0, 0, ["JL"])
+    iota(T.IG[:], [[1, 16], [0, 16]], 0, 0, ["IG"])
+    iota(T.H2[:], [[0, 32], [1, 2]], 0, 0, ["H2"])
+    GF, PF, WW, B1, B2, W16, P8, P4, DUM, QF, KF, AN, AC = 0, 1, 2, 3, 4, 5, 6, 7, 8, 9, 10, 11, 12
+    ms(T.SEL[:], 0.0, ["SEL0", "SEL1", "SEL2", "SEL3"])
+    ts(ci(1), ci(0), 4, A.arith_shift_right, ["q"], ["g32"])
+    ts(ci(2), ci(0), 15, A.bitwise_and, ["q"], ["p32"])
+    ts(ci(3), ci(0), 31, A.bitwise_and, ["q"], ["x32"])
+    tt(ci(4), ci(0), ci(1), A.add, ["q", "g32"], ["t32"])
+    cp(cf(PF), ci(2), ["p32"], ["pf"])
+    ts(cf(WW), ci(3), 16.0, A.is_equal, ["x32"], ["ww"], 256.0, A.mult)
+    ts(ci(5), ci(4), 1, A.bitwise_and, ["t32"], ["b0"])
+    cp(cf(GF), ci(1), ["g32"], ["gf"])
+    ts(cf(B1), cf(PF), 16.0, A.mult, ["pf", "ww"], ["b1"], cf(WW), A.add)
+    ts(ci(6), ci(2), 3, A.arith_shift_right, ["p32"], ["p8i"])
+    ts(cf(B2), ci(5), 240.0, A.mult, ["b0", "b1"], ["b2"], cf(B1), A.add)
+    ts(ci(7), ci(2), 2, A.arith_shift_right, ["p32"], ["p4i"])
+    ts(T.TL[:], T.AGE[:], cf(B2), A.add, ["AGE", "b2"], ["TL"])
+    cp(cf(P8), ci(6), ["p8i"], ["p8"])
+    cp(cf(P4), ci(7), ["p4i"], ["p4"])
+    cp(T.RF[:, 0:256], T.RI[:], ["RI"], ["RFa"])
+    cp(T.RF[:, 256:272], T.RI[:, 0:16], ["RI"], ["RFb"])
+    op("v", lambda: V.transpose(T.TR[:, 0:256], T.RF[:, 0:256]), ["RFa"], ["TRa"])
+    op("v", lambda: V.transpose(T.TR[:, 256:512], T.RF[:, 16:272]), ["RFa", "RFb"], ["TRb"])
+    ts(T.DM[:], T.JL[:, 0:256], cf(PF), A.is_equal, ["JL", "pf"], ["DM"])
+    cp(T.T0[:, 0:256], T.TR[:].indirect(T.TL[:]), ["TRa", "TRb", "TL"], ["T0own"])
+    send([(0, T.T0[:, 0:256], T.T0[:, 256:512])], ["T0own"])
+    iota(T.J[:], [[1, 192]], 0, 0, ["J"])
+    iota(T.Q4[:], [[0, 16], [1, 4]], 0, 0, ["Q4"])
+    iota(T.KAQ[:], [[16, 4], [1, 16], [0, 4]], 192, 0, ["KAQ"])
+    iota(T.DUI[:], [[0, 16 // KS], [16, KS]], 2048, 0, ["DUI"], small=False)
+    need("gp", "arr0", arrivals(0))
+    send([(s, T.T0[:, 0:256], TT[s][:, 256 + 16 * s:512 + 16 * s]) for s in range(1, RO)], ["T0own"])
+    dmas("y", "cp", [(TT[s][:, 16 * s:256], T.T0[:, 0:256 - 16 * s], ["T0own"], ["T%down" % s]) for s in range(1, RO)])
+    dmas("y", "yr0", [(T.yr[4:128, :], T.RF[0:124, 0:256], ["RFa"], ["yr"])])
+
+    ts(T.BON[:], T.IG[:, 0:128], cf(GF), A.is_equal, ["IG", "gf"], ["BON"])
+    ts(cf(W16), T.WI[:], 16.0, A.mult, ["WI"], ["w16"])
+    cp(T.EU[:, 64:96], T.T0[:, 0:32], ["T0own"], ["EU0", "EU-1"])
+    tt(idm(0), T.DM[:, 0:128], T.BON[:], A.mult, ["DM", "BON"], ["ID0"])
+    ts(T.SEL[:, 432 + 7:432 + 128:8], T.IG[:, 0:128:8], cf(GF), A.is_equal, ["IG", "gf", "w16"], ["SEL3"], cf(W16), A.mult)
+    ts(T.HP[:], T.H2[:], cf(P8), A.not_equal, ["H2", "p8"], ["HP"], -4194304.0, A.mult)
+    cp(cf(KF), T.KI[:], ["KI"], ["kf"])
+
+    def late_scalar():
+        act(idm(17), idm(0), F.Copy, ["ID0"], ["ID17"], scale=-128.0)
+        act(idm(16), idm(0), F.Copy, ["ID0"], ["ID16"], scale=-1.0)
+        for m in range(1, 16):
+            act(idm(m), idm(0), F.Copy, ["ID0"], ["ID%d" % m], scale=float(2 * m + 1))
+
+    def mid_vector():
+        ts(T.KD[:], T.DM[:, 0:16], cf(KF), A.mult, ["DM", "kf"], ["KD"])
+        mm(T.PK1[:, 0:16], T.BON[:], T.KD[:], True, True, ["BON", "KD"], ["P:K1"])
+        ms(T.ONES[:], 1.0, ["ONES"])
+        ts(T.NDM[:], T.JL[:], cf(PF), A.not_equal, ["JL", "pf"], ["NDM"])
+
+    def late_vector():
+        ts(T.QC[:], T.DM[:], 68157440.0, A.mult, ["DM"], ["QC"], -1048576.0, A.add)
+        ts(cf(QF), cf(PF), -1048576.0, A.mult, ["pf"], ["qf"], 15728640.0, A.add)
+        ms(T.C1024[:], 1024.0, ["C1024"])
+        ms(cf(AC), -1024.0, ["ac0"])
+        for m in range(16):
+            ts(T.KM[:, 128 * m:128 * (m + 1)], idm(0), T.PK1[:, m:m + 1], A.mult, ["ID0", "P:K1"], ["KM%d" % m])
+
+    def last_vector():
+        ts(T.SEL[:, 15:128:16], T.IG[:, 0:128:16], cf(GF), A.is_equal, ["IG", "gf"], ["SEL0"], 256.0, A.mult)
+        ts(T.SEL[:, 144 + 3:144 + 128:4], T.IG[:, 0:128:4], cf(GF), A.is_equal, ["IG", "gf"], ["SEL1"], 512.0, A.mult)
+        ts(T.SEL[:, 288 + 3:288 + 128:4], T.IG[:, 0:128:4], cf(GF), A.is_equal, ["IG", "gf"], ["SEL2"], -256.0, A.mult)
+        ts(T.KB[:], T.JL[:, 0:64], -1048576.0, A.mult, ["JL"], ["KB"], 15728640.0, A.add)
+        ts(T.KT[:, 0:64], T.Q4[:], cf(P4), A.not_equal, ["Q4", "p4"], ["KTa"], 33554432.0, A.mult)
+        ts(T.KT[:, 64:128], T.IG[:, 0:256:4], -1048576.0, A.mult, ["IG"], ["KTb"], 15728640.0, A.add)
+        ts(T.PEN[:], T.DM[:], -4096.0, A.mult, ["DM"], ["PEN"])
+        tt(T.KBQ[:, 0:64], T.KT[:, 0:64], T.KT[:, 64:128], A.max, ["KTa", "KTb"], ["KBQa"])
+        tt(T.KBQ[:, 64:128], T.KT[:, 0:64], T.KT[:, 64:128], A.max, ["KTa", "KTb"], ["KBQb"])
+        ts(cf(DUM), cf(PF), 1048577.0, A.mult, ["pf"], ["dum"], -15728640.0, A.add)
+        ts(T.B4K[:], T.BON[:], 4096.0, A.mult, ["BON"], ["B4K"])
+        ts(T.DUT[:], T.DUI[:], cf(DUM), A.add, ["DUI", "dum"], ["DUT"])
+
+    def eu(k):
+        return T.EU[:, 64 - 16 * k:80 - 16 * k]
+
+    def hash_open():
+        mm(T.PH[:, 0:64], idm(0), T.HP[:], True, False, ["ID0", "HP"], ["P:H"])
+        mm(T.PH[:, 0:32], idm(0), T.IG[:, 0:256:8], False, False, ["ID0", "IG"], ["P:H"])
+        mm(T.PH[:, 32:64], idm(0), T.IG[:, 0:256:8], False, False, ["ID0", "IG"], ["P:H"])
+
+    def dk(a, b):
+        return ["D%d" % m for m in range(a, b)]
+
+    def ak(a, b):
+        return ["AB%d" % m for m in range(a, b)]
+
+    def cuk(a, b):
+        return (["CUa"] if a < CA else []) + (["CUb"] if b > CA else [])
+
+    def vgather(a, b):
+        tt(T.D[:, 256 * a:256 * b], XW.indirect(T.CU[:, 16 * a:16 * b]), T.Y[:, 0:256 * (b - a)], A.subtract,
+           ["X", "Ya"] + (["Yb"] if b - a > 1 else []) + cuk(a, b), dk(a, b))
+
+    def vrelu(a, b):
+        ts(T.AB[:, 256 * a:256 * b], T.D[:, 256 * a:256 * b], 0.0, A.max, dk(a, b), ak(a, b))
+
+    def sabs(a, b):
+        act(T.AB[:, 256 * a:256 * b], T.D[:, 256 * a:256 * b], F.Abs, dk(a, b), ak(a, b))
+
+    def dense_open(bank, key, a):
+        mm(bank[:, 0:64], idm(0), T.KB[:], True, False, ["ID0", "KB"], [key])
+        mm(bank[:, 0:64], idm(0), T.J[:, 16 * a:16 * a + 64], False, False, ["ID0", "J"], [key])
+
+    def dense(bank, key, a):
+        for p in range(16):
+            mm(bank[:, 0:64], sel(0, 15 - p), T.AB[:, 256 * a + p:256 * (a + 4):16], False, p == 15,
+               ["SEL0"] + ak(a, a + 4), [key])
+
+    def quad_open(bank, key, a, b):
+        n = 64 * (b - a)
+        mm(bank[:, 0:n], idm(0), T.KBQ[:, 0:n], True, False, ["ID0", "KBQa", "KBQb"], [key])
+        mm(bank[:, 0:n], idm(0), T.KAQ[:, 64 * (a - 12):64 * (b - 12)], False, False, ["ID0", "KAQ"], [key])
+
+    def quad(bank, key, a, b, part):
+        n = 64 * (b - a)
+        for k in range(4):
+            if part == 0:
+                mm(bank[:, 0:n], sel(2, 3 - k), T.D[:, 256 * a + k:256 * b:4], False, False, ["SEL2"] + dk(a, b), [key])
+            else:
+                mm(bank[:, 0:n], sel(1, 3 - k), T.AB[:, 256 * a + k:256 * b:4], False, k == 3, ["SEL1"] + ak(a, b), [key])
+
+    hash_open()
+    for t in range(RO):
+        Tt = TT[t]
+        last = t == RO - 1
+        cp(T.G01[:, 0:256], XW.indirect(eu(t)), ["X", "EU%d" % t], ["G0"])
+        act(T.G01[:, 256:512], XW.indirect(eu(t - 1)), F.Copy, ["X", "EU%d" % (t - 1)], ["G1"])
+        for k in range(8):
+            mm(T.PH[:, 0:64], sel(3, 7 - k), T.G01[:, k:512:8], False, k == 7, ["SEL3", "G0", "G1"], ["P:H"])
+        if t == 0:
+            mid_vector()
+            late_scalar()
+        scan(T.HS[:], T.H2[:], T.PH[:, 0:64], 0.0, A.mult, A.max, ["H2", "P:H"], ["HS"])
+        ts(T.HA[:], T.HS[:, 1:64:2], 511, A.bitwise_and, ["HS"], ["HA"])
+        cp(T.OFF[:], T.HA[:], ["HA"], ["OFF"])
+        if not last:
+            ts(T.FO[:], T.HA[:], 256.0, A.is_ge, ["HA"], ["FO"])
+            mm(T.PH[:, 64:96], T.ONES[:], T.FO[:], True, True, ["ONES", "FO"], ["P:H"])
+        if t == 0:
+            late_vector()
+        na, nb = 16 * CA, 256 - 16 * CA
+        mm(T.PC0[:, 0:na], idm(0), T.C1024[:, 0:na], True, False, ["ID0", "C1024"], ["P:C0"])
+        mm(T.PC1[:, 0:nb], idm(0), T.C1024[:, 0:nb], True, False, ["ID0", "C1024"], ["P:C1"])
+        need("v", "arr%d" % t, arrivals(t))
+        need("s", "arr%d" % t, arrivals(t))
+        tk = ["T%down" % t] + ["T%de%d" % (t, u) for u in range(t)]
+        tt(T.GP[:], Tt[:, 0:512].indirect(T.OFF[:, 0:16]), T.DM[:], A.mult, tk + ["OFF", "DM"], ["GP"])
+        act(T.GQ[:], Tt[:, 0:512].indirect(T.OFF[:, 16:32]), F.Copy, tk + ["OFF"], ["GQ"])
+        if not last:
+            op("v", lambda: V.tensor_reduce(cf(AN), T.PH[:, 64:96], AxisListType.X, A.add), ["P:H"], ["an"])
+        scan(T.SP[:], T.NDM[:, 0:256], T.GP[:], 0.0, A.mult, A.add, ["NDM", "GP"], ["SP"])
+        if not last:
+            cp(ci(8), cf(AN), ["an"], ["ai"])
+        P16 = T.SP[:, 15:256:16]
+        cp(T.OP[:], P16, ["SP"], ["OP"])
+        scan(T.SQ[:], T.QC[:], T.GQ[:], 0.0, A.add, A.min, ["QC", "GQ"], ["SQ"])
+        act(T.XP[:], XW.indirect(T.OP[:]), F.Copy, ["X", "OP"], ["XP"])
+
+        def pc(m):
+            if m < CA:
+                return T.PC0[:, 16 * m:16 * m + 16], "P:C0"
+            return T.PC1[:, 16 * (m - CA):16 * (m - CA) + 16], "P:C1"
+
+        for m in range(16):
+            o, k = pc(m)
+            mm(o, T.KM[:, 128 * m:128 * (m + 1)], P16, False, False, ["KM%d" % m, "SP"], [k])
+        if not last:
+            ts(ci(9), ci(8), 63, A.bitwise_and, ["ai"], ["aj"])
+        ts(T.OQ[:], T.SQ[:, 15:256:16], cf(QF), A.add, ["SQ", "qf"], ["OQ"])
+        ts(T.Q16[:], T.SQ[:, 15:256:16], cf(QF), A.add, ["SQ", "qf"], ["Q16"])
+        act(T.XQ[:], XW.indirect(T.OQ[:]), F.Copy, ["X", "OQ"], ["XQ"])
+        if not last:
+            ts(cf(AC + t + 1), ci(9), -1024.0, A.add, ["aj"], ["ac%d" % (t + 1)])
+        tt(T.PQ[:], P16, T.Q16[:], A.mult, ["SP", "Q16"], ["PQ"])
+        ts(T.FI[:], T.PQ[:], 5, A.arith_shift_right, ["PQ"], ["FI"], 2047, A.bitwise_and)
+        ts(T.F16[:], T.FI[:], cf(AC + t), A.add, ["FI", "ac%d" % t], ["F16"])
+        mm(T.PY[:, 0:256], idm(0), T.XP[:], True, False, ["ID0", "XP"], ["P:Y"])
+        mm(T.PD0[:, 0:256], idm(0), T.XP[:], True, False, ["ID0", "XP"], ["P:D0"])
+        for m in range(CA):
+            o, k = pc(m)
+            mm(o, idm(m), T.Q16[:], False, False, ["ID%d" % m, "Q16"], [k])
+        mm(T.PY[:, 0:256], idm(0), T.XQ[:], False, True, ["ID0", "XQ"], ["P:Y"])
+        for m in range(CA):
+            o, k = pc(m)
+            mm(o, idm(0), T.F16[:], False, m == CA - 1, ["ID0", "F16"], [k])
+        act(T.SG[:], T.PY[:, 0:256], F.Sign, ["P:Y"], ["SG"], bias=-255.5)
+        mm(T.PD0[:, 0:256], idm(0), T.XQ[:], False, False, ["ID0", "XQ"], ["P:D0"])
+        mm(T.PD0[:, 0:256], idm(17), T.SG[:], False, True, ["ID17", "SG"], ["P:D0"])
+        for m in range(CA, 16):
+            o, k = pc(m)
+            mm(o, idm(m), T.Q16[:], False, False, ["ID%d" % m, "Q16"], [k])
+            mm(o, idm(0), T.F16[:], False, m == 15, ["ID0", "F16"], [k])
+        act(T.Y[:, 0:256], T.PD0[:, 0:256], F.Identity, ["P:D0"], ["Ya"], bias=-128.0)
+        act(T.Y[:, 256:512], T.PD0[:, 0:256], F.Identity, ["P:D0"], ["Yb"], bias=-128.0)
+        if t == 0:
+            last_vector()
+        cp(T.CR[:, 0:na], T.PC0[:, 0:na], ["P:C0"], ["CRa"])
+        ts(T.C32[:, 0:na], T.CR[:, 0:na], 2047, A.bitwise_and, ["CRa"], ["C32a"])
+        cp(T.CU[:, 0:na], T.C32[:, 0:na], ["C32a"], ["CUa"])
+        dense_open(T.PK0, "P:K0", 0)
+        dense_open(T.PK1, "P:K1", 4)
+        quad_open(T.PC0, "P:C0", 12, 13)
+        act(T.D[:, 0:512], XW.indirect(T.CU[:, 0:32]), F.Copy, ["X", "CUa"], dk(0, 2))
+        act(T.D[:, 512:1024], XW.indirect(T.CU[:, 32:64]), F.Copy, ["X", "CUa"], dk(2, 4))
+        for h, bank in enumerate((T.PD0, T.PD1)):
+            mm(bank[:], idm(16), T.Y[:], True, False, ["ID16", "Ya", "Yb"], ["P:D%d" % h])
+            mm(bank[:], idm(0), T.D[:, 512 * h:512 * h + 512], False, True, ["ID0"] + dk(2 * h, 2 * h + 2), ["P:D%d" % h])
+        vgather(4, 5)
+        cp(T.CR[:, na:256], T.PC1[:, 0:nb], ["P:C1"], ["CRb"])
+        quad_open(T.PC1, "P:C1", 13, 15)
+        vgather(5, 7)
+        ts(T.C32[:, na:256], T.CR[:, na:256], 2047, A.bitwise_and, ["CRb"], ["C32b"])
+        for h, bank in enumerate((T.PD0, T.PD1)):
+            act(T.AB[:, 512 * h:512 * h + 512], bank[:], F.Abs, ["P:D%d" % h], ak(2 * h, 2 * h + 2))
+        dense(T.PK0, "P:K0", 0)
+        quad_open(T.PD0, "P:D0", 15, 16)
+        vgather(7, 9)
+        cp(T.CU[:, na:256], T.C32[:, na:256], ["C32b"], ["CUb"])
+        sabs(4, 8)
+        dense(T.PK1, "P:K1", 4)
+        vgather(9, 11)
+        vgather(11, 13)
+        sabs(8, 12)
+        cp(T.R0[:], T.PK0[:, 0:64], ["P:K0"], ["R0"])
+        dense_open(T.PK0, "P:K0", 8)
+        vrelu(12, 13)
+        quad(T.PC0, "P:C0", 12, 13, 0)
+        quad(T.PC0, "P:C0", 12, 13, 1)
+        vgather(13, 15)
+        dense(T.PK0, "P:K0", 8)
+        quad(T.PC1, "P:C1", 13, 15, 0)
+        tt(T.R1[:], T.PK1[:, 0:64], T.R0[:], A.min, ["P:K1", "R0"], ["R1"])
+        vrelu(13, 15)
+        quad(T.PC1, "P:C1", 13, 15, 1)
+        vgather(15, 16)
+        quad(T.PD0, "P:D0", 15, 16, 0)
+        cp(T.L0[:], T.PC0[:, 0:64], ["P:C0"], ["L0"])
+        vrelu(15, 16)
+        quad(T.PD0, "P:D0", 15, 16, 1)
+        mm(T.PH[:, 0:256], idm(0), T.PEN[:], True, False, ["ID0", "PEN"], ["P:H"])
+        mm(T.PY[:, 0:128], idm(0), T.Y[:, 128:256], True, False, ["ID0", "Ya"], ["P:Y"])
+        mm(T.PD1[:, 0:128], idm(0), T.Y[:, 0:128], True, False, ["ID0", "Ya"], ["P:D1"])
+        tt(T.R2[:], T.PK0[:, 0:64], T.R1[:], A.min, ["P:K0", "R1"], ["R2"])
+        tt(T.L1[:], T.PC1[:, 0:64], T.L0[:], A.min, ["P:C1", "L0"], ["L1"])
+        tt(T.R3[:], T.R2[:, 0:32], T.R2[:, 32:64], A.min, ["R2"], ["R3"])
+        tt(T.L2[:], T.PC1[:, 64:128], T.L1[:], A.min, ["P:C1", "L1"], ["L2"])
+        tt(T.R4[:], T.R3[:, 0:16], T.R3[:, 16:32], A.min, ["R3"], ["R4"])
+        tt(T.L2[:, 0:64:4], T.L2[:, 0:64:4], T.R4[:], A.min, ["L2", "R4"], ["L2"])
+        scan(T.SC[:], T.L2[:], T.PD0[:, 0:64], 67108864.0, A.min, A.min, ["L2", "P:D0"], ["SC"])
+        ts(T.MA[:], T.SC[:, 3:64:4], 255, A.bitwise_and, ["SC"], ["MA"])
+        cp(T.OM[:], T.MA[:], ["MA"], ["OM"])
+        tt(T.GE[:, 0:256], T.C32[:].indirect(T.OM[:]), T.DM[:], A.mult, ["C32a", "C32b", "OM", "DM"], ["GE"])
+        mm(T.PH[:, 0:256], T.BON[:], T.GE[:], False, True, ["BON", "GE"], ["P:H"])
+        mm(T.PK1[:, 0:256], T.BON[:], T.GE[:], True, True, ["BON", "GE"], ["P:K1"])
+        mm(T.PC0[:, 0:256], T.BON[:], T.GE[:], True, False, ["BON", "GE"], ["P:C0"])
+        scan(T.SE[:], T.NDM[:], T.GE[:], -1.0, A.mult, A.add, ["NDM", "GE"], ["SE"])
+        E16 = T.SE[:, 15:256:16]
+        ek = "EU%d" % (t + 1)
+        cp(eu(t + 1), E16, ["SE"], [ek])
+        if not last:
+            k1 = "T%de%d" % (t + 1, t)
+            cp(TT[t + 1][:, 0:16], E16, ["SE"], [k1])
+            src = TT[t + 1][:, 0:16]
+            far = [(s, src, TT[s][:, 256 + 16 * (s - 1 - t):272 + 16 * (s - 1 - t)]) for s in range(t + 1, RO)]
+            send(far[:1], [k1])
+            if t + 2 < RO:
+                send(far[1:], [k1])
+                dmas("y", "ce%d" % t, [(TT[s][:, 16 * (s - 1 - t):16 * (s - t)], src, [k1], ["T%de%d" % (s, t)])
+                                       for s in range(t + 2, RO)])
+        for k in range(KS):
+            n = 256 - 16 * k
+            bank, key = (T.PH, "P:H") if k == 0 else (T.PK1, "P:K1")
+            tt(T.EQ[:, 256 * k:256 * k + n], bank[:, 16 * k:256], T.SE[:, 0:n], A.is_equal, [key, "SE"], ["EQ%d" % k])
+        halves = ((1, T.PY, "P:Y"), (0, T.PD1, "P:D1"))
+        for h, bank, k in halves:
+            act(T.XE[:, 128 * h:128 * h + 128], XW.indirect(eu(t + 1)[:, 8 * h:8 * h + 8]), F.Copy, ["X", ek], ["XE%d" % h])
+        for k in range(KS):
+            mm(T.PC0[:, 16 * k:256], T.B4K[:], T.EQ[:, 256 * k:256 * k + 256 - 16 * k], False, k == KS - 1,
+               ["B4K", "EQ%d" % k], ["P:C0"])
+            if k < 2:
+                h, bank, key = halves[k]
+                mm(bank[:, 0:128], idm(0), T.XE[:, 128 * h:128 * h + 128], False, True, ["ID0", "XE%d" % h], [key])
+        for h, bank, k in halves:
+            act(T.N1[:, 128 * h:128 * h + 128], bank[:, 0:128], F.Identity, [k], ["N1%d" % h], bias=MAGIC, scale=0.4995)
+        for h in (1, 0):
+            act(T.NX[:, 128 * h:128 * h + 128], T.N1[:, 128 * h:128 * h + 128], F.Identity, ["N1%d" % h], ["NX%d" % h], bias=-MAGIC)
+        act(T.EB[:], T.PK1[:, 0:256], F.Copy, ["P:K1"], ["EB"])
+        dmas("y", "ye%d" % t, [(T.yr[RO - 1 - t:128:16, :], T.EB[0:128:16, :], ["EB"], ["yr"])])
+        if not last:
+            hash_open()
+        scan(T.LS[:], T.QC[:], T.PC0[:, 0:256], 0.0, A.add, A.min, ["QC", "P:C0"], ["LS"])
+        tt(T.OF[:], T.LS[:, 15:256:16], T.DUT[:], A.min, ["LS", "DUT"], ["OF"])
+        ts(T.OS[:], T.OF[:], cf(QF), A.add, ["OF", "qf"], ["OS"])
+        for c in range(16 - KS, -1, -KS):
+            cp(T.X[:].indirect(T.OS[:, c:c + KS]), T.NX[:, 16 * c:16 * (c + KS)], ["OS", "NX%d" % (c // 8)], ["X"])
+
+    dmas("y", "yxa", [(T.yx[0:64, :], T.X[0:64, 0:2048], ["X"], ["yxa"])])
+    dmas("s", "yxb", [(T.yx[64:128, :], T.X[64:128, 0:2048], ["X"], ["yxb"])])
+    for sem in sorted(cnt):
+        need("gp", sem, cnt[sem])

@@ -3,7 +3,8 @@ from concourse.mybir import AluOpType as A, AxisListType, ActivationFunctionType
 
 N, RO = 8, 4
 KS = 4
-CA = 9
+PA = 8
+CA = 8
 BF, H, FL, I32, U16 = "bfloat16", "float16", "float32", "int32", "uint16"
 
 
@@ -16,19 +17,19 @@ SCRATCH = {
     "RF": _sb(272, FL), "TR": _sb(512, FL), "TL": _sb(16, U16),
     "T0": _sb(560, FL), "T1": _sb(560, FL), "T2": _sb(560, FL), "T3": _sb(560, FL),
     "CI": _sb(16, I32), "CF": _sb(32, FL), "AGE": _sb(16, I32),
-    "JL": _sb(256, BF), "IG": _sb(256, BF), "H2": _sb(64, BF), "J": _sb(192, BF), "Q4": _sb(64, BF), "KAQ": _sb(256, BF),
-    "SEL": _sb(576, BF), "ONES": _sb(128, BF), "C1024": _sb(16 * CA, BF),
+    "JL": _sb(256, BF), "IG": _sb(256, BF), "H2": _sb(64, BF), "J": _sb(128, BF), "Q4": _sb(256, BF), "KAQ": _sb(512, BF),
+    "SEL": _sb(720, BF), "ONES": _sb(128, BF), "C1024": _sb(16 * max(CA, 16 - CA), BF),
     "DM": _sb(256, BF), "NDM": _sb(256, BF), "QC": _sb(256, BF), "PEN": _sb(256, BF), "BON": _sb(128, BF),
-    "ID": _sb(18 * 128, BF), "KM": _sb(2048, H), "KD": _sb(16, H),
-    "HP": _sb(64, BF), "KB": _sb(64, BF), "KBQ": _sb(128, BF), "KT": _sb(128, BF),
+    "ID": _sb(17 * 128, BF), "KM": _sb(2048, H), "KD": _sb(16, H),
+    "HP": _sb(64, BF), "KB": _sb(64, BF), "KBQ": _sb(256, BF), "KT": _sb(512, BF),
     "EU": _sb(96, U16), "G01": _sb(512, BF), "HS": _sb(64, I32), "HA": _sb(32, I32),
     "OFF": _sb(32, U16), "FO": _sb(32, BF), "GP": _sb(256, H), "SP": _sb(256, H), "GQ": _sb(256, FL), "SQ": _sb(256, FL),
     "OP": _sb(16, U16), "OQ": _sb(16, U16), "Q16": _sb(16, H), "PQ": _sb(16, I32), "FI": _sb(16, I32), "F16": _sb(16, H),
     "XP": _sb(256, BF), "XQ": _sb(256, BF), "SG": _sb(256, BF), "Y": _sb(512, BF),
     "CR": _sb(256, I32), "C32": _sb(256, I32), "CU": _sb(256, U16),
     "D": _sb(4096, BF), "AB": _sb(4096, BF),
-    "R0": _sb(64, FL), "R1": _sb(64, FL), "R2": _sb(64, FL), "R3": _sb(32, FL), "R4": _sb(16, FL),
-    "L0": _sb(64, FL), "L1": _sb(64, FL), "L2": _sb(64, FL), "SC": _sb(64, I32),
+    "R0": _sb(64, FL), "R1": _sb(64, FL), "R3": _sb(32, FL), "TH": _sb(512, H),
+    "L0": _sb(256, FL), "LB": _sb(256, FL), "SC": _sb(256, I32),
     "MA": _sb(16, I32), "OM": _sb(16, U16),
     "GE": _sb(256, H), "SE": _sb(256, H), "EQ": _sb(256 * KS, BF), "LS": _sb(256, FL), "OF": _sb(16, FL), "OS": _sb(16, U16),
     "B4K": _sb(128, BF), "DUI": _sb(16, I32), "DUT": _sb(16, FL),
@@ -188,7 +189,7 @@ def rank_program(g, core, T, topo):
     iota(T.IG[:], [[1, 16], [0, 16]], 0, 0, ["IG"])
     iota(T.H2[:], [[0, 32], [1, 2]], 0, 0, ["H2"])
     GF, PF, WW, B1, B2, W16, P8, P4, DUM, QF, KF, AN, AC = 0, 1, 2, 3, 4, 5, 6, 7, 8, 9, 10, 11, 12
-    ms(T.SEL[:], 0.0, ["SEL0", "SEL1", "SEL2", "SEL3"])
+    ms(T.SEL[:], 0.0, ["SEL0", "SEL1", "SEL2", "SEL3", "SEL4"])
     ts(ci(1), ci(0), 4, A.arith_shift_right, ["q"], ["g32"])
     ts(ci(2), ci(0), 15, A.bitwise_and, ["q"], ["p32"])
     ts(ci(3), ci(0), 31, A.bitwise_and, ["q"], ["x32"])
@@ -209,12 +210,14 @@ def rank_program(g, core, T, topo):
     op("v", lambda: V.transpose(T.TR[:, 0:256], T.RF[:, 0:256]), ["RFa"], ["TRa"])
     op("v", lambda: V.transpose(T.TR[:, 256:512], T.RF[:, 16:272]), ["RFa", "RFb"], ["TRb"])
     ts(T.DM[:], T.JL[:, 0:256], cf(PF), A.is_equal, ["JL", "pf"], ["DM"])
-    cp(T.T0[:, 0:256], T.TR[:].indirect(T.TL[:]), ["TRa", "TRb", "TL"], ["T0own"])
-    send([(0, T.T0[:, 0:256], T.T0[:, 256:512])], ["T0own"])
-    iota(T.J[:], [[1, 192]], 0, 0, ["J"])
-    iota(T.Q4[:], [[0, 16], [1, 4]], 0, 0, ["Q4"])
-    iota(T.KAQ[:], [[16, 4], [1, 16], [0, 4]], 192, 0, ["KAQ"])
+    cp(T.TH[:, 0:256], T.TR[:].indirect(T.TL[:]), ["TRa", "TRb", "TL"], ["TH"])
+    send([(0, T.TH[:, 0:256], T.TH[:, 256:512])], ["TH"])
+    cp(T.T0[:, 0:256], T.TH[:, 0:256], ["TH"], ["T0own"])
+    iota(T.Q4[:], [[0, 16], [1, 4], [0, 4]], 0, 0, ["Q4"])
     iota(T.DUI[:], [[0, 16 // KS], [16, KS]], 2048, 0, ["DUI"], small=False)
+    iota(T.J[:], [[1, 128]], 0, 0, ["J"])
+    iota(T.KAQ[:, 0:256], [[1, 16], [0, 4], [16, 4]], 128, 0, ["KAQ0"])
+    iota(T.KAQ[:, 256:512], [[1, 16], [0, 4], [16, 4]], 192, 0, ["KAQ1"])
     need("gp", "arr0", arrivals(0))
     send([(s, T.T0[:, 0:256], TT[s][:, 256 + 16 * s:512 + 16 * s]) for s in range(1, RO)], ["T0own"])
     dmas("y", "cp", [(TT[s][:, 16 * s:256], T.T0[:, 0:256 - 16 * s], ["T0own"], ["T%down" % s]) for s in range(1, RO)])
@@ -229,7 +232,6 @@ def rank_program(g, core, T, topo):
     cp(cf(KF), T.KI[:], ["KI"], ["kf"])
 
     def late_scalar():
-        act(idm(17), idm(0), F.Copy, ["ID0"], ["ID17"], scale=-128.0)
         act(idm(16), idm(0), F.Copy, ["ID0"], ["ID16"], scale=-1.0)
         for m in range(1, 16):
             act(idm(m), idm(0), F.Copy, ["ID0"], ["ID%d" % m], scale=float(2 * m + 1))
@@ -253,11 +255,12 @@ def rank_program(g, core, T, topo):
         ts(T.SEL[:, 144 + 3:144 + 128:4], T.IG[:, 0:128:4], cf(GF), A.is_equal, ["IG", "gf"], ["SEL1"], 512.0, A.mult)
         ts(T.SEL[:, 288 + 3:288 + 128:4], T.IG[:, 0:128:4], cf(GF), A.is_equal, ["IG", "gf"], ["SEL2"], -256.0, A.mult)
         ts(T.KB[:], T.JL[:, 0:64], -1048576.0, A.mult, ["JL"], ["KB"], 15728640.0, A.add)
-        ts(T.KT[:, 0:64], T.Q4[:], cf(P4), A.not_equal, ["Q4", "p4"], ["KTa"], 33554432.0, A.mult)
-        ts(T.KT[:, 64:128], T.IG[:, 0:256:4], -1048576.0, A.mult, ["IG"], ["KTb"], 15728640.0, A.add)
+        ts(T.SEL[:, 576 + 3:576 + 128:4], T.IG[:, 0:128:4], cf(GF), A.is_equal, ["IG", "gf"], ["SEL4"], 256.0, A.mult)
+        ts(T.KT[:, 0:256], T.Q4[:], cf(P4), A.not_equal, ["Q4", "p4"], ["KTa"], 33554432.0, A.mult)
+        ts(T.KT[:, 256:512], T.IG[:], -1048576.0, A.mult, ["IG"], ["KTb"], 15728640.0, A.add)
         ts(T.PEN[:], T.DM[:], -4096.0, A.mult, ["DM"], ["PEN"])
-        tt(T.KBQ[:, 0:64], T.KT[:, 0:64], T.KT[:, 64:128], A.max, ["KTa", "KTb"], ["KBQa"])
-        tt(T.KBQ[:, 64:128], T.KT[:, 0:64], T.KT[:, 64:128], A.max, ["KTa", "KTb"], ["KBQb"])
+        ms(T.LB[:], 67108864.0, ["LB"])
+        tt(T.KBQ[:], T.KT[:, 0:256], T.KT[:, 256:512], A.max, ["KTa", "KTb"], ["KBQ"])
         ts(cf(DUM), cf(PF), 1048577.0, A.mult, ["pf"], ["dum"], -15728640.0, A.add)
         ts(T.B4K[:], T.BON[:], 4096.0, A.mult, ["BON"], ["B4K"])
         ts(T.DUT[:], T.DUI[:], cf(DUM), A.add, ["DUI", "dum"], ["DUT"])
@@ -298,18 +301,16 @@ def rank_program(g, core, T, topo):
             mm(bank[:, 0:64], sel(0, 15 - p), T.AB[:, 256 * a + p:256 * (a + 4):16], False, p == 15,
                ["SEL0"] + ak(a, a + 4), [key])
 
-    def quad_open(bank, key, a, b):
-        n = 64 * (b - a)
-        mm(bank[:, 0:n], idm(0), T.KBQ[:, 0:n], True, False, ["ID0", "KBQa", "KBQb"], [key])
-        mm(bank[:, 0:n], idm(0), T.KAQ[:, 64 * (a - 12):64 * (b - 12)], False, False, ["ID0", "KAQ"], [key])
+    def quad_open(bank, key, j):
+        mm(bank[:, 0:256], idm(0), T.KBQ[:], True, False, ["ID0", "KBQ"], [key])
+        mm(bank[:, 0:256], idm(0), T.KAQ[:, 256 * j:256 * j + 256], False, False, ["ID0", "KAQ%d" % j], [key])
 
-    def quad(bank, key, a, b, part):
-        n = 64 * (b - a)
+    def quad(m, src, which):
+        bank, key = (T.PC0, "P:C0") if m < 12 else (T.PC1, "P:C1")
+        rk = dk(m, m + 1) if which == 2 else ak(m, m + 1)
         for k in range(4):
-            if part == 0:
-                mm(bank[:, 0:n], sel(2, 3 - k), T.D[:, 256 * a + k:256 * b:4], False, False, ["SEL2"] + dk(a, b), [key])
-            else:
-                mm(bank[:, 0:n], sel(1, 3 - k), T.AB[:, 256 * a + k:256 * b:4], False, k == 3, ["SEL1"] + ak(a, b), [key])
+            mm(bank[:, m % 4:256:4], sel(which, 3 - k), src[:, 256 * m + k:256 * m + 256:4], False,
+               k == 3 and m % 4 == 3 and which != 2, ["SEL%d" % which] + rk, [key])
 
     hash_open()
     for t in range(RO):
@@ -330,121 +331,128 @@ def rank_program(g, core, T, topo):
             mm(T.PH[:, 64:96], T.ONES[:], T.FO[:], True, True, ["ONES", "FO"], ["P:H"])
         if t == 0:
             late_vector()
+            last_vector()
         na, nb = 16 * CA, 256 - 16 * CA
         mm(T.PC0[:, 0:na], idm(0), T.C1024[:, 0:na], True, False, ["ID0", "C1024"], ["P:C0"])
         mm(T.PC1[:, 0:nb], idm(0), T.C1024[:, 0:nb], True, False, ["ID0", "C1024"], ["P:C1"])
         need("v", "arr%d" % t, arrivals(t))
-        need("s", "arr%d" % t, arrivals(t))
         tk = ["T%down" % t] + ["T%de%d" % (t, u) for u in range(t)]
+        if t == 0:
+            cp(T.T0[:, 256:512], T.TH[:, 256:512], [], ["T0far"])
+            tk.append("T0far")
+        else:
+            need("s", "arr%d" % t, arrivals(t))
         tt(T.GP[:], Tt[:, 0:512].indirect(T.OFF[:, 0:16]), T.DM[:], A.mult, tk + ["OFF", "DM"], ["GP"])
         act(T.GQ[:], Tt[:, 0:512].indirect(T.OFF[:, 16:32]), F.Copy, tk + ["OFF"], ["GQ"])
         if not last:
             op("v", lambda: V.tensor_reduce(cf(AN), T.PH[:, 64:96], AxisListType.X, A.add), ["P:H"], ["an"])
+        scan(T.SQ[:], T.QC[:], T.GQ[:], 0.0, A.add, A.min, ["QC", "GQ"], ["SQ"])
         scan(T.SP[:], T.NDM[:, 0:256], T.GP[:], 0.0, A.mult, A.add, ["NDM", "GP"], ["SP"])
         if not last:
             cp(ci(8), cf(AN), ["an"], ["ai"])
         P16 = T.SP[:, 15:256:16]
-        cp(T.OP[:], P16, ["SP"], ["OP"])
-        scan(T.SQ[:], T.QC[:], T.GQ[:], 0.0, A.add, A.min, ["QC", "GQ"], ["SQ"])
-        act(T.XP[:], XW.indirect(T.OP[:]), F.Copy, ["X", "OP"], ["XP"])
 
         def pc(m):
             if m < CA:
                 return T.PC0[:, 16 * m:16 * m + 16], "P:C0"
             return T.PC1[:, 16 * (m - CA):16 * (m - CA) + 16], "P:C1"
 
-        for m in range(16):
-            o, k = pc(m)
-            mm(o, T.KM[:, 128 * m:128 * (m + 1)], P16, False, False, ["KM%d" % m, "SP"], [k])
-        if not last:
-            ts(ci(9), ci(8), 63, A.bitwise_and, ["ai"], ["aj"])
+        def cpart(which, ms_):
+            for m in ms_:
+                o, k = pc(m)
+                if which == "P":
+                    mm(o, T.KM[:, 128 * m:128 * (m + 1)], P16, False, False, ["KM%d" % m, "SP"], [k])
+                elif which == "Q":
+                    mm(o, idm(m), T.Q16[:], False, False, ["ID%d" % m, "Q16"], [k])
+                else:
+                    mm(o, idm(0), T.F16[:], False, m in (CA - 1, 15), ["ID0", "F16"], [k])
+
+        cpart("P", range(PA))
         ts(T.OQ[:], T.SQ[:, 15:256:16], cf(QF), A.add, ["SQ", "qf"], ["OQ"])
         ts(T.Q16[:], T.SQ[:, 15:256:16], cf(QF), A.add, ["SQ", "qf"], ["Q16"])
         act(T.XQ[:], XW.indirect(T.OQ[:]), F.Copy, ["X", "OQ"], ["XQ"])
+        cp(T.OP[:], P16, ["SP"], ["OP"])
+        if not last:
+            ts(ci(9), ci(8), 63, A.bitwise_and, ["ai"], ["aj"])
+        tt(T.PQ[:], P16, T.Q16[:], A.mult, ["SP", "Q16"], ["PQ"])
+        cp(T.XP[:], XW.indirect(T.OP[:]), ["X", "OP"], ["XP"])
+        ts(T.FI[:], T.PQ[:], 5, A.arith_shift_right, ["PQ"], ["FI"], 2047, A.bitwise_and)
         if not last:
             ts(cf(AC + t + 1), ci(9), -1024.0, A.add, ["aj"], ["ac%d" % (t + 1)])
-        tt(T.PQ[:], P16, T.Q16[:], A.mult, ["SP", "Q16"], ["PQ"])
-        ts(T.FI[:], T.PQ[:], 5, A.arith_shift_right, ["PQ"], ["FI"], 2047, A.bitwise_and)
         ts(T.F16[:], T.FI[:], cf(AC + t), A.add, ["FI", "ac%d" % t], ["F16"])
-        mm(T.PY[:, 0:256], idm(0), T.XP[:], True, False, ["ID0", "XP"], ["P:Y"])
-        mm(T.PD0[:, 0:256], idm(0), T.XP[:], True, False, ["ID0", "XP"], ["P:D0"])
-        for m in range(CA):
-            o, k = pc(m)
-            mm(o, idm(m), T.Q16[:], False, False, ["ID%d" % m, "Q16"], [k])
-        mm(T.PY[:, 0:256], idm(0), T.XQ[:], False, True, ["ID0", "XQ"], ["P:Y"])
-        for m in range(CA):
-            o, k = pc(m)
-            mm(o, idm(0), T.F16[:], False, m == CA - 1, ["ID0", "F16"], [k])
-        act(T.SG[:], T.PY[:, 0:256], F.Sign, ["P:Y"], ["SG"], bias=-255.5)
-        mm(T.PD0[:, 0:256], idm(0), T.XQ[:], False, False, ["ID0", "XQ"], ["P:D0"])
-        mm(T.PD0[:, 0:256], idm(17), T.SG[:], False, True, ["ID17", "SG"], ["P:D0"])
-        for m in range(CA, 16):
-            o, k = pc(m)
-            mm(o, idm(m), T.Q16[:], False, False, ["ID%d" % m, "Q16"], [k])
-            mm(o, idm(0), T.F16[:], False, m == 15, ["ID0", "F16"], [k])
-        act(T.Y[:, 0:256], T.PD0[:, 0:256], F.Identity, ["P:D0"], ["Ya"], bias=-128.0)
-        act(T.Y[:, 256:512], T.PD0[:, 0:256], F.Identity, ["P:D0"], ["Yb"], bias=-128.0)
-        if t == 0:
-            last_vector()
+        cpart("Q", range(CA))
+        mm(T.PY[:, 0:256], idm(0), T.XQ[:], True, False, ["ID0", "XQ"], ["P:Y"])
+        mm(T.PY[:, 0:256], idm(0), T.XP[:], False, True, ["ID0", "XP"], ["P:Y"])
+        cpart("F", range(CA))
+        cpart("P", range(PA, 16))
+        cpart("Q", range(CA, 16))
+        cpart("F", range(CA, 16))
+        ts(T.SG[:], T.PY[:, 0:256], 256.0, A.is_ge, ["P:Y"], ["SG"], -256.0, A.mult)
         cp(T.CR[:, 0:na], T.PC0[:, 0:na], ["P:C0"], ["CRa"])
+        tt(T.Y[:, 0:256], T.PY[:, 0:256], T.SG[:], A.add, ["P:Y", "SG"], ["Ya"])
+        act(T.Y[:, 256:512], T.Y[:, 0:256], F.Copy, ["Ya"], ["Yb"])
         ts(T.C32[:, 0:na], T.CR[:, 0:na], 2047, A.bitwise_and, ["CRa"], ["C32a"])
         cp(T.CU[:, 0:na], T.C32[:, 0:na], ["C32a"], ["CUa"])
+
+        def sgather(h, a, bank):
+            act(T.D[:, 256 * a:256 * a + 512], XW.indirect(T.CU[:, 16 * a:16 * a + 32]), F.Copy, ["X"] + cuk(a, a + 2), dk(a, a + 2))
+            mm(bank[:], idm(16), T.Y[:], True, False, ["ID16", "Ya", "Yb"], ["P:D%d" % h])
+            mm(bank[:], idm(0), T.D[:, 256 * a:256 * a + 512], False, True, ["ID0"] + dk(a, a + 2), ["P:D%d" % h])
+
         dense_open(T.PK0, "P:K0", 0)
         dense_open(T.PK1, "P:K1", 4)
-        quad_open(T.PC0, "P:C0", 12, 13)
-        act(T.D[:, 0:512], XW.indirect(T.CU[:, 0:32]), F.Copy, ["X", "CUa"], dk(0, 2))
-        act(T.D[:, 512:1024], XW.indirect(T.CU[:, 32:64]), F.Copy, ["X", "CUa"], dk(2, 4))
-        for h, bank in enumerate((T.PD0, T.PD1)):
-            mm(bank[:], idm(16), T.Y[:], True, False, ["ID16", "Ya", "Yb"], ["P:D%d" % h])
-            mm(bank[:], idm(0), T.D[:, 512 * h:512 * h + 512], False, True, ["ID0"] + dk(2 * h, 2 * h + 2), ["P:D%d" % h])
-        vgather(4, 5)
+        sgather(0, 0, T.PD0)
+        vgather(4, 6)
         cp(T.CR[:, na:256], T.PC1[:, 0:nb], ["P:C1"], ["CRb"])
-        quad_open(T.PC1, "P:C1", 13, 15)
-        vgather(5, 7)
+        sgather(1, 2, T.PD1)
+        quad_open(T.PC0, "P:C0", 0)
+        quad_open(T.PC1, "P:C1", 1)
+        vgather(6, 7)
         ts(T.C32[:, na:256], T.CR[:, na:256], 2047, A.bitwise_and, ["CRb"], ["C32b"])
-        for h, bank in enumerate((T.PD0, T.PD1)):
-            act(T.AB[:, 512 * h:512 * h + 512], bank[:], F.Abs, ["P:D%d" % h], ak(2 * h, 2 * h + 2))
-        dense(T.PK0, "P:K0", 0)
-        quad_open(T.PD0, "P:D0", 15, 16)
-        vgather(7, 9)
+        vgather(7, 8)
         cp(T.CU[:, na:256], T.C32[:, na:256], ["C32b"], ["CUb"])
+        act(T.AB[:, 0:512], T.PD0[:], F.Abs, ["P:D0"], ak(0, 2))
+        act(T.AB[:, 512:1024], T.PD1[:], F.Abs, ["P:D1"], ak(2, 4))
+        dense(T.PK0, "P:K0", 0)
         sabs(4, 8)
         dense(T.PK1, "P:K1", 4)
-        vgather(9, 11)
-        vgather(11, 13)
+        vgather(8, 10)
+        vgather(10, 12)
         sabs(8, 12)
+        for m in range(8, 12):
+            quad(m, T.AB, 4)
         cp(T.R0[:], T.PK0[:, 0:64], ["P:K0"], ["R0"])
-        dense_open(T.PK0, "P:K0", 8)
-        vrelu(12, 13)
-        quad(T.PC0, "P:C0", 12, 13, 0)
-        quad(T.PC0, "P:C0", 12, 13, 1)
-        vgather(13, 15)
-        dense(T.PK0, "P:K0", 8)
-        quad(T.PC1, "P:C1", 13, 15, 0)
+        vgather(12, 14)
+        sabs(12, 14)
+        quad(12, T.AB, 4)
+        quad(13, T.AB, 4)
         tt(T.R1[:], T.PK1[:, 0:64], T.R0[:], A.min, ["P:K1", "R0"], ["R1"])
-        vrelu(13, 15)
-        quad(T.PC1, "P:C1", 13, 15, 1)
+        vgather(14, 15)
+        sabs(14, 15)
+        quad(14, T.AB, 4)
+        tt(T.R3[:], T.R1[:, 0:32], T.R1[:, 32:64], A.min, ["R1"], ["R3"])
         vgather(15, 16)
-        quad(T.PD0, "P:D0", 15, 16, 0)
-        cp(T.L0[:], T.PC0[:, 0:64], ["P:C0"], ["L0"])
+        quad(15, T.D, 2)
+        tt(T.LB[:, 0:256:16], T.R3[:, 0:16], T.R3[:, 16:32], A.min, ["R3"], ["LB"])
         vrelu(15, 16)
-        quad(T.PD0, "P:D0", 15, 16, 1)
-        mm(T.PH[:, 0:256], idm(0), T.PEN[:], True, False, ["ID0", "PEN"], ["P:H"])
+        quad(15, T.AB, 1)
+        mm(T.PH[:, 0:128], idm(0), T.PEN[:, 0:128], True, False, ["ID0", "PEN"], ["P:H"])
+        mm(T.PD0[:, 0:128], idm(0), T.PEN[:, 0:128], True, False, ["ID0", "PEN"], ["P:D0"])
         mm(T.PY[:, 0:128], idm(0), T.Y[:, 128:256], True, False, ["ID0", "Ya"], ["P:Y"])
         mm(T.PD1[:, 0:128], idm(0), T.Y[:, 0:128], True, False, ["ID0", "Ya"], ["P:D1"])
-        tt(T.R2[:], T.PK0[:, 0:64], T.R1[:], A.min, ["P:K0", "R1"], ["R2"])
-        tt(T.L1[:], T.PC1[:, 0:64], T.L0[:], A.min, ["P:C1", "L0"], ["L1"])
-        tt(T.R3[:], T.R2[:, 0:32], T.R2[:, 32:64], A.min, ["R2"], ["R3"])
-        tt(T.L2[:], T.PC1[:, 64:128], T.L1[:], A.min, ["P:C1", "L1"], ["L2"])
-        tt(T.R4[:], T.R3[:, 0:16], T.R3[:, 16:32], A.min, ["R3"], ["R4"])
-        tt(T.L2[:, 0:64:4], T.L2[:, 0:64:4], T.R4[:], A.min, ["L2", "R4"], ["L2"])
-        scan(T.SC[:], T.L2[:], T.PD0[:, 0:64], 67108864.0, A.min, A.min, ["L2", "P:D0"], ["SC"])
-        ts(T.MA[:], T.SC[:, 3:64:4], 255, A.bitwise_and, ["SC"], ["MA"])
+        scan(T.L0[:], T.LB[:], T.PC0[:, 0:256], 67108864.0, A.min, A.min, ["LB", "P:C0"], ["L0"])
+        scan(T.SC[:], T.L0[:], T.PC1[:, 0:256], 67108864.0, A.min, A.min, ["L0", "P:C1"], ["SC"])
+        ts(T.MA[:], T.SC[:, 15:256:16], 255, A.bitwise_and, ["SC"], ["MA"])
         cp(T.OM[:], T.MA[:], ["MA"], ["OM"])
         tt(T.GE[:, 0:256], T.C32[:].indirect(T.OM[:]), T.DM[:], A.mult, ["C32a", "C32b", "OM", "DM"], ["GE"])
-        mm(T.PH[:, 0:256], T.BON[:], T.GE[:], False, True, ["BON", "GE"], ["P:H"])
-        mm(T.PK1[:, 0:256], T.BON[:], T.GE[:], True, True, ["BON", "GE"], ["P:K1"])
-        mm(T.PC0[:, 0:256], T.BON[:], T.GE[:], True, False, ["BON", "GE"], ["P:C0"])
+        e0 = ((T.PD0, "P:D0"), (T.PH, "P:H"))
+        e1 = ((T.PK0, "P:K0"), (T.PK1, "P:K1"))
+        cb = ((T.PC1, "P:C1"), (T.PC0, "P:C0"))
+        for h in (1, 0):
+            ge = T.GE[:, 128 * h:128 * h + 128]
+            mm(e0[h][0][:, 0:128], T.BON[:], ge, False, True, ["BON", "GE"], [e0[h][1]])
+            mm(e1[h][0][:, 0:128], T.BON[:], ge, True, True, ["BON", "GE"], [e1[h][1]])
+            mm(cb[h][0][:, 0:128], T.BON[:], ge, True, False, ["BON", "GE"], [cb[h][1]])
         scan(T.SE[:], T.NDM[:], T.GE[:], -1.0, A.mult, A.add, ["NDM", "GE"], ["SE"])
         E16 = T.SE[:, 15:256:16]
         ek = "EU%d" % (t + 1)
@@ -459,32 +467,70 @@ def rank_program(g, core, T, topo):
                 send(far[1:], [k1])
                 dmas("y", "ce%d" % t, [(TT[s][:, 16 * (s - 1 - t):16 * (s - t)], src, [k1], ["T%de%d" % (s, t)])
                                        for s in range(t + 2, RO)])
-        for k in range(KS):
-            n = 256 - 16 * k
-            bank, key = (T.PH, "P:H") if k == 0 else (T.PK1, "P:K1")
-            tt(T.EQ[:, 256 * k:256 * k + n], bank[:, 16 * k:256], T.SE[:, 0:n], A.is_equal, [key, "SE"], ["EQ%d" % k])
-        halves = ((1, T.PY, "P:Y"), (0, T.PD1, "P:D1"))
-        for h, bank, k in halves:
-            act(T.XE[:, 128 * h:128 * h + 128], XW.indirect(eu(t + 1)[:, 8 * h:8 * h + 8]), F.Copy, ["X", ek], ["XE%d" % h])
-        for k in range(KS):
-            mm(T.PC0[:, 16 * k:256], T.B4K[:], T.EQ[:, 256 * k:256 * k + 256 - 16 * k], False, k == KS - 1,
-               ["B4K", "EQ%d" % k], ["P:C0"])
-            if k < 2:
-                h, bank, key = halves[k]
-                mm(bank[:, 0:128], idm(0), T.XE[:, 128 * h:128 * h + 128], False, True, ["ID0", "XE%d" % h], [key])
-        for h, bank, k in halves:
-            act(T.N1[:, 128 * h:128 * h + 128], bank[:, 0:128], F.Identity, [k], ["N1%d" % h], bias=MAGIC, scale=0.4995)
+        nb2 = ((T.PD1, "P:D1"), (T.PY, "P:Y"))
+
+        def twins(h, k):
+            lo, hi = max(128 * h, 16 * k), 128 * h + 128
+            bank, key = e0[h] if k == 0 else e1[h]
+            eq = T.EQ[:, 256 * k + lo:256 * k + hi]
+            tt(eq, bank[:, lo - 128 * h:128], T.SE[:, lo - 16 * k:hi - 16 * k], A.is_equal, [key, "SE"], ["EQ%d%d" % (h, k)])
+            mm(cb[h][0][:, lo - 128 * h:128], T.B4K[:], eq, False, k == KS - 1, ["B4K", "EQ%d%d" % (h, k)], [cb[h][1]])
+
+        def xe_sum(h):
+            mm(nb2[h][0][:, 0:128], idm(0), T.XE[:, 128 * h:128 * h + 128], False, True, ["ID0", "XE%d" % h], [nb2[h][1]])
+
+        def pick(h):
+            scan(T.LS[:, 128 * h:128 * h + 128], T.QC[:, 0:128], cb[h][0][:, 0:128], 0.0, A.add, A.min,
+                 ["QC", cb[h][1]], ["LS%d" % h])
+
+        def clamp(h):
+            tt(T.OF[:, 8 * h:8 * h + 8], T.LS[:, 128 * h + 15:128 * h + 128:16], T.DUT[:, 8 * h:8 * h + 8], A.min,
+               ["LS%d" % h, "DUT"], ["OF%d" % h])
+
+        def offs(h):
+            ts(T.OS[:, 8 * h:8 * h + 8], T.OF[:, 8 * h:8 * h + 8], cf(QF), A.add, ["OF%d" % h, "qf"], ["OS%d" % h])
+
+        def scatter(c):
+            cp(T.X[:].indirect(T.OS[:, c:c + KS]), T.NX[:, 16 * c:16 * (c + KS)], ["OS%d" % (c // 8), "NX%d" % (c // 8)], ["X"])
+
+        def newval(h, part):
+            cols = slice(128 * h, 128 * h + 128)
+            if part == 0:
+                act(T.N1[:, cols], nb2[h][0][:, 0:128], F.Identity, [nb2[h][1]], ["N1%d" % h], bias=MAGIC, scale=0.4995)
+            else:
+                act(T.NX[:, cols], T.N1[:, cols], F.Identity, ["N1%d" % h], ["NX%d" % h], bias=-MAGIC)
+
         for h in (1, 0):
-            act(T.NX[:, 128 * h:128 * h + 128], T.N1[:, 128 * h:128 * h + 128], F.Identity, ["N1%d" % h], ["NX%d" % h], bias=-MAGIC)
-        act(T.EB[:], T.PK1[:, 0:256], F.Copy, ["P:K1"], ["EB"])
-        dmas("y", "ye%d" % t, [(T.yr[RO - 1 - t:128:16, :], T.EB[0:128:16, :], ["EB"], ["yr"])])
+            act(T.XE[:, 128 * h:128 * h + 128], XW.indirect(eu(t + 1)[:, 8 * h:8 * h + 8]), F.Copy, ["X", ek], ["XE%d" % h])
+        twins(1, 0)
+        twins(1, 1)
+        xe_sum(1)
+        twins(1, 2)
+        twins(1, 3)
+        xe_sum(0)
+        twins(0, 0)
+        twins(0, 1)
+        twins(0, 2)
+        newval(1, 0)
+        newval(0, 0)
+        newval(1, 1)
+        newval(0, 1)
+        pick(1)
+        twins(0, 3)
+        for h in (1, 0):
+            act(T.EB[:, 128 * h:128 * h + 128], e1[h][0][:, 0:128], F.Copy, [e1[h][1]], ["EB%d" % h])
+        dmas("y", "ye%d" % t, [(T.yr[RO - 1 - t:128:16, :], T.EB[0:128:16, :], ["EB0", "EB1"], ["yr"])])
         if not last:
             hash_open()
-        scan(T.LS[:], T.QC[:], T.PC0[:, 0:256], 0.0, A.add, A.min, ["QC", "P:C0"], ["LS"])
-        tt(T.OF[:], T.LS[:, 15:256:16], T.DUT[:], A.min, ["LS", "DUT"], ["OF"])
-        ts(T.OS[:], T.OF[:], cf(QF), A.add, ["OF", "qf"], ["OS"])
-        for c in range(16 - KS, -1, -KS):
-            cp(T.X[:].indirect(T.OS[:, c:c + KS]), T.NX[:, 16 * c:16 * (c + KS)], ["OS", "NX%d" % (c // 8)], ["X"])
+        clamp(1)
+        offs(1)
+        pick(0)
+        scatter(12)
+        clamp(0)
+        scatter(8)
+        offs(0)
+        scatter(4)
+        scatter(0)
 
     dmas("y", "yxa", [(T.yx[0:64, :], T.X[0:64, 0:2048], ["X"], ["yxa"])])
     dmas("s", "yxb", [(T.yx[64:128, :], T.X[64:128, 0:2048], ["X"], ["yxb"])])

@@ -13,14 +13,14 @@ def _sb(n, d):
 
 
 SCRATCH = {
-    "X": _sb(2048 + 16 * KS, BF), "RI": _sb(256, I32), "WI": _sb(1, I32), "KI": _sb(1, I32),
-    "RF": _sb(272, FL), "TR": _sb(512, FL), "TL": _sb(16, U16),
+    "X": _sb(2048 + 128, BF), "RI": _sb(272, I32), "WI": _sb(1, I32), "KI": _sb(1, I32),
+    "RF": _sb(256, FL), "TR": _sb(512, I32), "TL": _sb(16, U16),
     "T0": _sb(560, FL), "T1": _sb(560, FL), "T2": _sb(560, FL), "T3": _sb(560, FL),
     "CI": _sb(16, I32), "CF": _sb(32, FL), "AGE": _sb(16, I32),
     "JL": _sb(256, BF), "IG": _sb(256, BF), "H2": _sb(64, BF), "J": _sb(128, BF), "Q4": _sb(256, BF), "KAQ": _sb(512, BF),
     "SEL": _sb(720, BF), "ONES": _sb(128, BF), "C1024": _sb(16 * max(CA, 16 - CA), BF),
     "DM": _sb(256, BF), "NDM": _sb(256, BF), "QC": _sb(256, BF), "PEN": _sb(256, BF), "BON": _sb(128, BF),
-    "ID": _sb(17 * 128, BF), "KM": _sb(2048, H), "KD": _sb(16, H),
+    "ID": _sb(18 * 128, BF), "KM": _sb(2048, H), "KD": _sb(16, H),
     "HP": _sb(64, BF), "KB": _sb(64, BF), "KBQ": _sb(256, BF), "KT": _sb(512, BF),
     "EU": _sb(96, U16), "G01": _sb(512, BF), "HS": _sb(64, I32), "HA": _sb(32, I32),
     "OFF": _sb(32, U16), "FO": _sb(32, BF), "GP": _sb(256, H), "SP": _sb(256, H), "GQ": _sb(256, FL), "SQ": _sb(256, FL),
@@ -31,9 +31,9 @@ SCRATCH = {
     "R0": _sb(64, FL), "R1": _sb(64, FL), "R3": _sb(32, FL), "TH": _sb(512, H),
     "L0": _sb(256, FL), "LB": _sb(256, FL), "SC": _sb(256, I32),
     "MA": _sb(16, I32), "OM": _sb(16, U16),
-    "GE": _sb(256, H), "SE": _sb(256, H), "EQ": _sb(256 * KS, BF), "LS": _sb(256, FL), "OF": _sb(16, FL), "OS": _sb(16, U16),
-    "B4K": _sb(128, BF), "DUI": _sb(16, I32), "DUT": _sb(16, FL),
-    "XE": _sb(256, BF), "N1": _sb(256, FL), "NX": _sb(256, BF), "EB": _sb(256, FL),
+    "GE": _sb(256, H), "SE": _sb(256, H), "EQ": _sb(256 * KS, BF), "LS": _sb(256, FL), "OS": _sb(16, U16),
+    "B4K": _sb(128, BF), "DUI": _sb(128, I32), "DUT": _sb(128, FL), "NBG": _sb(128, BF),
+    "XE": _sb(256, BF), "QTR": _sb(128, BF), "NX": _sb(256, BF), "EB": _sb(256, FL),
 }
 for _n in ("PH", "PC0", "PC1", "PY", "PD0", "PD1", "PK0", "PK1"):
     SCRATCH[_n] = ("psum", [128, 512], FL)
@@ -178,10 +178,10 @@ def rank_program(g, core, T, topo):
             return share(1, n)
         return share(RO - 1, n) + share(1, n) + sum(share(RO - 2 - t, n) for t in range(s - 1))
 
-    dmas("y", "lr", [(T.RI[:], T.ring[:], [], ["RI"])])
+    dmas("y", "lr", [(T.RI[:, 0:256], T.ring[:], [], ["RI"])])
+    dmas("y", "lw", [(T.WI[:], T.wt[:], [], ["WI"])])
+    dmas("y", "lk", [(T.KI[:], T.kap[:], [], ["KI"])])
     dmas("y", "lx", [(XW, T.x[:], [], ["X"])])
-    dmas("s", "lw", [(T.WI[:], T.wt[:], [], ["WI"])])
-    dmas("s", "lk", [(T.KI[:], T.kap[:], [], ["KI"])])
 
     iota(ci(0), [[0, 1]], 0, 1, ["q"], small=False)
     iota(T.AGE[:], [[1, 16]], 0, 0, ["AGE"], small=False)
@@ -205,16 +205,16 @@ def rank_program(g, core, T, topo):
     ts(T.TL[:], T.AGE[:], cf(B2), A.add, ["AGE", "b2"], ["TL"])
     cp(cf(P8), ci(6), ["p8i"], ["p8"])
     cp(cf(P4), ci(7), ["p4i"], ["p4"])
-    cp(T.RF[:, 0:256], T.RI[:], ["RI"], ["RFa"])
-    cp(T.RF[:, 256:272], T.RI[:, 0:16], ["RI"], ["RFb"])
-    op("v", lambda: V.transpose(T.TR[:, 0:256], T.RF[:, 0:256]), ["RFa"], ["TRa"])
-    op("v", lambda: V.transpose(T.TR[:, 256:512], T.RF[:, 16:272]), ["RFa", "RFb"], ["TRb"])
+    cp(T.RI[:, 256:272], T.RI[:, 0:16], ["RI"], ["RIb"])
+    op("v", lambda: V.transpose(T.TR[:, 0:256], T.RI[:, 0:256]), ["RI"], ["TRa"])
+    op("v", lambda: V.transpose(T.TR[:, 256:512], T.RI[:, 16:272]), ["RI", "RIb"], ["TRb"])
     ts(T.DM[:], T.JL[:, 0:256], cf(PF), A.is_equal, ["JL", "pf"], ["DM"])
     cp(T.TH[:, 0:256], T.TR[:].indirect(T.TL[:]), ["TRa", "TRb", "TL"], ["TH"])
     send([(0, T.TH[:, 0:256], T.TH[:, 256:512])], ["TH"])
+    cp(T.RF[:], T.RI[:, 0:256], ["RI"], ["RFa"])
     cp(T.T0[:, 0:256], T.TH[:, 0:256], ["TH"], ["T0own"])
     iota(T.Q4[:], [[0, 16], [1, 4], [0, 4]], 0, 0, ["Q4"])
-    iota(T.DUI[:], [[0, 16 // KS], [16, KS]], 2048, 0, ["DUI"], small=False)
+    iota(T.DUI[:], [[1, 128]], 2048, 0, ["DUI"], small=False)
     iota(T.J[:], [[1, 128]], 0, 0, ["J"])
     iota(T.KAQ[:, 0:256], [[1, 16], [0, 4], [16, 4]], 128, 0, ["KAQ0"])
     iota(T.KAQ[:, 256:512], [[1, 16], [0, 4], [16, 4]], 192, 0, ["KAQ1"])
@@ -233,6 +233,7 @@ def rank_program(g, core, T, topo):
 
     def late_scalar():
         act(idm(16), idm(0), F.Copy, ["ID0"], ["ID16"], scale=-1.0)
+        act(idm(17), idm(0), F.Copy, ["ID0"], ["ID17"], scale=0.5)
         for m in range(1, 16):
             act(idm(m), idm(0), F.Copy, ["ID0"], ["ID%d" % m], scale=float(2 * m + 1))
 
@@ -261,9 +262,10 @@ def rank_program(g, core, T, topo):
         ts(T.PEN[:], T.DM[:], -4096.0, A.mult, ["DM"], ["PEN"])
         ms(T.LB[:], 67108864.0, ["LB"])
         tt(T.KBQ[:], T.KT[:, 0:256], T.KT[:, 256:512], A.max, ["KTa", "KTb"], ["KBQ"])
-        ts(cf(DUM), cf(PF), 1048577.0, A.mult, ["pf"], ["dum"], -15728640.0, A.add)
+        ms(T.QTR[:], -0.25, ["QTR"])
         ts(T.B4K[:], T.BON[:], 4096.0, A.mult, ["BON"], ["B4K"])
-        ts(T.DUT[:], T.DUI[:], cf(DUM), A.add, ["DUI", "dum"], ["DUT"])
+        ts(T.NBG[:], T.NDM[:, 0:128], 4194304.0, A.mult, ["NDM"], ["NBG"])
+        tt(T.DUT[:], T.DUI[:], T.DM[:, 0:128], A.mult, ["DUI", "DM"], ["DUT"])
 
     def eu(k):
         return T.EU[:, 64 - 16 * k:80 - 16 * k]
@@ -393,6 +395,7 @@ def rank_program(g, core, T, topo):
         act(T.Y[:, 256:512], T.Y[:, 0:256], F.Copy, ["Ya"], ["Yb"])
         ts(T.C32[:, 0:na], T.CR[:, 0:na], 2047, A.bitwise_and, ["CRa"], ["C32a"])
         cp(T.CU[:, 0:na], T.C32[:, 0:na], ["C32a"], ["CUa"])
+        cp(T.CR[:, na:256], T.PC1[:, 0:nb], ["P:C1"], ["CRb"])
 
         def sgather(h, a, bank):
             act(T.D[:, 256 * a:256 * a + 512], XW.indirect(T.CU[:, 16 * a:16 * a + 32]), F.Copy, ["X"] + cuk(a, a + 2), dk(a, a + 2))
@@ -403,14 +406,13 @@ def rank_program(g, core, T, topo):
         dense_open(T.PK1, "P:K1", 4)
         sgather(0, 0, T.PD0)
         vgather(4, 6)
-        cp(T.CR[:, na:256], T.PC1[:, 0:nb], ["P:C1"], ["CRb"])
+        ts(T.C32[:, na:256], T.CR[:, na:256], 2047, A.bitwise_and, ["CRb"], ["C32b"])
         sgather(1, 2, T.PD1)
         quad_open(T.PC0, "P:C0", 0)
         quad_open(T.PC1, "P:C1", 1)
         vgather(6, 7)
-        ts(T.C32[:, na:256], T.CR[:, na:256], 2047, A.bitwise_and, ["CRb"], ["C32b"])
-        vgather(7, 8)
         cp(T.CU[:, na:256], T.C32[:, na:256], ["C32b"], ["CUb"])
+        vgather(7, 8)
         act(T.AB[:, 0:512], T.PD0[:], F.Abs, ["P:D0"], ak(0, 2))
         act(T.AB[:, 512:1024], T.PD1[:], F.Abs, ["P:D1"], ak(2, 4))
         dense(T.PK0, "P:K0", 0)
@@ -421,27 +423,30 @@ def rank_program(g, core, T, topo):
         sabs(8, 12)
         for m in range(8, 12):
             quad(m, T.AB, 4)
-        cp(T.R0[:], T.PK0[:, 0:64], ["P:K0"], ["R0"])
         vgather(12, 14)
+        cp(T.R0[:], T.PK0[:, 0:64], ["P:K0"], ["R0"])
         sabs(12, 14)
         quad(12, T.AB, 4)
         quad(13, T.AB, 4)
-        tt(T.R1[:], T.PK1[:, 0:64], T.R0[:], A.min, ["P:K1", "R0"], ["R1"])
         vgather(14, 15)
+        tt(T.R1[:], T.PK1[:, 0:64], T.R0[:], A.min, ["P:K1", "R0"], ["R1"])
         sabs(14, 15)
         quad(14, T.AB, 4)
-        tt(T.R3[:], T.R1[:, 0:32], T.R1[:, 32:64], A.min, ["R1"], ["R3"])
         vgather(15, 16)
         quad(15, T.D, 2)
-        tt(T.LB[:, 0:256:16], T.R3[:, 0:16], T.R3[:, 16:32], A.min, ["R3"], ["LB"])
+        tt(T.R3[:], T.R1[:, 0:32], T.R1[:, 32:64], A.min, ["R1"], ["R3"])
         vrelu(15, 16)
         quad(15, T.AB, 1)
+        tt(T.LB[:, 0:256:16], T.R3[:, 0:16], T.R3[:, 16:32], A.min, ["R3"], ["LB"])
         mm(T.PH[:, 0:128], idm(0), T.PEN[:, 0:128], True, False, ["ID0", "PEN"], ["P:H"])
         mm(T.PD0[:, 0:128], idm(0), T.PEN[:, 0:128], True, False, ["ID0", "PEN"], ["P:D0"])
-        mm(T.PY[:, 0:128], idm(0), T.Y[:, 128:256], True, False, ["ID0", "Ya"], ["P:Y"])
-        mm(T.PD1[:, 0:128], idm(0), T.Y[:, 0:128], True, False, ["ID0", "Ya"], ["P:D1"])
+        for bank, key, a in ((T.PY, "P:Y", 128), (T.PD1, "P:D1", 0)):
+            mm(bank[:, 0:128], idm(17), T.Y[:, a:a + 128], True, False, ["ID17", "Ya"], [key])
+            mm(bank[:, 0:128], idm(0), T.QTR[:], False, False, ["ID0", "QTR"], [key])
         scan(T.L0[:], T.LB[:], T.PC0[:, 0:256], 67108864.0, A.min, A.min, ["LB", "P:C0"], ["L0"])
         scan(T.SC[:], T.L0[:], T.PC1[:, 0:256], 67108864.0, A.min, A.min, ["L0", "P:C1"], ["SC"])
+        mm(T.PC0[:, 0:128], idm(0), T.NBG[:], True, False, ["ID0", "NBG"], ["P:C0"])
+        mm(T.PC1[:, 0:128], idm(0), T.NBG[:], True, False, ["ID0", "NBG"], ["P:C1"])
         ts(T.MA[:], T.SC[:, 15:256:16], 255, A.bitwise_and, ["SC"], ["MA"])
         cp(T.OM[:], T.MA[:], ["MA"], ["OM"])
         tt(T.GE[:, 0:256], T.C32[:].indirect(T.OM[:]), T.DM[:], A.mult, ["C32a", "C32b", "OM", "DM"], ["GE"])
@@ -452,7 +457,7 @@ def rank_program(g, core, T, topo):
             ge = T.GE[:, 128 * h:128 * h + 128]
             mm(e0[h][0][:, 0:128], T.BON[:], ge, False, True, ["BON", "GE"], [e0[h][1]])
             mm(e1[h][0][:, 0:128], T.BON[:], ge, True, True, ["BON", "GE"], [e1[h][1]])
-            mm(cb[h][0][:, 0:128], T.BON[:], ge, True, False, ["BON", "GE"], [cb[h][1]])
+            mm(cb[h][0][:, 0:128], T.BON[:], ge, False, False, ["BON", "GE"], [cb[h][1]])
         scan(T.SE[:], T.NDM[:], T.GE[:], -1.0, A.mult, A.add, ["NDM", "GE"], ["SE"])
         E16 = T.SE[:, 15:256:16]
         ek = "EU%d" % (t + 1)
@@ -477,58 +482,46 @@ def rank_program(g, core, T, topo):
             mm(cb[h][0][:, lo - 128 * h:128], T.B4K[:], eq, False, k == KS - 1, ["B4K", "EQ%d%d" % (h, k)], [cb[h][1]])
 
         def xe_sum(h):
-            mm(nb2[h][0][:, 0:128], idm(0), T.XE[:, 128 * h:128 * h + 128], False, True, ["ID0", "XE%d" % h], [nb2[h][1]])
+            mm(nb2[h][0][:, 0:128], idm(17), T.XE[:, 128 * h:128 * h + 128], False, True, ["ID17", "XE%d" % h], [nb2[h][1]])
 
         def pick(h):
-            scan(T.LS[:, 128 * h:128 * h + 128], T.QC[:, 0:128], cb[h][0][:, 0:128], 0.0, A.add, A.min,
-                 ["QC", cb[h][1]], ["LS%d" % h])
-
-        def clamp(h):
-            tt(T.OF[:, 8 * h:8 * h + 8], T.LS[:, 128 * h + 15:128 * h + 128:16], T.DUT[:, 8 * h:8 * h + 8], A.min,
-               ["LS%d" % h, "DUT"], ["OF%d" % h])
+            scan(T.LS[:, 128 * h:128 * h + 128], T.DUT[:], cb[h][0][:, 0:128], 0.0, A.max, A.min,
+                 ["DUT", cb[h][1]], ["LS%d" % h])
 
         def offs(h):
-            ts(T.OS[:, 8 * h:8 * h + 8], T.OF[:, 8 * h:8 * h + 8], cf(QF), A.add, ["OF%d" % h, "qf"], ["OS%d" % h])
+            cp(T.OS[:, 8 * h:8 * h + 8], T.LS[:, 128 * h + 15:128 * h + 128:16], ["LS%d" % h], ["OS%d" % h])
 
         def scatter(c):
             cp(T.X[:].indirect(T.OS[:, c:c + KS]), T.NX[:, 16 * c:16 * (c + KS)], ["OS%d" % (c // 8), "NX%d" % (c // 8)], ["X"])
 
-        def newval(h, part):
-            cols = slice(128 * h, 128 * h + 128)
-            if part == 0:
-                act(T.N1[:, cols], nb2[h][0][:, 0:128], F.Identity, [nb2[h][1]], ["N1%d" % h], bias=MAGIC, scale=0.4995)
-            else:
-                act(T.NX[:, cols], T.N1[:, cols], F.Identity, ["N1%d" % h], ["NX%d" % h], bias=-MAGIC)
+        def newval(h):
+            ts(T.NX[:, 128 * h:128 * h + 128], nb2[h][0][:, 0:128], MAGIC, A.add, [nb2[h][1]], ["NX%d" % h], -MAGIC, A.add)
 
         for h in (1, 0):
             act(T.XE[:, 128 * h:128 * h + 128], XW.indirect(eu(t + 1)[:, 8 * h:8 * h + 8]), F.Copy, ["X", ek], ["XE%d" % h])
         twins(1, 0)
         twins(1, 1)
-        xe_sum(1)
         twins(1, 2)
         twins(1, 3)
-        xe_sum(0)
+        xe_sum(1)
         twins(0, 0)
         twins(0, 1)
+        xe_sum(0)
         twins(0, 2)
-        newval(1, 0)
-        newval(0, 0)
-        newval(1, 1)
-        newval(0, 1)
-        pick(1)
         twins(0, 3)
+        pick(1)
+        newval(1)
         for h in (1, 0):
             act(T.EB[:, 128 * h:128 * h + 128], e1[h][0][:, 0:128], F.Copy, [e1[h][1]], ["EB%d" % h])
         dmas("y", "ye%d" % t, [(T.yr[RO - 1 - t:128:16, :], T.EB[0:128:16, :], ["EB0", "EB1"], ["yr"])])
         if not last:
             hash_open()
-        clamp(1)
         offs(1)
         pick(0)
         scatter(12)
-        clamp(0)
-        scatter(8)
         offs(0)
+        newval(0)
+        scatter(8)
         scatter(4)
         scatter(0)
 

@@ -2,8 +2,8 @@ from concourse.bass import DstId, RemoteDMATransfer
 from concourse.mybir import AluOpType as A, AxisListType, ActivationFunctionType as F
 
 N, RO = 8, 4
-KS = 4
-PA = 8
+KS = (8, 4)
+PA = 16
 CA = 8
 BF, H, FL, I32, U16 = "bfloat16", "float16", "float32", "int32", "uint16"
 
@@ -19,9 +19,9 @@ SCRATCH = {
     "CI": _sb(16, I32), "CF": _sb(32, FL), "AGE": _sb(16, I32),
     "JL": _sb(256, BF), "IG": _sb(256, BF), "H2": _sb(64, BF), "J": _sb(128, BF), "Q4": _sb(256, BF), "KAQ": _sb(512, BF),
     "SEL": _sb(720, BF), "ONES": _sb(128, BF), "C1024": _sb(16 * max(CA, 16 - CA), BF),
-    "DM": _sb(256, BF), "NDM": _sb(256, BF), "QC": _sb(256, BF), "PEN": _sb(256, BF), "BON": _sb(128, BF),
+    "DM": _sb(256, BF), "NDM": _sb(256, BF), "QC": _sb(256, BF), "PEN": _sb(128, BF), "BON": _sb(128, BF),
     "ID": _sb(18 * 128, BF), "KM": _sb(2048, H), "KD": _sb(16, H),
-    "HP": _sb(64, BF), "KB": _sb(64, BF), "KBQ": _sb(256, BF), "KT": _sb(512, BF),
+    "HP": _sb(64, BF), "KB": _sb(64, BF), "KT": _sb(512, BF),
     "EU": _sb(96, U16), "G01": _sb(512, BF), "HS": _sb(64, I32), "HA": _sb(32, I32),
     "OFF": _sb(32, U16), "FO": _sb(32, BF), "GP": _sb(256, H), "SP": _sb(256, H), "GQ": _sb(256, FL), "SQ": _sb(256, FL),
     "OP": _sb(16, U16), "OQ": _sb(16, U16), "Q16": _sb(16, H), "PQ": _sb(16, I32), "FI": _sb(16, I32), "F16": _sb(16, H),
@@ -31,7 +31,7 @@ SCRATCH = {
     "R0": _sb(64, FL), "R1": _sb(64, FL), "R3": _sb(32, FL), "TH": _sb(512, H),
     "L0": _sb(256, FL), "LB": _sb(256, FL), "SC": _sb(256, I32),
     "MA": _sb(16, I32), "OM": _sb(16, U16),
-    "GE": _sb(256, H), "SE": _sb(256, H), "EQ": _sb(256 * KS, BF), "LS": _sb(256, FL), "OS": _sb(16, U16),
+    "GE": _sb(256, H), "SE": _sb(256, H), "EQ": _sb(256 * 8, BF), "LS": _sb(256, FL), "OS": _sb(16, U16),
     "B4K": _sb(128, BF), "DUI": _sb(128, I32), "DUT": _sb(128, FL), "NBG": _sb(128, BF),
     "XE": _sb(256, BF), "QTR": _sb(128, BF), "NX": _sb(256, BF), "EB": _sb(256, FL),
 }
@@ -193,25 +193,29 @@ def rank_program(g, core, T, topo):
     ts(ci(1), ci(0), 4, A.arith_shift_right, ["q"], ["g32"])
     ts(ci(2), ci(0), 15, A.bitwise_and, ["q"], ["p32"])
     ts(ci(3), ci(0), 31, A.bitwise_and, ["q"], ["x32"])
+    ms(T.ONES[:], 1.0, ["ONES"])
     tt(ci(4), ci(0), ci(1), A.add, ["q", "g32"], ["t32"])
     cp(cf(PF), ci(2), ["p32"], ["pf"])
     ts(cf(WW), ci(3), 16.0, A.is_equal, ["x32"], ["ww"], 256.0, A.mult)
+    ms(T.C1024[:], 1024.0, ["C1024"])
+    ms(cf(AC), -1024.0, ["ac0"])
     ts(ci(5), ci(4), 1, A.bitwise_and, ["t32"], ["b0"])
     cp(cf(GF), ci(1), ["g32"], ["gf"])
     ts(cf(B1), cf(PF), 16.0, A.mult, ["pf", "ww"], ["b1"], cf(WW), A.add)
     ts(ci(6), ci(2), 3, A.arith_shift_right, ["p32"], ["p8i"])
+    ms(T.QTR[:], -0.25, ["QTR"])
     ts(cf(B2), ci(5), 240.0, A.mult, ["b0", "b1"], ["b2"], cf(B1), A.add)
     ts(ci(7), ci(2), 2, A.arith_shift_right, ["p32"], ["p4i"])
     ts(T.TL[:], T.AGE[:], cf(B2), A.add, ["AGE", "b2"], ["TL"])
     cp(cf(P8), ci(6), ["p8i"], ["p8"])
     cp(cf(P4), ci(7), ["p4i"], ["p4"])
+    ms(T.LB[:], 67108864.0, ["LB"])
     cp(T.RI[:, 256:272], T.RI[:, 0:16], ["RI"], ["RIb"])
     op("v", lambda: V.transpose(T.TR[:, 0:256], T.RI[:, 0:256]), ["RI"], ["TRa"])
     op("v", lambda: V.transpose(T.TR[:, 256:512], T.RI[:, 16:272]), ["RI", "RIb"], ["TRb"])
     ts(T.DM[:], T.JL[:, 0:256], cf(PF), A.is_equal, ["JL", "pf"], ["DM"])
     cp(T.TH[:, 0:256], T.TR[:].indirect(T.TL[:]), ["TRa", "TRb", "TL"], ["TH"])
     send([(0, T.TH[:, 0:256], T.TH[:, 256:512])], ["TH"])
-    cp(T.RF[:], T.RI[:, 0:256], ["RI"], ["RFa"])
     cp(T.T0[:, 0:256], T.TH[:, 0:256], ["TH"], ["T0own"])
     iota(T.Q4[:], [[0, 16], [1, 4], [0, 4]], 0, 0, ["Q4"])
     iota(T.DUI[:], [[1, 128]], 2048, 0, ["DUI"], small=False)
@@ -221,7 +225,6 @@ def rank_program(g, core, T, topo):
     need("gp", "arr0", arrivals(0))
     send([(s, T.T0[:, 0:256], TT[s][:, 256 + 16 * s:512 + 16 * s]) for s in range(1, RO)], ["T0own"])
     dmas("y", "cp", [(TT[s][:, 16 * s:256], T.T0[:, 0:256 - 16 * s], ["T0own"], ["T%down" % s]) for s in range(1, RO)])
-    dmas("y", "yr0", [(T.yr[4:128, :], T.RF[0:124, 0:256], ["RFa"], ["yr"])])
 
     ts(T.BON[:], T.IG[:, 0:128], cf(GF), A.is_equal, ["IG", "gf"], ["BON"])
     ts(cf(W16), T.WI[:], 16.0, A.mult, ["WI"], ["w16"])
@@ -240,14 +243,11 @@ def rank_program(g, core, T, topo):
     def mid_vector():
         ts(T.KD[:], T.DM[:, 0:16], cf(KF), A.mult, ["DM", "kf"], ["KD"])
         mm(T.PK1[:, 0:16], T.BON[:], T.KD[:], True, True, ["BON", "KD"], ["P:K1"])
-        ms(T.ONES[:], 1.0, ["ONES"])
         ts(T.NDM[:], T.JL[:], cf(PF), A.not_equal, ["JL", "pf"], ["NDM"])
 
     def late_vector():
         ts(T.QC[:], T.DM[:], 68157440.0, A.mult, ["DM"], ["QC"], -1048576.0, A.add)
         ts(cf(QF), cf(PF), -1048576.0, A.mult, ["pf"], ["qf"], 15728640.0, A.add)
-        ms(T.C1024[:], 1024.0, ["C1024"])
-        ms(cf(AC), -1024.0, ["ac0"])
         for m in range(16):
             ts(T.KM[:, 128 * m:128 * (m + 1)], idm(0), T.PK1[:, m:m + 1], A.mult, ["ID0", "P:K1"], ["KM%d" % m])
 
@@ -259,13 +259,13 @@ def rank_program(g, core, T, topo):
         ts(T.SEL[:, 576 + 3:576 + 128:4], T.IG[:, 0:128:4], cf(GF), A.is_equal, ["IG", "gf"], ["SEL4"], 256.0, A.mult)
         ts(T.KT[:, 0:256], T.Q4[:], cf(P4), A.not_equal, ["Q4", "p4"], ["KTa"], 33554432.0, A.mult)
         ts(T.KT[:, 256:512], T.IG[:], -1048576.0, A.mult, ["IG"], ["KTb"], 15728640.0, A.add)
-        ts(T.PEN[:], T.DM[:], -4096.0, A.mult, ["DM"], ["PEN"])
-        ms(T.LB[:], 67108864.0, ["LB"])
-        tt(T.KBQ[:], T.KT[:, 0:256], T.KT[:, 256:512], A.max, ["KTa", "KTb"], ["KBQ"])
-        ms(T.QTR[:], -0.25, ["QTR"])
+
+    def gap_vector():
+        ts(T.PEN[:], T.DM[:, 0:128], -4096.0, A.mult, ["DM"], ["PEN"])
         ts(T.B4K[:], T.BON[:], 4096.0, A.mult, ["BON"], ["B4K"])
         ts(T.NBG[:], T.NDM[:, 0:128], 4194304.0, A.mult, ["NDM"], ["NBG"])
-        tt(T.DUT[:], T.DUI[:], T.DM[:, 0:128], A.mult, ["DUI", "DM"], ["DUT"])
+        cp(T.RF[:], T.RI[:, 0:256], ["RI"], ["RFa"])
+        dmas("y", "yr0", [(T.yr[4:128, :], T.RF[0:124, 0:256], ["RFa"], ["yr"])])
 
     def eu(k):
         return T.EU[:, 64 - 16 * k:80 - 16 * k]
@@ -286,7 +286,7 @@ def rank_program(g, core, T, topo):
 
     def vgather(a, b):
         tt(T.D[:, 256 * a:256 * b], XW.indirect(T.CU[:, 16 * a:16 * b]), T.Y[:, 0:256 * (b - a)], A.subtract,
-           ["X", "Ya"] + (["Yb"] if b - a > 1 else []) + cuk(a, b), dk(a, b))
+           ["X", "Y0", "Ya"] + (["Yb"] if b - a > 1 else []) + cuk(a, b), dk(a, b))
 
     def vrelu(a, b):
         ts(T.AB[:, 256 * a:256 * b], T.D[:, 256 * a:256 * b], 0.0, A.max, dk(a, b), ak(a, b))
@@ -304,7 +304,8 @@ def rank_program(g, core, T, topo):
                ["SEL0"] + ak(a, a + 4), [key])
 
     def quad_open(bank, key, j):
-        mm(bank[:, 0:256], idm(0), T.KBQ[:], True, False, ["ID0", "KBQ"], [key])
+        mm(bank[:, 0:256], idm(0), T.KT[:, 0:256], True, False, ["ID0", "KTa"], [key])
+        mm(bank[:, 0:256], idm(0), T.KT[:, 256:512], False, False, ["ID0", "KTb"], [key])
         mm(bank[:, 0:256], idm(0), T.KAQ[:, 256 * j:256 * j + 256], False, False, ["ID0", "KAQ%d" % j], [key])
 
     def quad(m, src, which):
@@ -341,6 +342,7 @@ def rank_program(g, core, T, topo):
         tk = ["T%down" % t] + ["T%de%d" % (t, u) for u in range(t)]
         if t == 0:
             cp(T.T0[:, 256:512], T.TH[:, 256:512], [], ["T0far"])
+            tt(T.DUT[:], T.DUI[:], T.DM[:, 0:128], A.mult, ["DUI", "DM"], ["DUT"])
             tk.append("T0far")
         else:
             need("s", "arr%d" % t, arrivals(t))
@@ -377,46 +379,53 @@ def rank_program(g, core, T, topo):
         if not last:
             ts(ci(9), ci(8), 63, A.bitwise_and, ["ai"], ["aj"])
         tt(T.PQ[:], P16, T.Q16[:], A.mult, ["SP", "Q16"], ["PQ"])
-        cp(T.XP[:], XW.indirect(T.OP[:]), ["X", "OP"], ["XP"])
+        cp(T.XP[:, 0:128], XW.indirect(T.OP[:, 0:8]), ["X", "OP"], ["XPa"])
         ts(T.FI[:], T.PQ[:], 5, A.arith_shift_right, ["PQ"], ["FI"], 2047, A.bitwise_and)
+        cp(T.XP[:, 128:256], XW.indirect(T.OP[:, 8:16]), ["X", "OP"], ["XP"])
+        ts(T.F16[:], T.FI[:], cf(AC + t), A.add, ["FI", "ac%d" % t], ["F16"])
         if not last:
             ts(cf(AC + t + 1), ci(9), -1024.0, A.add, ["aj"], ["ac%d" % (t + 1)])
-        ts(T.F16[:], T.FI[:], cf(AC + t), A.add, ["FI", "ac%d" % t], ["F16"])
         cpart("Q", range(CA))
-        mm(T.PY[:, 0:256], idm(0), T.XQ[:], True, False, ["ID0", "XQ"], ["P:Y"])
-        mm(T.PY[:, 0:256], idm(0), T.XP[:], False, True, ["ID0", "XP"], ["P:Y"])
+        yb = ((T.PY, "P:Y", "XPa"), (T.PD0, "P:D0", "XP"))
+        for h in (0, 1):
+            mm(yb[h][0][:, 0:128], idm(0), T.XQ[:, 128 * h:128 * h + 128], True, False, ["ID0", "XQ"], [yb[h][1]])
+            mm(yb[h][0][:, 0:128], idm(0), T.XP[:, 128 * h:128 * h + 128], False, True, ["ID0", yb[h][2]], [yb[h][1]])
         cpart("F", range(CA))
         cpart("P", range(PA, 16))
         cpart("Q", range(CA, 16))
         cpart("F", range(CA, 16))
-        ts(T.SG[:], T.PY[:, 0:256], 256.0, A.is_ge, ["P:Y"], ["SG"], -256.0, A.mult)
+        if t == 0:
+            gap_vector()
+        for h in (0, 1):
+            ts(T.SG[:, 128 * h:128 * h + 128], yb[h][0][:, 0:128], 256.0, A.is_ge, [yb[h][1]], ["SG%d" % h], -256.0, A.mult)
+        tt(T.Y[:, 0:128], T.PY[:, 0:128], T.SG[:, 0:128], A.add, ["P:Y", "SG0"], ["Y0"])
         cp(T.CR[:, 0:na], T.PC0[:, 0:na], ["P:C0"], ["CRa"])
-        tt(T.Y[:, 0:256], T.PY[:, 0:256], T.SG[:], A.add, ["P:Y", "SG"], ["Ya"])
-        act(T.Y[:, 256:512], T.Y[:, 0:256], F.Copy, ["Ya"], ["Yb"])
+        tt(T.Y[:, 128:256], T.PD0[:, 0:128], T.SG[:, 128:256], A.add, ["P:D0", "SG1"], ["Ya"])
+        act(T.Y[:, 256:512], T.Y[:, 0:256], F.Copy, ["Y0", "Ya"], ["Yb"])
         ts(T.C32[:, 0:na], T.CR[:, 0:na], 2047, A.bitwise_and, ["CRa"], ["C32a"])
-        cp(T.CU[:, 0:na], T.C32[:, 0:na], ["C32a"], ["CUa"])
         cp(T.CR[:, na:256], T.PC1[:, 0:nb], ["P:C1"], ["CRb"])
+        cp(T.CU[:, 0:na], T.C32[:, 0:na], ["C32a"], ["CUa"])
+        ts(T.C32[:, na:256], T.CR[:, na:256], 2047, A.bitwise_and, ["CRb"], ["C32b"])
 
         def sgather(h, a, bank):
             act(T.D[:, 256 * a:256 * a + 512], XW.indirect(T.CU[:, 16 * a:16 * a + 32]), F.Copy, ["X"] + cuk(a, a + 2), dk(a, a + 2))
-            mm(bank[:], idm(16), T.Y[:], True, False, ["ID16", "Ya", "Yb"], ["P:D%d" % h])
+            mm(bank[:], idm(16), T.Y[:], True, False, ["ID16", "Y0", "Ya", "Yb"], ["P:D%d" % h])
             mm(bank[:], idm(0), T.D[:, 256 * a:256 * a + 512], False, True, ["ID0"] + dk(a, a + 2), ["P:D%d" % h])
 
         dense_open(T.PK0, "P:K0", 0)
         dense_open(T.PK1, "P:K1", 4)
         sgather(0, 0, T.PD0)
         vgather(4, 6)
-        ts(T.C32[:, na:256], T.CR[:, na:256], 2047, A.bitwise_and, ["CRb"], ["C32b"])
+        cp(T.CU[:, na:256], T.C32[:, na:256], ["C32b"], ["CUb"])
         sgather(1, 2, T.PD1)
         quad_open(T.PC0, "P:C0", 0)
         quad_open(T.PC1, "P:C1", 1)
-        vgather(6, 7)
-        cp(T.CU[:, na:256], T.C32[:, na:256], ["C32b"], ["CUb"])
-        vgather(7, 8)
+        vgather(6, 8)
         act(T.AB[:, 0:512], T.PD0[:], F.Abs, ["P:D0"], ak(0, 2))
+        sabs(4, 6)
         act(T.AB[:, 512:1024], T.PD1[:], F.Abs, ["P:D1"], ak(2, 4))
         dense(T.PK0, "P:K0", 0)
-        sabs(4, 8)
+        sabs(6, 8)
         dense(T.PK1, "P:K1", 4)
         vgather(8, 10)
         vgather(10, 12)
@@ -431,9 +440,9 @@ def rank_program(g, core, T, topo):
         vgather(14, 15)
         tt(T.R1[:], T.PK1[:, 0:64], T.R0[:], A.min, ["P:K1", "R0"], ["R1"])
         sabs(14, 15)
-        quad(14, T.AB, 4)
         vgather(15, 16)
         quad(15, T.D, 2)
+        quad(14, T.AB, 4)
         tt(T.R3[:], T.R1[:, 0:32], T.R1[:, 32:64], A.min, ["R1"], ["R3"])
         vrelu(15, 16)
         quad(15, T.AB, 1)
@@ -441,30 +450,42 @@ def rank_program(g, core, T, topo):
         mm(T.PH[:, 0:128], idm(0), T.PEN[:, 0:128], True, False, ["ID0", "PEN"], ["P:H"])
         mm(T.PD0[:, 0:128], idm(0), T.PEN[:, 0:128], True, False, ["ID0", "PEN"], ["P:D0"])
         for bank, key, a in ((T.PY, "P:Y", 128), (T.PD1, "P:D1", 0)):
-            mm(bank[:, 0:128], idm(17), T.Y[:, a:a + 128], True, False, ["ID17", "Ya"], [key])
+            mm(bank[:, 0:128], idm(17), T.Y[:, a:a + 128], True, False, ["ID17", "Y0", "Ya"], [key])
             mm(bank[:, 0:128], idm(0), T.QTR[:], False, False, ["ID0", "QTR"], [key])
-        scan(T.L0[:], T.LB[:], T.PC0[:, 0:256], 67108864.0, A.min, A.min, ["LB", "P:C0"], ["L0"])
-        scan(T.SC[:], T.L0[:], T.PC1[:, 0:256], 67108864.0, A.min, A.min, ["L0", "P:C1"], ["SC"])
-        mm(T.PC0[:, 0:128], idm(0), T.NBG[:], True, False, ["ID0", "NBG"], ["P:C0"])
-        mm(T.PC1[:, 0:128], idm(0), T.NBG[:], True, False, ["ID0", "NBG"], ["P:C1"])
-        ts(T.MA[:], T.SC[:, 15:256:16], 255, A.bitwise_and, ["SC"], ["MA"])
-        cp(T.OM[:], T.MA[:], ["MA"], ["OM"])
-        tt(T.GE[:, 0:256], T.C32[:].indirect(T.OM[:]), T.DM[:], A.mult, ["C32a", "C32b", "OM", "DM"], ["GE"])
         e0 = ((T.PD0, "P:D0"), (T.PH, "P:H"))
         e1 = ((T.PK0, "P:K0"), (T.PK1, "P:K1"))
         cb = ((T.PC1, "P:C1"), (T.PC0, "P:C0"))
+        nb2 = ((T.PD1, "P:D1"), (T.PY, "P:Y"))
+        ek = ("EU%d" % (t + 1), "EUh%d" % (t + 1))
+        wide = (slice(0, 128), slice(128, 256))
+        ends = (slice(15, 128, 16), slice(143, 256, 16))
+        thin = (slice(0, 8), slice(8, 16))
         for h in (1, 0):
-            ge = T.GE[:, 128 * h:128 * h + 128]
-            mm(e0[h][0][:, 0:128], T.BON[:], ge, False, True, ["BON", "GE"], [e0[h][1]])
-            mm(e1[h][0][:, 0:128], T.BON[:], ge, True, True, ["BON", "GE"], [e1[h][1]])
-            mm(cb[h][0][:, 0:128], T.BON[:], ge, False, False, ["BON", "GE"], [cb[h][1]])
-        scan(T.SE[:], T.NDM[:], T.GE[:], -1.0, A.mult, A.add, ["NDM", "GE"], ["SE"])
-        E16 = T.SE[:, 15:256:16]
-        ek = "EU%d" % (t + 1)
-        cp(eu(t + 1), E16, ["SE"], [ek])
-        if not last:
+            scan(T.L0[:, wide[h]], T.LB[:, wide[h]], T.PC0[:, wide[h]], 67108864.0, A.min, A.min, ["LB", "P:C0"], ["L0%d" % h])
+        for h in (1, 0):
+            scan(T.SC[:, wide[h]], T.L0[:, wide[h]], T.PC1[:, wide[h]], 67108864.0, A.min, A.min, ["L0%d" % h, "P:C1"], ["SC%d" % h])
+        mm(T.PC0[:, 0:128], idm(0), T.NBG[:], True, False, ["ID0", "NBG"], ["P:C0"])
+        mm(T.PC1[:, 0:128], idm(0), T.NBG[:], True, False, ["ID0", "NBG"], ["P:C1"])
+        for h in (1, 0):
+            ts(T.MA[:, thin[h]], T.SC[:, ends[h]], 255, A.bitwise_and, ["SC%d" % h], ["MA%d" % h])
+        for h in (1, 0):
+            cp(T.OM[:, thin[h]], T.MA[:, thin[h]], ["MA%d" % h], ["OM%d" % h])
+        for h in (1, 0):
+            ge, gk = T.GE[:, wide[h]], "GE%d" % h
+            tt(ge, T.C32[:].indirect(T.OM[:, thin[h]]), T.DM[:, 0:128], A.mult, ["C32a", "C32b", "OM%d" % h, "DM"], [gk])
+            mm(e0[h][0][:, 0:128], T.BON[:], ge, False, True, ["BON", gk], [e0[h][1]])
+            mm(e1[h][0][:, 0:128], T.BON[:], ge, True, True, ["BON", gk], [e1[h][1]])
+            mm(cb[h][0][:, 0:128], T.BON[:], ge, False, False, ["BON", gk], [cb[h][1]])
+        for h in (1, 0):
+            scan(T.SE[:, wide[h]], T.NDM[:, 0:128], T.GE[:, wide[h]], -1.0, A.mult, A.add, ["NDM", "GE%d" % h], ["SE%d" % h])
+
+        def elist(h):
+            cp(eu(t + 1)[:, thin[h]], T.SE[:, ends[h]], ["SE%d" % h], [ek[h]])
+            act(T.XE[:, wide[h]], XW.indirect(eu(t + 1)[:, thin[h]]), F.Copy, ["X", ek[h]], ["XE%d" % h])
+
+        def publish():
             k1 = "T%de%d" % (t + 1, t)
-            cp(TT[t + 1][:, 0:16], E16, ["SE"], [k1])
+            cp(TT[t + 1][:, 0:16], T.SE[:, 15:256:16], ["SE0", "SE1"], [k1])
             src = TT[t + 1][:, 0:16]
             far = [(s, src, TT[s][:, 256 + 16 * (s - 1 - t):272 + 16 * (s - 1 - t)]) for s in range(t + 1, RO)]
             send(far[:1], [k1])
@@ -472,14 +493,13 @@ def rank_program(g, core, T, topo):
                 send(far[1:], [k1])
                 dmas("y", "ce%d" % t, [(TT[s][:, 16 * (s - 1 - t):16 * (s - t)], src, [k1], ["T%de%d" % (s, t)])
                                        for s in range(t + 2, RO)])
-        nb2 = ((T.PD1, "P:D1"), (T.PY, "P:Y"))
 
         def twins(h, k):
-            lo, hi = max(128 * h, 16 * k), 128 * h + 128
+            lo, hi = 128 * h + 16 * k, 128 * h + 128
             bank, key = e0[h] if k == 0 else e1[h]
             eq = T.EQ[:, 256 * k + lo:256 * k + hi]
-            tt(eq, bank[:, lo - 128 * h:128], T.SE[:, lo - 16 * k:hi - 16 * k], A.is_equal, [key, "SE"], ["EQ%d%d" % (h, k)])
-            mm(cb[h][0][:, lo - 128 * h:128], T.B4K[:], eq, False, k == KS - 1, ["B4K", "EQ%d%d" % (h, k)], [cb[h][1]])
+            tt(eq, bank[:, lo - 128 * h:128], T.SE[:, lo - 16 * k:hi - 16 * k], A.is_equal, [key, "SE%d" % h], ["EQ%d%d" % (h, k)])
+            mm(cb[h][0][:, lo - 128 * h:128], T.B4K[:], eq, False, k == KS[h] - 1, ["B4K", "EQ%d%d" % (h, k)], [cb[h][1]])
 
         def xe_sum(h):
             mm(nb2[h][0][:, 0:128], idm(17), T.XE[:, 128 * h:128 * h + 128], False, True, ["ID17", "XE%d" % h], [nb2[h][1]])
@@ -491,39 +511,44 @@ def rank_program(g, core, T, topo):
         def offs(h):
             cp(T.OS[:, 8 * h:8 * h + 8], T.LS[:, 128 * h + 15:128 * h + 128:16], ["LS%d" % h], ["OS%d" % h])
 
-        def scatter(c):
-            cp(T.X[:].indirect(T.OS[:, c:c + KS]), T.NX[:, 16 * c:16 * (c + KS)], ["OS%d" % (c // 8), "NX%d" % (c // 8)], ["X"])
+        def scatter(c, n):
+            cp(T.X[:].indirect(T.OS[:, c:c + n]), T.NX[:, 16 * c:16 * (c + n)], ["OS%d" % (c // 8), "NX%d" % (c // 8)], ["X"])
 
         def newval(h):
             ts(T.NX[:, 128 * h:128 * h + 128], nb2[h][0][:, 0:128], MAGIC, A.add, [nb2[h][1]], ["NX%d" % h], -MAGIC, A.add)
 
-        for h in (1, 0):
-            act(T.XE[:, 128 * h:128 * h + 128], XW.indirect(eu(t + 1)[:, 8 * h:8 * h + 8]), F.Copy, ["X", ek], ["XE%d" % h])
+        elist(1)
         twins(1, 0)
         twins(1, 1)
+        if not last:
+            publish()
         twins(1, 2)
         twins(1, 3)
         xe_sum(1)
+        elist(0)
         twins(0, 0)
         twins(0, 1)
-        xe_sum(0)
         twins(0, 2)
         twins(0, 3)
         pick(1)
         newval(1)
+        xe_sum(0)
+        twins(0, 4)
+        offs(1)
+        twins(0, 5)
+        twins(0, 6)
+        twins(0, 7)
         for h in (1, 0):
             act(T.EB[:, 128 * h:128 * h + 128], e1[h][0][:, 0:128], F.Copy, [e1[h][1]], ["EB%d" % h])
         dmas("y", "ye%d" % t, [(T.yr[RO - 1 - t:128:16, :], T.EB[0:128:16, :], ["EB0", "EB1"], ["yr"])])
         if not last:
             hash_open()
-        offs(1)
-        pick(0)
-        scatter(12)
-        offs(0)
+        scatter(12, 4)
         newval(0)
-        scatter(8)
-        scatter(4)
-        scatter(0)
+        pick(0)
+        scatter(8, 4)
+        offs(0)
+        scatter(0, 8)
 
     dmas("y", "yxa", [(T.yx[0:64, :], T.X[0:64, 0:2048], ["X"], ["yxa"])])
     dmas("s", "yxb", [(T.yx[64:128, :], T.X[64:128, 0:2048], ["X"], ["yxb"])])

@@ -2,9 +2,10 @@ from concourse.bass import DstId, RemoteDMATransfer
 from concourse.mybir import AluOpType as A, AxisListType, ActivationFunctionType as F
 
 N, RO = 8, 4
-KS = (8, 4)
-PA = 16
+CH = ((0, 8), (8, 12), (12, 16))
+KS = (8, 4, 4)
 CA = 8
+QB = 12
 BF, H, FL, I32, U16 = "bfloat16", "float16", "float32", "int32", "uint16"
 
 
@@ -13,35 +14,38 @@ def _sb(n, d):
 
 
 SCRATCH = {
-    "X": _sb(2048 + 128, BF), "RI": _sb(272, I32), "WI": _sb(1, I32), "KI": _sb(1, I32),
-    "RF": _sb(256, FL), "TR": _sb(512, I32), "TL": _sb(16, U16),
+    "X": _sb(2048 + 256, BF), "RI": _sb(272, I32), "WI": _sb(1, I32), "KI": _sb(1, I32),
+    "RF": _sb(256, FL), "TR": _sb(512, I32), "TL": _sb(16, U16), "TH": _sb(512, H),
     "T0": _sb(560, FL), "T1": _sb(560, FL), "T2": _sb(560, FL), "T3": _sb(560, FL),
     "CI": _sb(16, I32), "CF": _sb(32, FL), "AGE": _sb(16, I32),
-    "JL": _sb(256, BF), "IG": _sb(256, BF), "H2": _sb(64, BF), "J": _sb(128, BF), "Q4": _sb(256, BF), "KAQ": _sb(512, BF),
-    "SEL": _sb(720, BF), "ONES": _sb(128, BF), "C1024": _sb(16 * max(CA, 16 - CA), BF),
-    "DM": _sb(256, BF), "NDM": _sb(256, BF), "QC": _sb(256, BF), "PEN": _sb(128, BF), "BON": _sb(128, BF),
+    "JL": _sb(256, BF), "IG": _sb(256, BF), "H2": _sb(64, BF), "J": _sb(192, BF), "J4": _sb(128, BF),
+    "SEL": _sb(6 * 144, BF), "ONES": _sb(128, BF), "C1024": _sb(192, BF), "C248": _sb(64, BF), "MG": _sb(128, BF), "M9": _sb(64, BF),
+    "DM": _sb(256, BF), "NDM": _sb(256, BF), "HK": _sb(256, BF), "HL": _sb(512, BF), "BON": _sb(128, BF), "B4K": _sb(128, BF),
     "ID": _sb(18 * 128, BF), "KM": _sb(2048, H), "KD": _sb(16, H),
-    "HP": _sb(64, BF), "KB": _sb(64, BF), "KT": _sb(512, BF),
-    "EU": _sb(96, U16), "G01": _sb(512, BF), "HS": _sb(64, I32), "HA": _sb(32, I32),
-    "OFF": _sb(32, U16), "FO": _sb(32, BF), "GP": _sb(256, H), "SP": _sb(256, H), "GQ": _sb(256, FL), "SQ": _sb(256, FL),
-    "OP": _sb(16, U16), "OQ": _sb(16, U16), "Q16": _sb(16, H), "PQ": _sb(16, I32), "FI": _sb(16, I32), "F16": _sb(16, H),
-    "XP": _sb(256, BF), "XQ": _sb(256, BF), "SG": _sb(256, BF), "Y": _sb(512, BF),
-    "CR": _sb(256, I32), "C32": _sb(256, I32), "CU": _sb(256, U16),
+    "HP": _sb(64, H), "HQ": _sb(32, BF), "KB": _sb(64, BF), "KT": _sb(256, BF), "KL": _sb(128, BF),
+    "NBG": ("sbuf", [128, 8, 17], H), "TQ": _sb(16, U16),
+    "EU": _sb(96, U16), "G01": _sb(512, BF), "OFF": _sb(32, U16), "FO": _sb(32, BF),
+    "GP": _sb(256, H), "SP": _sb(256, H), "GQ": _sb(256, H), "SQ": _sb(256, H),
+    "OP": _sb(16, U16), "OQ": _sb(16, U16), "PQ": _sb(16, FL), "FI": _sb(16, I32),
+    "XP": _sb(256, BF), "YS": _sb(256, I32), "YI": _sb(256, I32), "Y": _sb(512, BF),
+    "RR": _sb(256, FL), "CR": _sb(256, I32), "C32": _sb(256, I32), "CU": _sb(256, U16),
     "D": _sb(4096, BF), "AB": _sb(4096, BF),
-    "R0": _sb(64, FL), "R1": _sb(64, FL), "R3": _sb(32, FL), "TH": _sb(512, H),
-    "L0": _sb(256, FL), "LB": _sb(256, FL), "SC": _sb(256, I32),
-    "MA": _sb(16, I32), "OM": _sb(16, U16),
-    "GE": _sb(256, H), "SE": _sb(256, H), "EQ": _sb(256 * 8, BF), "LS": _sb(256, FL), "OS": _sb(16, U16),
-    "B4K": _sb(128, BF), "DUI": _sb(128, I32), "DUT": _sb(128, FL), "NBG": _sb(128, BF),
-    "XE": _sb(256, BF), "QTR": _sb(128, BF), "NX": _sb(256, BF), "EB": _sb(256, FL),
+    "R0": _sb(64, FL), "R1": _sb(64, FL), "LB": _sb(256, FL), "SC": _sb(256, I32),
+    "MA": _sb(16, I32), "OM": _sb(16, U16), "OD": _sb(16, U16),
+    "GE": _sb(256, H), "SE": _sb(256, H), "EQ": _sb(256 * 8, BF), "OS": _sb(16, U16),
+    "XE": _sb(256, H), "NX": _sb(256, BF), "EB": _sb(256, FL),
+    "PH": ("psum", [128, 256, 2], FL),
 }
-for _n in ("PH", "PC0", "PC1", "PY", "PD0", "PD1", "PK0", "PK1"):
+for _n in ("PC0", "PC1", "PK0", "PK1"):
     SCRATCH[_n] = ("psum", [128, 512], FL)
+for _n in ("PD0", "PD1", "PY"):
+    SCRATCH[_n] = ("psum", [128, 16, 32], FL)
 
-SEMAPHORES = (["v", "s", "p", "gp", "sent", "lr", "lx", "lw", "lk", "cp", "yr0", "yxa", "yxb"]
+SEMAPHORES = (["v", "s", "p", "gp", "sent", "lr", "lb", "lx", "lw", "lk", "cp", "yr0", "yxa", "yxb"]
               + ["arr%d" % k for k in range(RO)] + ["ce%d" % k for k in range(RO)] + ["ye%d" % k for k in range(RO)])
 
 MAGIC = 12582912.0
+AOFF = -1024.0 - 15.5 / 32
 
 
 def rank_program(g, core, T, topo):
@@ -59,14 +63,14 @@ def rank_program(g, core, T, topo):
             Q[q].wait_ge(T.sem[sem], val)
             waited[(q, sem)] = val
 
-    def deps(q, r, w, loose=False):
+    def deps(q, r, w):
         for k in r:
             t = lastw.get(k)
             if t and not (t[0] == q and (q == "p" or not t[3])):
                 need(q, t[1], t[2])
         for k in w:
             t = lastw.get(k)
-            if t and not (t[0] == q and (q == "p" or loose or not t[3])):
+            if t and not (t[0] == q and (q == "p" or not t[3])):
                 need(q, t[1], t[2])
             for t in readers.get(k, []):
                 if not (t[0] == q == "p"):
@@ -82,8 +86,8 @@ def rank_program(g, core, T, topo):
             lastw[k] = (q, sem, val, True)
             readers[k] = []
 
-    def op(q, fn, r, w, loose=False):
-        deps(q, r, w, loose)
+    def op(q, fn, r, w):
+        deps(q, r, w)
         cnt[q] = cnt.get(q, 0) + 1
         fn().then_inc(T.sem[q], 1)
         note(q, q, cnt[q], r, w)
@@ -99,8 +103,8 @@ def rank_program(g, core, T, topo):
 
     V, S, P = g.vector, g.scalar, g.tensor
 
-    def cp(o, i, r, w, loose=False):
-        op("v", lambda: V.tensor_copy(o, i), r, w, loose)
+    def cp(o, i, r, w):
+        op("v", lambda: V.tensor_copy(o, i), r, w)
 
     def ts(o, i, s1, o1, r, w, s2=None, o2=None):
         if o2 is None:
@@ -113,6 +117,9 @@ def rank_program(g, core, T, topo):
 
     def scan(o, d0, d1, init, o0, o1, r, w):
         op("v", lambda: V.tensor_tensor_scan(o, d0, d1, init, o0, o1), r, w)
+
+    def red(o, i, how, r, w):
+        op("v", lambda: V.tensor_reduce(o, i, AxisListType.X, how), r, w)
 
     def ms(o, c, w):
         op("v", lambda: V.memset(o, c), [], w)
@@ -138,11 +145,23 @@ def rank_program(g, core, T, topo):
     def cf(k):
         return T.CF[:, k:k + 1]
 
+    def cols(bank, a, b):
+        return bank[:, a // 2:b // 2, :] if bank.name == "PH" else bank[:, a:b]
+
     def idm(k):
         return T.ID[:, 128 * k:128 * (k + 1)]
 
-    def sel(which, shift):
-        return T.SEL[:, 144 * which + shift:144 * which + shift + 128]
+    SELS = {"d": (0, 16, 256.0), "q2": (1, 4, 512.0), "qn": (2, 4, -256.0), "h": (3, 8, None), "q": (4, 4, 256.0),
+            "hn": (5, 8, None)}
+
+    def sel(which, k):
+        a, n, _ = SELS[which]
+        return T.SEL[:, 144 * a + n - 1 - k:144 * a + n - 1 - k + 128]
+
+    def make_sel(which, factor=None, r=()):
+        a, n, c = SELS[which]
+        ts(T.SEL[:, 144 * a + n - 1:144 * a + 128:n], T.IG[:, 0:128:n], cf(GF), A.is_equal, ["IG", "gf"] + list(r),
+           ["SEL" + which], c if factor is None else factor, A.mult)
 
     def peer(s):
         return T.cores[(rank - 1 - s) % N]
@@ -179,6 +198,7 @@ def rank_program(g, core, T, topo):
         return share(RO - 1, n) + share(1, n) + sum(share(RO - 2 - t, n) for t in range(s - 1))
 
     dmas("y", "lr", [(T.RI[:, 0:256], T.ring[:], [], ["RI"])])
+    dmas("s", "lb", [(T.RI[:, 256:272], T.ring[:, 0:16], [], ["RIb"])])
     dmas("y", "lw", [(T.WI[:], T.wt[:], [], ["WI"])])
     dmas("y", "lk", [(T.KI[:], T.kap[:], [], ["KI"])])
     dmas("y", "lx", [(XW, T.x[:], [], ["X"])])
@@ -188,92 +208,159 @@ def rank_program(g, core, T, topo):
     iota(T.JL[:], [[0, 16], [1, 16]], 0, 0, ["JL"])
     iota(T.IG[:], [[1, 16], [0, 16]], 0, 0, ["IG"])
     iota(T.H2[:], [[0, 32], [1, 2]], 0, 0, ["H2"])
-    GF, PF, WW, B1, B2, W16, P8, P4, DUM, QF, KF, AN, AC = 0, 1, 2, 3, 4, 5, 6, 7, 8, 9, 10, 11, 12
-    ms(T.SEL[:], 0.0, ["SEL0", "SEL1", "SEL2", "SEL3", "SEL4"])
+    iota(T.KT[0:32, :], [[0, 16], [1, 4], [0, 4]], 0, 0, ["KTa"])
+    iota(T.J4[:], [[0, 8], [1, 4], [0, 4]], 0, 0, ["J4"])
+    GF, PF, WW, B1, B2, W16, W16N, P8, QF, KF, AN, AC = 0, 1, 2, 3, 4, 5, 6, 7, 9, 10, 11, 12
+    QQ, S1, S2, S3 = 20, 21, 22, 23
+    ms(T.SEL[:], 0.0, ["SEL" + k for k in SELS])
+    act(T.LB[:], T.SEL[:, 0:256], F.Copy, ["SELd", "SELq2"], ["LB0", "LB1", "LB2", "LB3"], bias=67108864.0)
+    for buf, key, c in ((T.ONES, "ONES", 1.0), (T.C1024, "C1024", 1024.0), (T.MG, "MG", MAGIC), (T.C248, "C248", 248.0),
+                        (T.M9, "M9", MAGIC * 512)):
+        act(buf[:], T.SEL[:, 0:buf.shape[1]], F.Copy, ["SELd", "SELq2"], [key], bias=c)
     ts(ci(1), ci(0), 4, A.arith_shift_right, ["q"], ["g32"])
     ts(ci(2), ci(0), 15, A.bitwise_and, ["q"], ["p32"])
     ts(ci(3), ci(0), 31, A.bitwise_and, ["q"], ["x32"])
-    ms(T.ONES[:], 1.0, ["ONES"])
     tt(ci(4), ci(0), ci(1), A.add, ["q", "g32"], ["t32"])
     cp(cf(PF), ci(2), ["p32"], ["pf"])
     ts(cf(WW), ci(3), 16.0, A.is_equal, ["x32"], ["ww"], 256.0, A.mult)
-    ms(T.C1024[:], 1024.0, ["C1024"])
-    ms(cf(AC), -1024.0, ["ac0"])
+    ms(cf(AC), AOFF, ["ac0"])
     ts(ci(5), ci(4), 1, A.bitwise_and, ["t32"], ["b0"])
     cp(cf(GF), ci(1), ["g32"], ["gf"])
     ts(cf(B1), cf(PF), 16.0, A.mult, ["pf", "ww"], ["b1"], cf(WW), A.add)
     ts(ci(6), ci(2), 3, A.arith_shift_right, ["p32"], ["p8i"])
-    ms(T.QTR[:], -0.25, ["QTR"])
     ts(cf(B2), ci(5), 240.0, A.mult, ["b0", "b1"], ["b2"], cf(B1), A.add)
-    ts(ci(7), ci(2), 2, A.arith_shift_right, ["p32"], ["p4i"])
+    ts(cf(QF), cf(PF), -1.0, A.add, ["pf"], ["qf"])
+    ts(cf(S3), cf(PF), 2.0, A.mult, ["pf"], ["s3"], 2048.0, A.add)
     ts(T.TL[:], T.AGE[:], cf(B2), A.add, ["AGE", "b2"], ["TL"])
     cp(cf(P8), ci(6), ["p8i"], ["p8"])
-    cp(cf(P4), ci(7), ["p4i"], ["p4"])
-    ms(T.LB[:], 67108864.0, ["LB"])
-    cp(T.RI[:, 256:272], T.RI[:, 0:16], ["RI"], ["RIb"])
+    ts(T.DM[:], T.JL[:, 0:256], cf(PF), A.is_equal, ["JL", "pf"], ["DM"])
     op("v", lambda: V.transpose(T.TR[:, 0:256], T.RI[:, 0:256]), ["RI"], ["TRa"])
     op("v", lambda: V.transpose(T.TR[:, 256:512], T.RI[:, 16:272]), ["RI", "RIb"], ["TRb"])
-    ts(T.DM[:], T.JL[:, 0:256], cf(PF), A.is_equal, ["JL", "pf"], ["DM"])
-    cp(T.TH[:, 0:256], T.TR[:].indirect(T.TL[:]), ["TRa", "TRb", "TL"], ["TH"])
-    send([(0, T.TH[:, 0:256], T.TH[:, 256:512])], ["TH"])
-    cp(T.T0[:, 0:256], T.TH[:, 0:256], ["TH"], ["T0own"])
-    iota(T.Q4[:], [[0, 16], [1, 4], [0, 4]], 0, 0, ["Q4"])
-    iota(T.DUI[:], [[1, 128]], 2048, 0, ["DUI"], small=False)
-    iota(T.J[:], [[1, 128]], 0, 0, ["J"])
-    iota(T.KAQ[:, 0:256], [[1, 16], [0, 4], [16, 4]], 128, 0, ["KAQ0"])
-    iota(T.KAQ[:, 256:512], [[1, 16], [0, 4], [16, 4]], 192, 0, ["KAQ1"])
-    need("gp", "arr0", arrivals(0))
-    send([(s, T.T0[:, 0:256], TT[s][:, 256 + 16 * s:512 + 16 * s]) for s in range(1, RO)], ["T0own"])
-    dmas("y", "cp", [(TT[s][:, 16 * s:256], T.T0[:, 0:256 - 16 * s], ["T0own"], ["T%down" % s]) for s in range(1, RO)])
-
     ts(T.BON[:], T.IG[:, 0:128], cf(GF), A.is_equal, ["IG", "gf"], ["BON"])
     ts(cf(W16), T.WI[:], 16.0, A.mult, ["WI"], ["w16"])
-    cp(T.EU[:, 64:96], T.T0[:, 0:32], ["T0own"], ["EU0", "EU-1"])
+    ts(cf(W16N), T.WI[:], -16.0, A.mult, ["WI"], ["w16n"])
+    cp(T.TH[:, 0:128], T.TR[:].indirect(T.TL[:, 0:8]), ["TRa", "TRb", "TL"], ["TH"])
+    act(T.TH[:, 128:256], T.TR[:].indirect(T.TL[:, 8:16]), F.Copy, ["TRa", "TRb", "TL"], ["THb"])
+    send([(0, T.TH[:, 0:256], T.TH[:, 256:512])], ["TH", "THb"])
+    act(T.T0[:, 0:256], T.TR[:].indirect(T.TL[:]), F.Copy, ["TRa", "TRb", "TL"], ["T0own"])
+    iota(T.J[:], [[1, 192]], 0, 0, ["J"])
+    need("gp", "gp", cnt["gp"])
+    iota(T.KT[32:64, :], [[-1, 16], [0, 16]], 15, 0, ["KTb"])
+    need("gp", "gp", cnt["gp"])
+    iota(T.KT[64:96, :], [[1, 16], [0, 4], [16, 4]], 16 * QB, 0, ["KTc"])
+    need("gp", "arr0", arrivals(0))
+    send([(s, T.T0[:, 0:256], TT[s][:, 256 + 16 * s:512 + 16 * s]) for s in range(1, RO)], ["T0own"])
+    need("y", "arr0", arrivals(0))
+    dmas("y", "cp", [(TT[s][:, 16 * s:256], T.T0[:, 0:256 - 16 * s], ["T0own"], ["T%down" % s]) for s in range(1, RO)])
+
     tt(idm(0), T.DM[:, 0:128], T.BON[:], A.mult, ["DM", "BON"], ["ID0"])
-    ts(T.SEL[:, 432 + 7:432 + 128:8], T.IG[:, 0:128:8], cf(GF), A.is_equal, ["IG", "gf", "w16"], ["SEL3"], cf(W16), A.mult)
-    ts(T.HP[:], T.H2[:], cf(P8), A.not_equal, ["H2", "p8"], ["HP"], -4194304.0, A.mult)
+    ts(T.HQ[:], T.H2[:, 0:32], cf(P8), A.not_equal, ["H2", "p8"], ["HQ"], -1024.0, A.mult)
+    cp(T.EU[:, 64:96], T.TH[:, 0:32], ["TH"], ["EU0", "EU-1"])
+    make_sel("h", cf(W16), ["w16"])
+    make_sel("hn", cf(W16N), ["w16n"])
+    act(idm(16), idm(0), F.Copy, ["ID0"], ["ID16"], scale=-1.0)
+    for k in (0, 1):
+        tt(T.HP[:, 32 * k:32 * k + 32], T.HQ[:], T.IG[:, 0:256:8], A.add, ["HQ", "IG"], ["HP%d" % k])
     cp(cf(KF), T.KI[:], ["KI"], ["kf"])
+    ts(T.HK[:], T.JL[:], 15.0, A.is_equal, ["JL"], ["HK"], 4096.0, A.mult)
+    ts(T.HL[:, 0:256], T.JL[:], cf(QF), A.is_equal, ["JL", "qf"], ["HL"], 2048.0, A.mult)
+    ts(T.KD[:], T.DM[:, 0:16], cf(KF), A.mult, ["DM", "kf"], ["KD"])
+    mm(T.PK1[:, 0:16], T.BON[:], T.KD[:], True, True, ["BON", "KD"], ["P:K1"])
+    ts(T.HL[:, 256:512], T.JL[:], cf(PF), A.is_equal, ["JL", "pf"], ["HM"], -2048.0, A.mult)
+    mm(T.PY[:, 0:8, :], idm(0), T.HK[:], True, False, ["ID0", "HK"], ["P:Y"])
+    mm(T.PY[:, 0:8, :], idm(0), T.HL[:, 0:256], False, False, ["ID0", "HL"], ["P:Y"])
+    mm(T.PY[:, 0:8, :], idm(0), T.HL[:, 256:512], False, True, ["ID0", "HM"], ["P:Y"])
 
     def late_scalar():
-        act(idm(16), idm(0), F.Copy, ["ID0"], ["ID16"], scale=-1.0)
-        act(idm(17), idm(0), F.Copy, ["ID0"], ["ID17"], scale=0.5)
+        act(T.NDM[:], T.DM[:], F.Copy, ["DM"], ["NDM"], scale=-1.0, bias=1.0)
+        act(T.HK[:], T.PY[:, 0:8, :], F.Copy, ["P:Y"], ["HK"])
         for m in range(1, 16):
             act(idm(m), idm(0), F.Copy, ["ID0"], ["ID%d" % m], scale=float(2 * m + 1))
+        act(idm(17), idm(0), F.Copy, ["ID0"], ["ID17"], scale=0.5)
+        act(T.KB[:], T.JL[:, 0:64], F.Copy, ["JL"], ["KB"], scale=-1048576.0, bias=15728640.0)
+        act(T.B4K[:], T.BON[:], F.Copy, ["BON"], ["B4K"], scale=4096.0)
+        act(T.NBG[:, :, 0:16], T.DM[:, 0:128], F.Copy, ["DM"], ["NBG"], scale=-36864.0, bias=32768.0)
+        act(T.RF[:], T.RI[:, 0:256], F.Copy, ["RI"], ["RFa"])
+        dmas("y", "yr0", [(T.yr[4:128, :], T.RF[0:124, 0:256], ["RFa"], ["yr"])])
 
-    def mid_vector():
-        ts(T.KD[:], T.DM[:, 0:16], cf(KF), A.mult, ["DM", "kf"], ["KD"])
-        mm(T.PK1[:, 0:16], T.BON[:], T.KD[:], True, True, ["BON", "KD"], ["P:K1"])
-        ts(T.NDM[:], T.JL[:], cf(PF), A.not_equal, ["JL", "pf"], ["NDM"])
-
-    def late_vector():
-        ts(T.QC[:], T.DM[:], 68157440.0, A.mult, ["DM"], ["QC"], -1048576.0, A.add)
-        ts(cf(QF), cf(PF), -1048576.0, A.mult, ["pf"], ["qf"], 15728640.0, A.add)
+    def kaps():
         for m in range(16):
             ts(T.KM[:, 128 * m:128 * (m + 1)], idm(0), T.PK1[:, m:m + 1], A.mult, ["ID0", "P:K1"], ["KM%d" % m])
 
-    def last_vector():
-        ts(T.SEL[:, 15:128:16], T.IG[:, 0:128:16], cf(GF), A.is_equal, ["IG", "gf"], ["SEL0"], 256.0, A.mult)
-        ts(T.SEL[:, 144 + 3:144 + 128:4], T.IG[:, 0:128:4], cf(GF), A.is_equal, ["IG", "gf"], ["SEL1"], 512.0, A.mult)
-        ts(T.SEL[:, 288 + 3:288 + 128:4], T.IG[:, 0:128:4], cf(GF), A.is_equal, ["IG", "gf"], ["SEL2"], -256.0, A.mult)
-        ts(T.KB[:], T.JL[:, 0:64], -1048576.0, A.mult, ["JL"], ["KB"], 15728640.0, A.add)
-        ts(T.SEL[:, 576 + 3:576 + 128:4], T.IG[:, 0:128:4], cf(GF), A.is_equal, ["IG", "gf"], ["SEL4"], 256.0, A.mult)
-        ts(T.KT[:, 0:256], T.Q4[:], cf(P4), A.not_equal, ["Q4", "p4"], ["KTa"], 33554432.0, A.mult)
-        ts(T.KT[:, 256:512], T.IG[:], -1048576.0, A.mult, ["IG"], ["KTb"], 15728640.0, A.add)
-
-    def gap_vector():
-        ts(T.PEN[:], T.DM[:, 0:128], -4096.0, A.mult, ["DM"], ["PEN"])
-        ts(T.B4K[:], T.BON[:], 4096.0, A.mult, ["BON"], ["B4K"])
-        ts(T.NBG[:], T.NDM[:, 0:128], 4194304.0, A.mult, ["NDM"], ["NBG"])
-        cp(T.RF[:], T.RI[:, 0:256], ["RI"], ["RFa"])
-        dmas("y", "yr0", [(T.yr[4:128, :], T.RF[0:124, 0:256], ["RFa"], ["yr"])])
+    def late_vector():
+        for k in ("d", "q2", "qn", "q"):
+            make_sel(k)
+        ts(T.TQ[:], T.JL[:, 0:256:16], cf(PF), A.add, ["JL", "pf"], ["TQ"])
+        ts(T.NBG[:, :, 16], T.IG[:, 0:128:16], 32.0, A.mult, ["IG", "s3"], ["NBGb"], cf(S3), A.add)
+        cp(cf(QQ), ci(0), ["q"], ["qq"])
+        ts(cf(S1), ci(0), 32.0, A.is_equal, ["q"], ["s1"], 1048576.0, A.mult)
+        ts(T.KT[0:32, :], T.KT[0:32, :], T.CF[0:32, QQ:QQ + 1], A.not_equal, ["KTa", "qq"], ["KTa"], 33554432.0, A.mult)
+        ts(cf(S2), ci(0), 64.0, A.is_equal, ["q", "s1"], ["s2"], cf(S1), A.add)
+        ts(T.KL[:], T.J4[:], cf(QQ), A.is_equal, ["J4", "qq", "s2"], ["KL"], cf(S2), A.add)
 
     def eu(k):
         return T.EU[:, 64 - 16 * k:80 - 16 * k]
 
     def hash_open():
-        mm(T.PH[:, 0:64], idm(0), T.HP[:], True, False, ["ID0", "HP"], ["P:H"])
-        mm(T.PH[:, 0:32], idm(0), T.IG[:, 0:256:8], False, False, ["ID0", "IG"], ["P:H"])
-        mm(T.PH[:, 32:64], idm(0), T.IG[:, 0:256:8], False, False, ["ID0", "IG"], ["P:H"])
+        mm(T.PH[:, 0:32, :], idm(0), T.C248[:], True, False, ["ID0", "C248"], ["P:H"])
+
+    wide = (slice(0, 128), slice(128, 256))
+    thin = (slice(0, 8), slice(8, 16))
+    P16, Q16 = T.SP[:, 15:256:16], T.SQ[:, 15:256:16]
+    rbank = ((T.PC0, "P:C0"), (T.PC1, "P:C1"))
+    blk = (slice(0, 16 * CA), slice(16 * CA, 256))
+    nblk = (CA, 16 - CA)
+
+    def take_p():
+        scan(T.SP[:], T.NDM[:, 0:256], T.GP[:], 0.0, A.mult, A.add, ["NDM", "GP"], ["SP"])
+
+    def take_q():
+        scan(T.SQ[:], T.GQ[:], T.HK[:], 0.0, A.min, A.add, ["HK", "GQ"], ["SQ"])
+
+    def plist():
+        cp(T.OP[:], P16, ["SP"], ["OP0", "OP1"])
+
+    def qlist():
+        cp(T.OQ[:], Q16, ["SQ"], ["OQ"])
+
+    def product():
+        tt(T.PQ[:], P16, Q16, A.mult, ["SP", "SQ"], ["PQ"])
+
+    def cpart(which, h):
+        bank, key = rbank[h]
+        for m in range(CA * h, CA if h == 0 else 16):
+            o = bank[:, 16 * (m - CA * h):16 * (m - CA * h) + 16]
+            if which == "P":
+                mm(o, T.KM[:, 128 * m:128 * (m + 1)], P16, False, False, ["KM%d" % m, "SP"], [key])
+            else:
+                mm(o, idm(m), Q16, False, m in (CA - 1, 15), ["ID%d" % m, "SQ"], [key])
+
+    def xp(h):
+        act(T.XP[:, wide[h]], XW.indirect(T.OP[:, thin[h]]), F.Copy, ["X", "OP%d" % h], ["XP%d" % h])
+
+    def ysum(h):
+        tt(T.YS[:, wide[h]], XW.indirect(T.OQ[:, thin[h]]), T.XP[:, wide[h]], A.add, ["X", "OQ", "XP%d" % h], ["YS%d" % h])
+
+    def yand(h):
+        ts(T.YI[:, wide[h]], T.YS[:, wide[h]], 255, A.bitwise_and, ["YS%d" % h], ["YI%d" % h])
+
+    def ytile(j):
+        act(T.Y[:, 256 * j:256 * j + 256], T.YI[:], F.Copy, ["YI0", "YI1"], ["Y" + "ab"[j]])
+
+    def rr(h):
+        act(T.RR[:, blk[h]], rbank[h][0][:, 0:16 * nblk[h]], F.Copy, [rbank[h][1]], ["RR%d" % h])
+
+    def csum(h):
+        tt(T.CR[:, blk[h]], T.FI[:].indirect(T.TQ[:, 0:nblk[h]]), T.RR[:, blk[h]], A.add, ["FI", "TQ", "RR%d" % h], ["CR%d" % h])
+
+    def cand(h):
+        ts(T.C32[:, blk[h]], T.CR[:, blk[h]], 2047, A.bitwise_and, ["CR%d" % h], ["C32" + "ab"[h]])
+
+    def cu(h):
+        cp(T.CU[:, blk[h]], T.C32[:, blk[h]], ["C32" + "ab"[h]], ["CU" + "ab"[h]])
+
+    kbank = ((T.PK0, "P:K0"), (T.PK1, "P:K1"), (T.PH, "P:H"))
+    dbank = ((T.PD0, "P:D0"), (T.PD1, "P:D1"))
 
     def dk(a, b):
         return ["D%d" % m for m in range(a, b)]
@@ -285,8 +372,8 @@ def rank_program(g, core, T, topo):
         return (["CUa"] if a < CA else []) + (["CUb"] if b > CA else [])
 
     def vgather(a, b):
-        tt(T.D[:, 256 * a:256 * b], XW.indirect(T.CU[:, 16 * a:16 * b]), T.Y[:, 0:256 * (b - a)], A.subtract,
-           ["X", "Y0", "Ya"] + (["Yb"] if b - a > 1 else []) + cuk(a, b), dk(a, b))
+        y, yk = (T.YI[:], ["YI0", "YI1"]) if b - a == 1 else (T.Y[:], ["Ya", "Yb"])
+        tt(T.D[:, 256 * a:256 * b], XW.indirect(T.CU[:, 16 * a:16 * b]), y, A.subtract, ["X"] + yk + cuk(a, b), dk(a, b))
 
     def vrelu(a, b):
         ts(T.AB[:, 256 * a:256 * b], T.D[:, 256 * a:256 * b], 0.0, A.max, dk(a, b), ak(a, b))
@@ -294,198 +381,180 @@ def rank_program(g, core, T, topo):
     def sabs(a, b):
         act(T.AB[:, 256 * a:256 * b], T.D[:, 256 * a:256 * b], F.Abs, dk(a, b), ak(a, b))
 
-    def dense_open(bank, key, a):
-        mm(bank[:, 0:64], idm(0), T.KB[:], True, False, ["ID0", "KB"], [key])
-        mm(bank[:, 0:64], idm(0), T.J[:, 16 * a:16 * a + 64], False, False, ["ID0", "J"], [key])
+    def sgather(a, b):
+        act(T.D[:, 256 * a:256 * b], XW.indirect(T.CU[:, 16 * a:16 * b]), F.Copy, ["X"] + cuk(a, b), dk(a, b))
 
-    def dense(bank, key, a):
+    def yneg(n, j):
+        for k in range(n):
+            mm(dbank[j][0][:, 8 * k:8 * k + 8, :], idm(16), T.Y[:, 0:256], k == 0, False, ["ID16", "Ya"], [dbank[j][1]])
+
+    def xadd(a, b, j):
+        mm(dbank[j][0][:, 0:8 * (b - a), :], idm(0), T.D[:, 256 * a:256 * b], False, True, ["ID0"] + dk(a, b), [dbank[j][1]])
+
+    def pabs(a, b, j):
+        act(T.AB[:, 256 * a:256 * b], dbank[j][0][:, 0:8 * (b - a), :], F.Abs, [dbank[j][1]], ak(a, b))
+
+    def pdiff(a, b, j):
+        act(T.D[:, 256 * a:256 * b], dbank[j][0][:, 0:8 * (b - a), :], F.Copy, [dbank[j][1]], dk(a, b))
+
+    def dense_open(j):
+        bank, key = kbank[j]
+        mm(cols(bank, 0, 64), idm(0), T.KB[:], True, False, ["ID0", "KB"], [key])
+        mm(cols(bank, 0, 64), idm(0), T.J[:, 64 * j:64 * j + 64], False, False, ["ID0", "J"], [key])
+
+    def dense(j):
+        bank, key = kbank[j]
         for p in range(16):
-            mm(bank[:, 0:64], sel(0, 15 - p), T.AB[:, 256 * a + p:256 * (a + 4):16], False, p == 15,
-               ["SEL0"] + ak(a, a + 4), [key])
+            mm(cols(bank, 0, 64), sel("d", p), T.AB[:, 1024 * j + p:1024 * (j + 1):16], False, p == 15,
+               ["SELd"] + ak(4 * j, 4 * j + 4), [key])
 
-    def quad_open(bank, key, j):
-        mm(bank[:, 0:256], idm(0), T.KT[:, 0:256], True, False, ["ID0", "KTa"], [key])
-        mm(bank[:, 0:256], idm(0), T.KT[:, 256:512], False, False, ["ID0", "KTb"], [key])
-        mm(bank[:, 0:256], idm(0), T.KAQ[:, 256 * j:256 * j + 256], False, False, ["ID0", "KAQ%d" % j], [key])
+    def quad_open():
+        mm(T.PC0[:, 0:256], T.KL[0:96, :], T.KT[0:96, :], True, False, ["KL", "KTa", "KTb", "KTc"], ["P:C0"])
 
-    def quad(m, src, which):
-        bank, key = (T.PC0, "P:C0") if m < 12 else (T.PC1, "P:C1")
-        rk = dk(m, m + 1) if which == 2 else ak(m, m + 1)
+    def quad(m, which="q", stop=False):
+        src, rk = (T.D, dk(m, m + 1)) if which == "qn" else (T.AB, ak(m, m + 1))
         for k in range(4):
-            mm(bank[:, m % 4:256:4], sel(which, 3 - k), src[:, 256 * m + k:256 * m + 256:4], False,
-               k == 3 and m % 4 == 3 and which != 2, ["SEL%d" % which] + rk, [key])
+            mm(T.PC0[:, m - QB:256:4], sel(which, k), src[:, 256 * m + k:256 * m + 256:4], False,
+               stop and k == 3, ["SEL" + which] + rk, ["P:C0"])
+
+    def fold(j):
+        if j == 0:
+            act(T.R0[:], T.PK0[:, 0:64], F.Copy, ["P:K0"], ["R0"])
+        else:
+            tt(T.R1[:], T.PK1[:, 0:64], T.R0[:], A.min, ["P:K1", "R0"], ["R1"])
+
+    def put(k):
+        tt(T.LB[:, k:256:16], cols(T.PH, 16 * k, 16 * k + 16), T.R1[:, 16 * k:16 * k + 16], A.min, ["P:H", "R1"], ["LB%d" % k])
+
+    e1 = kbank
+    cb = ((T.PD1, "P:D1"), (T.PD0, "P:D0"), (T.PY, "P:Y"))
+    nb2 = ((T.PC1, "P:C1"), (T.PC0, "P:C0"), (T.PC1, "P:C1"))
+    cn = [b - a for a, b in CH]
+    cw = [slice(16 * a, 16 * b) for a, b in CH]
+    ct = [slice(a, b) for a, b in CH]
+    ce = [slice(16 * a + 15, 16 * b, 16) for a, b in CH]
+
+    def new_open(h):
+        mm(nb2[h][0][:, 0:16 * cn[h]], idm(0), T.Y[:, cw[h]], True, False, ["ID0", "Ya"], [nb2[h][1]])
+
+    def twin_open(h):
+        mm(cb[h][0][:, 0:cn[h], 0:17], idm(0), T.NBG[:, 0:cn[h], :], True, False, ["ID0", "NBG", "NBGb"], [cb[h][1]])
+
+    def least(h):
+        w = cw[h]
+        scan(T.SC[:, w], T.LB[:, w], T.PC0[:, w], 67108864.0, A.min, A.min, ["LB0", "LB1", "LB2", "LB3", "P:C0"], ["SC%d" % h])
+
+    def column(h):
+        ts(T.MA[:, ct[h]], T.SC[:, ce[h]], 255, A.bitwise_and, ["SC%d" % h], ["MA%d" % h])
+
+    def colist(h):
+        cp(T.OM[:, ct[h]], T.MA[:, ct[h]], ["MA%d" % h], ["OM%d" % h])
+
+    def dlist(h):
+        act(T.OD[:, ct[h]], T.MA[:, ct[h]], F.Identity, ["MA%d" % h, "pf"], ["OD%d" % h], scale=16.0, bias=cf(PF))
+
+    def choose(h):
+        tt(T.GE[:, cw[h]], T.C32[:].indirect(T.OM[:, ct[h]]), T.DM[:, 0:16 * cn[h]], A.mult,
+           ["C32a", "C32b", "OM%d" % h, "DM"], ["GE%d" % h])
+
+    def spread(h):
+        ge, gk = T.GE[:, cw[h]], "GE%d" % h
+        mm(cols(e1[h][0], 0, 16 * cn[h]), T.BON[:], ge, True, True, ["BON", gk], [e1[h][1]])
+        mm(cb[h][0][:, 0:cn[h], 0:16], T.BON[:], ge, False, False, ["BON", gk], [cb[h][1]])
+
+    def hold(h):
+        scan(T.SE[:, cw[h]], T.NDM[:, 0:16 * cn[h]], T.GE[:, cw[h]], -1.0, A.mult, A.add, ["NDM", "GE%d" % h], ["SE%d" % h])
+
+    def twins(h, k):
+        lo, hi = 16 * (CH[h][0] + k), 16 * CH[h][1]
+        bank, key = e1[h]
+        eq = T.EQ[:, 256 * k + lo:256 * k + hi]
+        tt(eq, cols(bank, 16 * k, 16 * cn[h]), T.SE[:, lo - 16 * k:hi - 16 * k], A.is_equal, [key, "SE%d" % h], ["EQ%d%d" % (h, k)])
+        mm(cb[h][0][:, k:cn[h], 0:16], T.B4K[:], eq, False, k == KS[h] - 1, ["B4K", "EQ%d%d" % (h, k)], [cb[h][1]])
+
+    def xe(h):
+        act(T.XE[:, cw[h]], T.D[:].indirect(T.OD[:, ct[h]]), F.Copy, dk(0, 16) + ["OD%d" % h], ["XE%d" % h], bias=-0.5)
+
+    def xe_sum(h):
+        bank, key = nb2[h]
+        n = 16 * cn[h]
+        mm(bank[:, 0:n], idm(17), T.XE[:, cw[h]], False, False, ["ID17", "XE%d" % h], [key])
+        mm(bank[:, 0:n], idm(0), T.MG[:, 0:n], False, False, ["ID0", "MG"], [key])
+        mm(bank[:, 0:n], idm(16), T.MG[:, 0:n], False, True, ["ID16", "MG"], [key])
+
+    def newval(h):
+        act(T.NX[:, cw[h]], nb2[h][0][:, 0:16 * cn[h]], F.Copy, [nb2[h][1]], ["NX%d" % h])
+
+    def pick(h):
+        red(T.OS[:, ct[h]], cb[h][0][:, 0:cn[h], 0:17], A.min, [cb[h][1]], ["OS%d" % h])
+
+    def scatter(c, n):
+        h = [a <= c < b for a, b in CH].index(True)
+        cp(T.X[:].indirect(T.OS[:, c:c + n]), T.NX[:, 16 * c:16 * (c + n)], ["OS%d" % h, "NX%d" % h], ["X"])
+
+    def erow(h):
+        act(T.EB[:, cw[h]], cols(e1[h][0], 0, 16 * cn[h]), F.Copy, [e1[h][1]], ["EB%d" % h])
 
     hash_open()
     for t in range(RO):
         Tt = TT[t]
         last = t == RO - 1
-        cp(T.G01[:, 0:256], XW.indirect(eu(t)), ["X", "EU%d" % t], ["G0"])
+        cp(T.G01[:, 0:256], XW.indirect(eu(t)), ["X", "EU%d" % t, "EUh%d" % t, "EUi%d" % t], ["G0"])
         act(T.G01[:, 256:512], XW.indirect(eu(t - 1)), F.Copy, ["X", "EU%d" % (t - 1)], ["G1"])
+        hb = T.PH[:, 0:32, :]
         for k in range(8):
-            mm(T.PH[:, 0:64], sel(3, 7 - k), T.G01[:, k:512:8], False, k == 7, ["SEL3", "G0", "G1"], ["P:H"])
+            mm(hb, sel("hn", k), T.G01[:, k:512:8], False, False, ["SELhn", "G0", "G1"], ["P:H"])
+        mm(hb, idm(0), T.M9[:], False, False, ["ID0", "M9"], ["P:H"])
+        mm(hb, idm(16), T.M9[:], False, False, ["ID16", "M9"], ["P:H"])
+        mm(hb, idm(0), T.HP[:], False, False, ["ID0", "HP0", "HP1"], ["P:H"])
+        for k in range(8):
+            mm(hb, sel("h", k), T.G01[:, k:512:8], False, k == 7, ["SELh", "G0", "G1"], ["P:H"])
         if t == 0:
-            mid_vector()
+            kaps()
             late_scalar()
-        scan(T.HS[:], T.H2[:], T.PH[:, 0:64], 0.0, A.mult, A.max, ["H2", "P:H"], ["HS"])
-        ts(T.HA[:], T.HS[:, 1:64:2], 511, A.bitwise_and, ["HS"], ["HA"])
-        cp(T.OFF[:], T.HA[:], ["HA"], ["OFF"])
+        red(T.OFF[:], hb, A.max, ["P:H"], ["OFF"])
         if not last:
-            ts(T.FO[:], T.HA[:], 256.0, A.is_ge, ["HA"], ["FO"])
-            mm(T.PH[:, 64:96], T.ONES[:], T.FO[:], True, True, ["ONES", "FO"], ["P:H"])
+            ts(T.FO[:], T.OFF[:], 256.0, A.is_ge, ["OFF"], ["FO"])
+            mm(T.PK0[:, 0:32], T.ONES[:], T.FO[:], True, True, ["ONES", "FO"], ["P:K0"])
         if t == 0:
             late_vector()
-            last_vector()
-        na, nb = 16 * CA, 256 - 16 * CA
-        mm(T.PC0[:, 0:na], idm(0), T.C1024[:, 0:na], True, False, ["ID0", "C1024"], ["P:C0"])
-        mm(T.PC1[:, 0:nb], idm(0), T.C1024[:, 0:nb], True, False, ["ID0", "C1024"], ["P:C1"])
+        for h in (0, 1):
+            mm(rbank[h][0][:, 0:16 * nblk[h]], idm(0), T.C1024[:, 0:16 * nblk[h]], True, False, ["ID0", "C1024"], [rbank[h][1]])
         need("v", "arr%d" % t, arrivals(t))
+        need("s", "arr%d" % t, arrivals(t))
         tk = ["T%down" % t] + ["T%de%d" % (t, u) for u in range(t)]
         if t == 0:
-            cp(T.T0[:, 256:512], T.TH[:, 256:512], [], ["T0far"])
-            tt(T.DUT[:], T.DUI[:], T.DM[:, 0:128], A.mult, ["DUI", "DM"], ["DUT"])
-            tk.append("T0far")
-        else:
-            need("s", "arr%d" % t, arrivals(t))
+            cp(T.T0[:, 256:384], T.TH[:, 256:384], [], ["T0far"])
+            act(T.T0[:, 384:512], T.TH[:, 384:512], F.Copy, [], ["T0farb"])
+            tk += ["T0far", "T0farb"]
         tt(T.GP[:], Tt[:, 0:512].indirect(T.OFF[:, 0:16]), T.DM[:], A.mult, tk + ["OFF", "DM"], ["GP"])
-        act(T.GQ[:], Tt[:, 0:512].indirect(T.OFF[:, 16:32]), F.Copy, tk + ["OFF"], ["GQ"])
-        if not last:
-            op("v", lambda: V.tensor_reduce(cf(AN), T.PH[:, 64:96], AxisListType.X, A.add), ["P:H"], ["an"])
-        scan(T.SQ[:], T.QC[:], T.GQ[:], 0.0, A.add, A.min, ["QC", "GQ"], ["SQ"])
-        scan(T.SP[:], T.NDM[:, 0:256], T.GP[:], 0.0, A.mult, A.add, ["NDM", "GP"], ["SP"])
-        if not last:
-            cp(ci(8), cf(AN), ["an"], ["ai"])
-        P16 = T.SP[:, 15:256:16]
+        act(T.GQ[:], Tt[:, 0:512].indirect(T.OFF[:, 16:32]), F.Copy, tk + ["OFF"], ["GQ"], bias=-2048.0)
+        ek = ("EU%d" % (t + 1), "EUh%d" % (t + 1), "EUi%d" % (t + 1))
 
-        def pc(m):
-            if m < CA:
-                return T.PC0[:, 16 * m:16 * m + 16], "P:C0"
-            return T.PC1[:, 16 * (m - CA):16 * (m - CA) + 16], "P:C1"
+        def count(k):
+            if last:
+                return
+            if k == 0:
+                red(cf(AN), T.PK0[:, 0:32], A.add, ["P:K0"], ["an"])
+            elif k == 1:
+                cp(ci(8), cf(AN), ["an"], ["ai"])
+            elif k == 2:
+                ts(ci(9), ci(8), 63, A.bitwise_and, ["ai"], ["aj"])
+            else:
+                act(cf(AC + t + 1), ci(9), F.Copy, ["aj"], ["ac%d" % (t + 1)], bias=AOFF)
 
-        def cpart(which, ms_):
-            for m in ms_:
-                o, k = pc(m)
-                if which == "P":
-                    mm(o, T.KM[:, 128 * m:128 * (m + 1)], P16, False, False, ["KM%d" % m, "SP"], [k])
-                elif which == "Q":
-                    mm(o, idm(m), T.Q16[:], False, False, ["ID%d" % m, "Q16"], [k])
-                else:
-                    mm(o, idm(0), T.F16[:], False, m in (CA - 1, 15), ["ID0", "F16"], [k])
-
-        cpart("P", range(PA))
-        ts(T.OQ[:], T.SQ[:, 15:256:16], cf(QF), A.add, ["SQ", "qf"], ["OQ"])
-        ts(T.Q16[:], T.SQ[:, 15:256:16], cf(QF), A.add, ["SQ", "qf"], ["Q16"])
-        act(T.XQ[:], XW.indirect(T.OQ[:]), F.Copy, ["X", "OQ"], ["XQ"])
-        cp(T.OP[:], P16, ["SP"], ["OP"])
-        if not last:
-            ts(ci(9), ci(8), 63, A.bitwise_and, ["ai"], ["aj"])
-        tt(T.PQ[:], P16, T.Q16[:], A.mult, ["SP", "Q16"], ["PQ"])
-        cp(T.XP[:, 0:128], XW.indirect(T.OP[:, 0:8]), ["X", "OP"], ["XPa"])
-        ts(T.FI[:], T.PQ[:], 5, A.arith_shift_right, ["PQ"], ["FI"], 2047, A.bitwise_and)
-        cp(T.XP[:, 128:256], XW.indirect(T.OP[:, 8:16]), ["X", "OP"], ["XP"])
-        ts(T.F16[:], T.FI[:], cf(AC + t), A.add, ["FI", "ac%d" % t], ["F16"])
-        if not last:
-            ts(cf(AC + t + 1), ci(9), -1024.0, A.add, ["aj"], ["ac%d" % (t + 1)])
-        cpart("Q", range(CA))
-        yb = ((T.PY, "P:Y", "XPa"), (T.PD0, "P:D0", "XP"))
-        for h in (0, 1):
-            mm(yb[h][0][:, 0:128], idm(0), T.XQ[:, 128 * h:128 * h + 128], True, False, ["ID0", "XQ"], [yb[h][1]])
-            mm(yb[h][0][:, 0:128], idm(0), T.XP[:, 128 * h:128 * h + 128], False, True, ["ID0", yb[h][2]], [yb[h][1]])
-        cpart("F", range(CA))
-        cpart("P", range(PA, 16))
-        cpart("Q", range(CA, 16))
-        cpart("F", range(CA, 16))
-        if t == 0:
-            gap_vector()
-        for h in (0, 1):
-            ts(T.SG[:, 128 * h:128 * h + 128], yb[h][0][:, 0:128], 256.0, A.is_ge, [yb[h][1]], ["SG%d" % h], -256.0, A.mult)
-        tt(T.Y[:, 0:128], T.PY[:, 0:128], T.SG[:, 0:128], A.add, ["P:Y", "SG0"], ["Y0"])
-        cp(T.CR[:, 0:na], T.PC0[:, 0:na], ["P:C0"], ["CRa"])
-        tt(T.Y[:, 128:256], T.PD0[:, 0:128], T.SG[:, 128:256], A.add, ["P:D0", "SG1"], ["Ya"])
-        act(T.Y[:, 256:512], T.Y[:, 0:256], F.Copy, ["Y0", "Ya"], ["Yb"])
-        ts(T.C32[:, 0:na], T.CR[:, 0:na], 2047, A.bitwise_and, ["CRa"], ["C32a"])
-        cp(T.CR[:, na:256], T.PC1[:, 0:nb], ["P:C1"], ["CRb"])
-        cp(T.CU[:, 0:na], T.C32[:, 0:na], ["C32a"], ["CUa"])
-        ts(T.C32[:, na:256], T.CR[:, na:256], 2047, A.bitwise_and, ["CRb"], ["C32b"])
-
-        def sgather(h, a, bank):
-            act(T.D[:, 256 * a:256 * a + 512], XW.indirect(T.CU[:, 16 * a:16 * a + 32]), F.Copy, ["X"] + cuk(a, a + 2), dk(a, a + 2))
-            mm(bank[:], idm(16), T.Y[:], True, False, ["ID16", "Y0", "Ya", "Yb"], ["P:D%d" % h])
-            mm(bank[:], idm(0), T.D[:, 256 * a:256 * a + 512], False, True, ["ID0"] + dk(a, a + 2), ["P:D%d" % h])
-
-        dense_open(T.PK0, "P:K0", 0)
-        dense_open(T.PK1, "P:K1", 4)
-        sgather(0, 0, T.PD0)
-        vgather(4, 6)
-        cp(T.CU[:, na:256], T.C32[:, na:256], ["C32b"], ["CUb"])
-        sgather(1, 2, T.PD1)
-        quad_open(T.PC0, "P:C0", 0)
-        quad_open(T.PC1, "P:C1", 1)
-        vgather(6, 8)
-        act(T.AB[:, 0:512], T.PD0[:], F.Abs, ["P:D0"], ak(0, 2))
-        sabs(4, 6)
-        act(T.AB[:, 512:1024], T.PD1[:], F.Abs, ["P:D1"], ak(2, 4))
-        dense(T.PK0, "P:K0", 0)
-        sabs(6, 8)
-        dense(T.PK1, "P:K1", 4)
-        vgather(8, 10)
-        vgather(10, 12)
-        sabs(8, 12)
-        for m in range(8, 12):
-            quad(m, T.AB, 4)
-        vgather(12, 14)
-        cp(T.R0[:], T.PK0[:, 0:64], ["P:K0"], ["R0"])
-        sabs(12, 14)
-        quad(12, T.AB, 4)
-        quad(13, T.AB, 4)
-        vgather(14, 15)
-        tt(T.R1[:], T.PK1[:, 0:64], T.R0[:], A.min, ["P:K1", "R0"], ["R1"])
-        sabs(14, 15)
-        vgather(15, 16)
-        quad(15, T.D, 2)
-        quad(14, T.AB, 4)
-        tt(T.R3[:], T.R1[:, 0:32], T.R1[:, 32:64], A.min, ["R1"], ["R3"])
-        vrelu(15, 16)
-        quad(15, T.AB, 1)
-        tt(T.LB[:, 0:256:16], T.R3[:, 0:16], T.R3[:, 16:32], A.min, ["R3"], ["LB"])
-        mm(T.PH[:, 0:128], idm(0), T.PEN[:, 0:128], True, False, ["ID0", "PEN"], ["P:H"])
-        mm(T.PD0[:, 0:128], idm(0), T.PEN[:, 0:128], True, False, ["ID0", "PEN"], ["P:D0"])
-        for bank, key, a in ((T.PY, "P:Y", 128), (T.PD1, "P:D1", 0)):
-            mm(bank[:, 0:128], idm(17), T.Y[:, a:a + 128], True, False, ["ID17", "Y0", "Ya"], [key])
-            mm(bank[:, 0:128], idm(0), T.QTR[:], False, False, ["ID0", "QTR"], [key])
-        e0 = ((T.PD0, "P:D0"), (T.PH, "P:H"))
-        e1 = ((T.PK0, "P:K0"), (T.PK1, "P:K1"))
-        cb = ((T.PC1, "P:C1"), (T.PC0, "P:C0"))
-        nb2 = ((T.PD1, "P:D1"), (T.PY, "P:Y"))
-        ek = ("EU%d" % (t + 1), "EUh%d" % (t + 1))
-        wide = (slice(0, 128), slice(128, 256))
-        ends = (slice(15, 128, 16), slice(143, 256, 16))
-        thin = (slice(0, 8), slice(8, 16))
-        for h in (1, 0):
-            scan(T.L0[:, wide[h]], T.LB[:, wide[h]], T.PC0[:, wide[h]], 67108864.0, A.min, A.min, ["LB", "P:C0"], ["L0%d" % h])
-        for h in (1, 0):
-            scan(T.SC[:, wide[h]], T.L0[:, wide[h]], T.PC1[:, wide[h]], 67108864.0, A.min, A.min, ["L0%d" % h, "P:C1"], ["SC%d" % h])
-        mm(T.PC0[:, 0:128], idm(0), T.NBG[:], True, False, ["ID0", "NBG"], ["P:C0"])
-        mm(T.PC1[:, 0:128], idm(0), T.NBG[:], True, False, ["ID0", "NBG"], ["P:C1"])
-        for h in (1, 0):
-            ts(T.MA[:, thin[h]], T.SC[:, ends[h]], 255, A.bitwise_and, ["SC%d" % h], ["MA%d" % h])
-        for h in (1, 0):
-            cp(T.OM[:, thin[h]], T.MA[:, thin[h]], ["MA%d" % h], ["OM%d" % h])
-        for h in (1, 0):
-            ge, gk = T.GE[:, wide[h]], "GE%d" % h
-            tt(ge, T.C32[:].indirect(T.OM[:, thin[h]]), T.DM[:, 0:128], A.mult, ["C32a", "C32b", "OM%d" % h, "DM"], [gk])
-            mm(e0[h][0][:, 0:128], T.BON[:], ge, False, True, ["BON", gk], [e0[h][1]])
-            mm(e1[h][0][:, 0:128], T.BON[:], ge, True, True, ["BON", gk], [e1[h][1]])
-            mm(cb[h][0][:, 0:128], T.BON[:], ge, False, False, ["BON", gk], [cb[h][1]])
-        for h in (1, 0):
-            scan(T.SE[:, wide[h]], T.NDM[:, 0:128], T.GE[:, wide[h]], -1.0, A.mult, A.add, ["NDM", "GE%d" % h], ["SE%d" % h])
+        def floor_pq():
+            ts(T.FI[:], T.PQ[:], 1.0 / 32, A.mult, ["PQ", "ac%d" % t], ["FI"], cf(AC + t), A.add)
 
         def elist(h):
-            cp(eu(t + 1)[:, thin[h]], T.SE[:, ends[h]], ["SE%d" % h], [ek[h]])
-            act(T.XE[:, wide[h]], XW.indirect(eu(t + 1)[:, thin[h]]), F.Copy, ["X", ek[h]], ["XE%d" % h])
+            if not last:
+                act(eu(t + 1)[:, ct[h]], T.SE[:, ce[h]], F.Copy, ["SE%d" % h], [ek[h]])
 
         def publish():
+            if last:
+                return
             k1 = "T%de%d" % (t + 1, t)
-            cp(TT[t + 1][:, 0:16], T.SE[:, 15:256:16], ["SE0", "SE1"], [k1])
+            act(TT[t + 1][:, 0:16], T.SE[:, 15:256:16], F.Copy, ["SE0", "SE1", "SE2"], [k1])
             src = TT[t + 1][:, 0:16]
             far = [(s, src, TT[s][:, 256 + 16 * (s - 1 - t):272 + 16 * (s - 1 - t)]) for s in range(t + 1, RO)]
             send(far[:1], [k1])
@@ -494,61 +563,14 @@ def rank_program(g, core, T, topo):
                 dmas("y", "ce%d" % t, [(TT[s][:, 16 * (s - 1 - t):16 * (s - t)], src, [k1], ["T%de%d" % (s, t)])
                                        for s in range(t + 2, RO)])
 
-        def twins(h, k):
-            lo, hi = 128 * h + 16 * k, 128 * h + 128
-            bank, key = e0[h] if k == 0 else e1[h]
-            eq = T.EQ[:, 256 * k + lo:256 * k + hi]
-            tt(eq, bank[:, lo - 128 * h:128], T.SE[:, lo - 16 * k:hi - 16 * k], A.is_equal, [key, "SE%d" % h], ["EQ%d%d" % (h, k)])
-            mm(cb[h][0][:, lo - 128 * h:128], T.B4K[:], eq, False, k == KS[h] - 1, ["B4K", "EQ%d%d" % (h, k)], [cb[h][1]])
+        def estore():
+            dmas("y", "ye%d" % t, [(T.yr[RO - 1 - t:128:16, :], T.EB[0:128:16, :], ["EB0", "EB1", "EB2"], ["yr"])])
 
-        def xe_sum(h):
-            mm(nb2[h][0][:, 0:128], idm(17), T.XE[:, 128 * h:128 * h + 128], False, True, ["ID17", "XE%d" % h], [nb2[h][1]])
+        def next_open():
+            if not last:
+                hash_open()
 
-        def pick(h):
-            scan(T.LS[:, 128 * h:128 * h + 128], T.DUT[:], cb[h][0][:, 0:128], 0.0, A.max, A.min,
-                 ["DUT", cb[h][1]], ["LS%d" % h])
-
-        def offs(h):
-            cp(T.OS[:, 8 * h:8 * h + 8], T.LS[:, 128 * h + 15:128 * h + 128:16], ["LS%d" % h], ["OS%d" % h])
-
-        def scatter(c, n):
-            cp(T.X[:].indirect(T.OS[:, c:c + n]), T.NX[:, 16 * c:16 * (c + n)], ["OS%d" % (c // 8), "NX%d" % (c // 8)], ["X"])
-
-        def newval(h):
-            ts(T.NX[:, 128 * h:128 * h + 128], nb2[h][0][:, 0:128], MAGIC, A.add, [nb2[h][1]], ["NX%d" % h], -MAGIC, A.add)
-
-        elist(1)
-        twins(1, 0)
-        twins(1, 1)
-        if not last:
-            publish()
-        twins(1, 2)
-        twins(1, 3)
-        xe_sum(1)
-        elist(0)
-        twins(0, 0)
-        twins(0, 1)
-        twins(0, 2)
-        twins(0, 3)
-        pick(1)
-        newval(1)
-        xe_sum(0)
-        twins(0, 4)
-        offs(1)
-        twins(0, 5)
-        twins(0, 6)
-        twins(0, 7)
-        for h in (1, 0):
-            act(T.EB[:, 128 * h:128 * h + 128], e1[h][0][:, 0:128], F.Copy, [e1[h][1]], ["EB%d" % h])
-        dmas("y", "ye%d" % t, [(T.yr[RO - 1 - t:128:16, :], T.EB[0:128:16, :], ["EB0", "EB1"], ["yr"])])
-        if not last:
-            hash_open()
-        scatter(12, 4)
-        newval(0)
-        pick(0)
-        scatter(8, 4)
-        offs(0)
-        scatter(0, 8)
+        twin_open(2); count(0); take_p(); cpart("P",0); take_q(); plist(); xp(1); xp(0); product(); qlist(); floor_pq(); ysum(1); ysum(0); cpart("Q",0); rr(0); csum(0); yand(1); yand(0); cand(0); cpart("P",1); cpart("Q",1); dense_open(2); rr(1); csum(1); cu(0); cand(1); ytile(0); dense_open(1); yneg(2,1); yneg(2,0); dense_open(0); ytile(1); sgather(4,6); xadd(4,6,1); sgather(0,2); vgather(2,3); cu(1); vgather(6,8); sabs(6,8); pabs(4,6,1); xadd(0,2,0); quad_open(); dense(1); new_open(2); vgather(3,4); sabs(2,4); vgather(10,12); pabs(0,2,0); dense(0); sabs(10,12); vgather(8,10); sabs(8,10); dense(2); vgather(12,14); sabs(12,14); quad(12); quad(13); vgather(14,15); vgather(15,16); count(1); quad(15,"qn"); fold(0); fold(1); sabs(14,15); quad(14); vrelu(15,16); put(0); put(3); put(1); put(2); pdiff(4, 6, 1); pdiff(0, 2, 0); count(2); count(3); quad(15,"q2",True); least(2); least(0); least(1); new_open(1); column(2); column(0); column(1); dlist(2); dlist(1); xe(2); colist(2); colist(0); colist(1); choose(2); choose(0); hold(2); choose(1); twin_open(0); twin_open(1); spread(2); xe_sum(2); xe(1); dlist(0); spread(0); hold(0); spread(1); twins(2, 2); twins(2, 0); xe_sum(1); twins(2, 1); twins(2, 3); hold(1); elist(0); newval(2); xe(0); erow(2); publish(); newval(1); twins(0, 3); twins(0, 4); twins(0, 2); twins(0, 5); twins(1, 2); twins(0, 0); new_open(0); twins(1, 0); twins(1, 1); twins(1, 3); pick(2); twins(0, 6); twins(0, 1); twins(0, 7); scatter(12, 4); pick(1); xe_sum(0); next_open(); newval(0); erow(0); erow(1); elist(1); estore(); elist(2); pick(0); scatter(8, 4); scatter(0, 8)
 
     dmas("y", "yxa", [(T.yx[0:64, :], T.X[0:64, 0:2048], ["X"], ["yxa"])])
     dmas("s", "yxb", [(T.yx[64:128, :], T.X[64:128, 0:2048], ["X"], ["yxb"])])

@@ -2,8 +2,8 @@ from concourse.bass import DstId, RemoteDMATransfer
 from concourse.mybir import AluOpType as A, AxisListType, ActivationFunctionType as F
 
 N, RO = 8, 4
-CH = ((0, 8), (8, 12), (12, 16))
-KS = (8, 4, 4)
+CH = ((0, 6), (6, 12), (12, 16))
+KS = (6, 6, 4)
 CA = 8
 QB = 12
 BF, H, FL, I32, U16 = "bfloat16", "float16", "float32", "int32", "uint16"
@@ -14,38 +14,39 @@ def _sb(n, d):
 
 
 SCRATCH = {
-    "X": _sb(2048 + 256, BF), "RI": _sb(272, I32), "WI": _sb(1, I32), "KI": _sb(1, I32),
-    "RF": _sb(256, FL), "TR": _sb(512, I32), "TL": _sb(16, U16), "TH": _sb(512, H),
+    "X": _sb(2048 + 256, BF), "RI": _sb(288, I32), "WI": _sb(1, I32), "KI": _sb(1, I32),
+    "RF": _sb(256, FL), "TR": _sb(544, I32), "TL": _sb(16, U16), "TH": _sb(512, H),
     "T0": _sb(560, FL), "T1": _sb(560, FL), "T2": _sb(560, FL), "T3": _sb(560, FL),
     "CI": _sb(16, I32), "CF": _sb(32, FL), "AGE": _sb(16, I32),
     "JL": _sb(256, BF), "IG": _sb(256, BF), "H2": _sb(64, BF), "J": _sb(192, BF), "J4": _sb(128, BF),
     "SEL": _sb(6 * 144, BF), "ONES": _sb(128, BF), "C1024": _sb(192, BF), "C248": _sb(64, BF), "MG": _sb(128, BF), "M9": _sb(64, BF),
-    "DM": _sb(256, BF), "NDM": _sb(256, BF), "HK": _sb(256, BF), "HL": _sb(512, BF), "BON": _sb(128, BF), "B4K": _sb(128, BF),
+    "DM": _sb(256, BF), "NDM": _sb(256, BF), "DM32": _sb(128, BF), "HK": _sb(128, BF), "HL": _sb(256, BF),
+    "BON": _sb(128, BF), "B4K": _sb(128, BF),
     "ID": _sb(18 * 128, BF), "KM": _sb(2048, H), "KD": _sb(16, H),
-    "HP": _sb(64, H), "HQ": _sb(32, BF), "KB": _sb(64, BF), "KT": _sb(256, BF), "KL": _sb(128, BF),
+    "HP": _sb(128, H), "HQ": _sb(64, BF), "HC": _sb(128, BF), "KB": _sb(64, BF), "KT": _sb(256, BF), "KL": _sb(128, BF),
     "NBG": ("sbuf", [128, 8, 17], H), "TQ": _sb(16, U16),
-    "EU": _sb(96, U16), "G01": _sb(512, BF), "OFF": _sb(32, U16), "FO": _sb(32, BF),
+    "EU": _sb(96, U16), "G01": _sb(512, BF), "OFF": _sb(32, U16), "FO": _sb(32, BF), "FS": _sb(32, FL),
     "GP": _sb(256, H), "SP": _sb(256, H), "GQ": _sb(256, H), "SQ": _sb(256, H),
-    "OP": _sb(16, U16), "OQ": _sb(16, U16), "PQ": _sb(16, FL), "FI": _sb(16, I32),
+    "OP": _sb(16, U16), "OQ": _sb(16, U16), "FI": _sb(16, FL),
     "XP": _sb(256, BF), "YS": _sb(256, I32), "YI": _sb(256, I32), "Y": _sb(512, BF),
-    "RR": _sb(256, FL), "CR": _sb(256, I32), "C32": _sb(256, I32), "CU": _sb(256, U16),
+    "RR": _sb(256, I32), "CR": _sb(256, I32), "C32": _sb(256, I32), "CU": _sb(256, U16),
     "D": _sb(4096, BF), "AB": _sb(4096, BF),
     "R0": _sb(64, FL), "R1": _sb(64, FL), "LB": _sb(256, FL), "SC": _sb(256, I32),
     "MA": _sb(16, I32), "OM": _sb(16, U16), "OD": _sb(16, U16),
     "GE": _sb(256, H), "SE": _sb(256, H), "EQ": _sb(256 * 8, BF), "OS": _sb(16, U16),
     "XE": _sb(256, H), "NX": _sb(256, BF), "EB": _sb(256, FL),
-    "PH": ("psum", [128, 256, 2], FL),
 }
-for _n in ("PC0", "PC1", "PK0", "PK1"):
+for _n in ("PC0", "PC1", "PK0"):
     SCRATCH[_n] = ("psum", [128, 512], FL)
+for _n in ("PH", "PK1"):
+    SCRATCH[_n] = ("psum", [128, 128, 4], FL)
 for _n in ("PD0", "PD1", "PY"):
     SCRATCH[_n] = ("psum", [128, 16, 32], FL)
 
-SEMAPHORES = (["v", "s", "p", "gp", "sent", "lr", "lb", "lx", "lw", "lk", "cp", "yr0", "yxa", "yxb"]
+SEMAPHORES = (["v", "s", "p", "gp", "sent", "lr", "lx", "lw", "lk", "cp", "yr0", "yxa", "yxb"]
               + ["arr%d" % k for k in range(RO)] + ["ce%d" % k for k in range(RO)] + ["ye%d" % k for k in range(RO)])
 
 MAGIC = 12582912.0
-AOFF = -1024.0 - 15.5 / 32
 
 
 def rank_program(g, core, T, topo):
@@ -146,13 +147,13 @@ def rank_program(g, core, T, topo):
         return T.CF[:, k:k + 1]
 
     def cols(bank, a, b):
-        return bank[:, a // 2:b // 2, :] if bank.name == "PH" else bank[:, a:b]
+        return bank[:, a // 4:b // 4, :] if bank.name in ("PH", "PK1") else bank[:, a:b]
 
     def idm(k):
         return T.ID[:, 128 * k:128 * (k + 1)]
 
-    SELS = {"d": (0, 16, 256.0), "q2": (1, 4, 512.0), "qn": (2, 4, -256.0), "h": (3, 8, None), "q": (4, 4, 256.0),
-            "hn": (5, 8, None)}
+    SELS = {"d": (0, 16, 256.0), "q2": (1, 4, 512.0), "qn": (2, 4, -256.0), "h": (3, 4, None), "q": (4, 4, 256.0),
+            "hn": (5, 4, None)}
 
     def sel(which, k):
         a, n, _ = SELS[which]
@@ -197,8 +198,7 @@ def rank_program(g, core, T, topo):
             return share(1, n)
         return share(RO - 1, n) + share(1, n) + sum(share(RO - 2 - t, n) for t in range(s - 1))
 
-    dmas("y", "lr", [(T.RI[:, 0:256], T.ring[:], [], ["RI"])])
-    dmas("s", "lb", [(T.RI[:, 256:272], T.ring[:, 0:16], [], ["RIb"])])
+    dmas("y", "lr", [(T.RI[:, 16:272], T.ring[:], [], ["RI"])])
     dmas("y", "lw", [(T.WI[:], T.wt[:], [], ["WI"])])
     dmas("y", "lk", [(T.KI[:], T.kap[:], [], ["KI"])])
     dmas("y", "lx", [(XW, T.x[:], [], ["X"])])
@@ -207,38 +207,35 @@ def rank_program(g, core, T, topo):
     iota(T.AGE[:], [[1, 16]], 0, 0, ["AGE"], small=False)
     iota(T.JL[:], [[0, 16], [1, 16]], 0, 0, ["JL"])
     iota(T.IG[:], [[1, 16], [0, 16]], 0, 0, ["IG"])
-    iota(T.H2[:], [[0, 32], [1, 2]], 0, 0, ["H2"])
+    iota(T.H2[:], [[0, 16], [1, 4]], 0, 0, ["H2"])
+    for k in (0, 1):
+        iota(T.HC[:, 64 * k:64 * k + 64], [[0, 2], [1, 8], [0, 4]], 8 * k, 0, ["HC%d" % k])
     iota(T.KT[0:32, :], [[0, 16], [1, 4], [0, 4]], 0, 0, ["KTa"])
     iota(T.J4[:], [[0, 8], [1, 4], [0, 4]], 0, 0, ["J4"])
-    GF, PF, WW, B1, B2, W16, W16N, P8, QF, KF, AN, AC = 0, 1, 2, 3, 4, 5, 6, 7, 9, 10, 11, 12
-    QQ, S1, S2, S3 = 20, 21, 22, 23
+    GF, PF, B1, B2, W16, W16N, P4, QF, KF, AN, AC = 0, 1, 3, 4, 5, 6, 7, 9, 10, 11, 12
+    QQ, S1, S2, S3, S4 = 20, 21, 22, 23, 24
     ms(T.SEL[:], 0.0, ["SEL" + k for k in SELS])
     act(T.LB[:], T.SEL[:, 0:256], F.Copy, ["SELd", "SELq2"], ["LB0", "LB1", "LB2", "LB3"], bias=67108864.0)
-    for buf, key, c in ((T.ONES, "ONES", 1.0), (T.C1024, "C1024", 1024.0), (T.MG, "MG", MAGIC), (T.C248, "C248", 248.0),
-                        (T.M9, "M9", MAGIC * 512)):
-        act(buf[:], T.SEL[:, 0:buf.shape[1]], F.Copy, ["SELd", "SELq2"], [key], bias=c)
+    for buf, key, c in ((T.ONES[:], "ONES", 1.0), (T.C1024[:], "C1024", 1024.0), (T.MG[:], "MG", MAGIC), (T.C248[:], "C248", 248.0),
+                        (T.M9[:], "M9", MAGIC * 512)):
+        act(buf, T.SEL[:, 0:buf.shape[1]], F.Copy, ["SELd", "SELq2"], [key], bias=c)
     ts(ci(1), ci(0), 4, A.arith_shift_right, ["q"], ["g32"])
     ts(ci(2), ci(0), 15, A.bitwise_and, ["q"], ["p32"])
-    ts(ci(3), ci(0), 31, A.bitwise_and, ["q"], ["x32"])
+    ms(T.RI[:, 0:16], 0, ["RIa"])
+    ms(T.RI[:, 272:288], 0, ["RIb"])
     tt(ci(4), ci(0), ci(1), A.add, ["q", "g32"], ["t32"])
     cp(cf(PF), ci(2), ["p32"], ["pf"])
-    ts(cf(WW), ci(3), 16.0, A.is_equal, ["x32"], ["ww"], 256.0, A.mult)
-    ms(cf(AC), AOFF, ["ac0"])
+    ms(cf(AC), -1024.0 - 15.5 / 32, ["ac0"])
     ts(ci(5), ci(4), 1, A.bitwise_and, ["t32"], ["b0"])
     cp(cf(GF), ci(1), ["g32"], ["gf"])
-    ts(cf(B1), cf(PF), 16.0, A.mult, ["pf", "ww"], ["b1"], cf(WW), A.add)
-    ts(ci(6), ci(2), 3, A.arith_shift_right, ["p32"], ["p8i"])
-    ts(cf(B2), ci(5), 240.0, A.mult, ["b0", "b1"], ["b2"], cf(B1), A.add)
-    ts(cf(QF), cf(PF), -1.0, A.add, ["pf"], ["qf"])
-    ts(cf(S3), cf(PF), 2.0, A.mult, ["pf"], ["s3"], 2048.0, A.add)
+    ts(cf(B1), cf(PF), 16.0, A.mult, ["pf"], ["b1"])
+    ts(ci(6), ci(2), 2, A.arith_shift_right, ["p32"], ["p4i"])
+    ts(cf(B2), ci(5), 272.0, A.mult, ["b0", "b1"], ["b2"], cf(B1), A.add)
     ts(T.TL[:], T.AGE[:], cf(B2), A.add, ["AGE", "b2"], ["TL"])
-    cp(cf(P8), ci(6), ["p8i"], ["p8"])
+    op("v", lambda: V.transpose(T.TR[:, 0:256], T.RI[:, 16:272]), ["RI"], ["TRa"])
+    op("v", lambda: V.transpose(T.TR[:, 256:544], T.RI[:]), ["RI", "RIa", "RIb"], ["TRb"])
     ts(T.DM[:], T.JL[:, 0:256], cf(PF), A.is_equal, ["JL", "pf"], ["DM"])
-    op("v", lambda: V.transpose(T.TR[:, 0:256], T.RI[:, 0:256]), ["RI"], ["TRa"])
-    op("v", lambda: V.transpose(T.TR[:, 256:512], T.RI[:, 16:272]), ["RI", "RIb"], ["TRb"])
     ts(T.BON[:], T.IG[:, 0:128], cf(GF), A.is_equal, ["IG", "gf"], ["BON"])
-    ts(cf(W16), T.WI[:], 16.0, A.mult, ["WI"], ["w16"])
-    ts(cf(W16N), T.WI[:], -16.0, A.mult, ["WI"], ["w16n"])
     cp(T.TH[:, 0:128], T.TR[:].indirect(T.TL[:, 0:8]), ["TRa", "TRb", "TL"], ["TH"])
     act(T.TH[:, 128:256], T.TR[:].indirect(T.TL[:, 8:16]), F.Copy, ["TRa", "TRb", "TL"], ["THb"])
     send([(0, T.TH[:, 0:256], T.TH[:, 256:512])], ["TH", "THb"])
@@ -253,47 +250,53 @@ def rank_program(g, core, T, topo):
     need("y", "arr0", arrivals(0))
     dmas("y", "cp", [(TT[s][:, 16 * s:256], T.T0[:, 0:256 - 16 * s], ["T0own"], ["T%down" % s]) for s in range(1, RO)])
 
+    cp(cf(P4), ci(6), ["p4i"], ["p4"])
+    ts(cf(W16), T.WI[:], 16.0, A.mult, ["WI"], ["w16"])
+    ts(cf(W16N), T.WI[:], -16.0, A.mult, ["WI"], ["w16n"])
     tt(idm(0), T.DM[:, 0:128], T.BON[:], A.mult, ["DM", "BON"], ["ID0"])
-    ts(T.HQ[:], T.H2[:, 0:32], cf(P8), A.not_equal, ["H2", "p8"], ["HQ"], -1024.0, A.mult)
+    ts(cf(QF), cf(PF), -1.0, A.add, ["pf"], ["qf"])
+    ts(cf(S3), cf(PF), 2.0, A.mult, ["pf"], ["s3"], 2048.0, A.add)
+    ts(T.HQ[:], T.H2[:], cf(P4), A.not_equal, ["H2", "p4"], ["HQ"], -1024.0, A.mult)
     cp(T.EU[:, 64:96], T.TH[:, 0:32], ["TH"], ["EU0", "EU-1"])
     make_sel("h", cf(W16), ["w16"])
     make_sel("hn", cf(W16N), ["w16n"])
     act(idm(16), idm(0), F.Copy, ["ID0"], ["ID16"], scale=-1.0)
     for k in (0, 1):
-        tt(T.HP[:, 32 * k:32 * k + 32], T.HQ[:], T.IG[:, 0:256:8], A.add, ["HQ", "IG"], ["HP%d" % k])
+        tt(T.HP[:, 64 * k:64 * k + 64], T.HQ[:], T.HC[:, 64 * k:64 * k + 64], A.add, ["HQ", "HC%d" % k], ["HP%d" % k])
     cp(cf(KF), T.KI[:], ["KI"], ["kf"])
-    ts(T.HK[:], T.JL[:], 15.0, A.is_equal, ["JL"], ["HK"], 4096.0, A.mult)
-    ts(T.HL[:, 0:256], T.JL[:], cf(QF), A.is_equal, ["JL", "qf"], ["HL"], 2048.0, A.mult)
-    ts(T.KD[:], T.DM[:, 0:16], cf(KF), A.mult, ["DM", "kf"], ["KD"])
-    mm(T.PK1[:, 0:16], T.BON[:], T.KD[:], True, True, ["BON", "KD"], ["P:K1"])
-    ts(T.HL[:, 256:512], T.JL[:], cf(PF), A.is_equal, ["JL", "pf"], ["HM"], -2048.0, A.mult)
-    mm(T.PY[:, 0:8, :], idm(0), T.HK[:], True, False, ["ID0", "HK"], ["P:Y"])
-    mm(T.PY[:, 0:8, :], idm(0), T.HL[:, 0:256], False, False, ["ID0", "HL"], ["P:Y"])
-    mm(T.PY[:, 0:8, :], idm(0), T.HL[:, 256:512], False, True, ["ID0", "HM"], ["P:Y"])
+    ts(T.HK[:], T.JL[:, 0:128], 15.0, A.is_equal, ["JL"], ["HK"], 4096.0, A.mult)
+    ts(T.HL[:, 0:128], T.JL[:, 0:128], cf(QF), A.is_equal, ["JL", "qf"], ["HL"], 2048.0, A.mult)
+    ts(T.KD[:], T.DM[:, 0:16], cf(KF), A.mult, ["DM", "kf"], ["KD"], 32.0, A.mult)
+    mm(T.PK0[:, 0:16], T.BON[:], T.KD[:], True, True, ["BON", "KD"], ["P:K0"])
+    ts(T.HL[:, 128:256], T.JL[:, 0:128], cf(PF), A.is_equal, ["JL", "pf"], ["HM"], -2048.0, A.mult)
+    mm(T.PY[:, 0:4, :], idm(0), T.HK[:], True, False, ["ID0", "HK"], ["P:Y"])
+    mm(T.PY[:, 0:4, :], idm(0), T.HL[:, 0:128], False, False, ["ID0", "HL"], ["P:Y"])
+    mm(T.PY[:, 0:4, :], idm(0), T.HL[:, 128:256], False, True, ["ID0", "HM"], ["P:Y"])
 
     def late_scalar():
         act(T.NDM[:], T.DM[:], F.Copy, ["DM"], ["NDM"], scale=-1.0, bias=1.0)
-        act(T.HK[:], T.PY[:, 0:8, :], F.Copy, ["P:Y"], ["HK"])
+        act(T.DM32[:], T.DM[:, 0:128], F.Copy, ["DM"], ["DM32"], scale=1.0 / 32)
+        act(T.HK[:], T.PY[:, 0:4, :], F.Copy, ["P:Y"], ["HK"])
         for m in range(1, 16):
             act(idm(m), idm(0), F.Copy, ["ID0"], ["ID%d" % m], scale=float(2 * m + 1))
         act(idm(17), idm(0), F.Copy, ["ID0"], ["ID17"], scale=0.5)
         act(T.KB[:], T.JL[:, 0:64], F.Copy, ["JL"], ["KB"], scale=-1048576.0, bias=15728640.0)
         act(T.B4K[:], T.BON[:], F.Copy, ["BON"], ["B4K"], scale=4096.0)
         act(T.NBG[:, :, 0:16], T.DM[:, 0:128], F.Copy, ["DM"], ["NBG"], scale=-36864.0, bias=32768.0)
-        act(T.RF[:], T.RI[:, 0:256], F.Copy, ["RI"], ["RFa"])
+        act(T.RF[:], T.RI[:, 16:272], F.Copy, ["RI"], ["RFa"])
         dmas("y", "yr0", [(T.yr[4:128, :], T.RF[0:124, 0:256], ["RFa"], ["yr"])])
 
     def kaps():
         for m in range(16):
-            ts(T.KM[:, 128 * m:128 * (m + 1)], idm(0), T.PK1[:, m:m + 1], A.mult, ["ID0", "P:K1"], ["KM%d" % m])
+            ts(T.KM[:, 128 * m:128 * (m + 1)], idm(0), T.PK0[:, m:m + 1], A.mult, ["ID0", "P:K0"], ["KM%d" % m])
 
     def late_vector():
         for k in ("d", "q2", "qn", "q"):
             make_sel(k)
-        ts(T.TQ[:], T.JL[:, 0:256:16], cf(PF), A.add, ["JL", "pf"], ["TQ"])
         ts(T.NBG[:, :, 16], T.IG[:, 0:128:16], 32.0, A.mult, ["IG", "s3"], ["NBGb"], cf(S3), A.add)
         cp(cf(QQ), ci(0), ["q"], ["qq"])
         ts(cf(S1), ci(0), 32.0, A.is_equal, ["q"], ["s1"], 1048576.0, A.mult)
+        ts(T.TQ[:], T.JL[:, 0:256:16], cf(PF), A.add, ["JL", "pf"], ["TQ"])
         ts(T.KT[0:32, :], T.KT[0:32, :], T.CF[0:32, QQ:QQ + 1], A.not_equal, ["KTa", "qq"], ["KTa"], 33554432.0, A.mult)
         ts(cf(S2), ci(0), 64.0, A.is_equal, ["q", "s1"], ["s2"], cf(S1), A.add)
         ts(T.KL[:], T.J4[:], cf(QQ), A.is_equal, ["J4", "qq", "s2"], ["KL"], cf(S2), A.add)
@@ -301,45 +304,67 @@ def rank_program(g, core, T, topo):
     def eu(k):
         return T.EU[:, 64 - 16 * k:80 - 16 * k]
 
-    def hash_open():
-        mm(T.PH[:, 0:32, :], idm(0), T.C248[:], True, False, ["ID0", "C248"], ["P:H"])
-
     wide = (slice(0, 128), slice(128, 256))
     thin = (slice(0, 8), slice(8, 16))
+    ends = (slice(15, 128, 16), slice(143, 256, 16))
     P16, Q16 = T.SP[:, 15:256:16], T.SQ[:, 15:256:16]
+    hbank = ((T.PH, "P:H"), (T.PK1, "P:K1"))
     rbank = ((T.PC0, "P:C0"), (T.PC1, "P:C1"))
     blk = (slice(0, 16 * CA), slice(16 * CA, 256))
     nblk = (CA, 16 - CA)
 
-    def take_p():
-        scan(T.SP[:], T.NDM[:, 0:256], T.GP[:], 0.0, A.mult, A.add, ["NDM", "GP"], ["SP"])
+    def hash_open(h):
+        mm(hbank[h][0][:, 0:16, :], idm(0), T.C248[:], True, False, ["ID0", "C248"], [hbank[h][1]])
 
-    def take_q():
-        scan(T.SQ[:], T.GQ[:], T.HK[:], 0.0, A.min, A.add, ["HK", "GQ"], ["SQ"])
+    def ages(h):
+        hb, key = hbank[h][0][:, 0:16, :], hbank[h][1]
+        gk = ["GA%d" % h, "GB%d" % h]
+        for k in range(4):
+            mm(hb, sel("hn", k), T.G01[:, 256 * h + k:256 * h + 256:4], False, False, ["SELhn"] + gk, [key])
+        mm(hb, idm(0), T.M9[:], False, False, ["ID0", "M9"], [key])
+        mm(hb, idm(16), T.M9[:], False, False, ["ID16", "M9"], [key])
+        mm(hb, idm(0), T.HP[:, 64 * h:64 * h + 64], False, False, ["ID0", "HP%d" % h], [key])
+        for k in range(4):
+            mm(hb, sel("h", k), T.G01[:, 256 * h + k:256 * h + 256:4], False, k == 3, ["SELh"] + gk, [key])
 
-    def plist():
-        cp(T.OP[:], P16, ["SP"], ["OP0", "OP1"])
+    def alist(h):
+        red(T.OFF[:, 16 * h:16 * h + 16], hbank[h][0][:, 0:16, :], A.max, [hbank[h][1]], ["OFF%d" % h])
 
-    def qlist():
-        cp(T.OQ[:], Q16, ["SQ"], ["OQ"])
+    def take_p(h):
+        scan(T.SP[:, wide[h]], T.NDM[:, 0:128], T.GP[:, wide[h]], 0.0, A.mult, A.add, ["NDM", "GP%d" % h], ["SP%d" % h])
+
+    def take_q(h):
+        scan(T.SQ[:, wide[h]], T.GQ[:, wide[h]], T.HK[:], 0.0, A.min, A.add, ["HK", "GQ%d" % h], ["SQ%d" % h])
+
+    def plist(h):
+        ts(T.OP[:, thin[h]], T.SP[:, ends[h]], 32.0, A.mult, ["SP%d" % h], ["OP%d" % h])
+
+    def qlist(h):
+        cp(T.OQ[:, thin[h]], T.SQ[:, ends[h]], ["SQ%d" % h], ["OQ%d" % h])
 
     def product():
-        tt(T.PQ[:], P16, Q16, A.mult, ["SP", "SQ"], ["PQ"])
+        tt(T.FI[:], P16, Q16, A.mult, ["SP0", "SP1", "SQ0", "SQ1"], ["FI"])
+
+    def r_open(h):
+        mm(rbank[h][0][:, 0:16 * nblk[h]], idm(0), T.C1024[:, 0:16 * nblk[h]], True, False, ["ID0", "C1024"], [rbank[h][1]])
 
     def cpart(which, h):
         bank, key = rbank[h]
         for m in range(CA * h, CA if h == 0 else 16):
             o = bank[:, 16 * (m - CA * h):16 * (m - CA * h) + 16]
             if which == "P":
-                mm(o, T.KM[:, 128 * m:128 * (m + 1)], P16, False, False, ["KM%d" % m, "SP"], [key])
+                mm(o, T.KM[:, 128 * m:128 * (m + 1)], P16, False, False, ["KM%d" % m, "SP0", "SP1"], [key])
             else:
-                mm(o, idm(m), Q16, False, m in (CA - 1, 15), ["ID%d" % m, "SQ"], [key])
+                mm(o, idm(m), Q16, False, m in (CA - 1, 15), ["ID%d" % m, "SQ0", "SQ1"], [key])
 
     def xp(h):
         act(T.XP[:, wide[h]], XW.indirect(T.OP[:, thin[h]]), F.Copy, ["X", "OP%d" % h], ["XP%d" % h])
 
+    def vxp(h):
+        cp(T.XP[:, wide[h]], XW.indirect(T.OP[:, thin[h]]), ["X", "OP%d" % h], ["XP%d" % h])
+
     def ysum(h):
-        tt(T.YS[:, wide[h]], XW.indirect(T.OQ[:, thin[h]]), T.XP[:, wide[h]], A.add, ["X", "OQ", "XP%d" % h], ["YS%d" % h])
+        tt(T.YS[:, wide[h]], XW.indirect(T.OQ[:, thin[h]]), T.XP[:, wide[h]], A.add, ["X", "OQ%d" % h, "XP%d" % h], ["YS%d" % h])
 
     def yand(h):
         ts(T.YI[:, wide[h]], T.YS[:, wide[h]], 255, A.bitwise_and, ["YS%d" % h], ["YI%d" % h])
@@ -347,11 +372,8 @@ def rank_program(g, core, T, topo):
     def ytile(j):
         act(T.Y[:, 256 * j:256 * j + 256], T.YI[:], F.Copy, ["YI0", "YI1"], ["Y" + "ab"[j]])
 
-    def rr(h):
-        act(T.RR[:, blk[h]], rbank[h][0][:, 0:16 * nblk[h]], F.Copy, [rbank[h][1]], ["RR%d" % h])
-
     def csum(h):
-        tt(T.CR[:, blk[h]], T.FI[:].indirect(T.TQ[:, 0:nblk[h]]), T.RR[:, blk[h]], A.add, ["FI", "TQ", "RR%d" % h], ["CR%d" % h])
+        tt(T.CR[:, blk[h]], rbank[h][0][:, 0:16 * nblk[h]], T.RR[:, blk[h]], A.add, [rbank[h][1], "RR%d" % h], ["CR%d" % h])
 
     def cand(h):
         ts(T.C32[:, blk[h]], T.CR[:, blk[h]], 2047, A.bitwise_and, ["CR%d" % h], ["C32" + "ab"[h]])
@@ -421,7 +443,7 @@ def rank_program(g, core, T, topo):
         if j == 0:
             act(T.R0[:], T.PK0[:, 0:64], F.Copy, ["P:K0"], ["R0"])
         else:
-            tt(T.R1[:], T.PK1[:, 0:64], T.R0[:], A.min, ["P:K1", "R0"], ["R1"])
+            tt(T.R1[:], T.PK1[:, 0:16, :], T.R0[:], A.min, ["P:K1", "R0"], ["R1"])
 
     def put(k):
         tt(T.LB[:, k:256:16], cols(T.PH, 16 * k, 16 * k + 16), T.R1[:, 16 * k:16 * k + 16], A.min, ["P:H", "R1"], ["LB%d" % k])
@@ -495,56 +517,62 @@ def rank_program(g, core, T, topo):
     def erow(h):
         act(T.EB[:, cw[h]], cols(e1[h][0], 0, 16 * cn[h]), F.Copy, [e1[h][1]], ["EB%d" % h])
 
-    hash_open()
+    hash_open(1)
+    hash_open(0)
     for t in range(RO):
         Tt = TT[t]
         last = t == RO - 1
-        cp(T.G01[:, 0:256], XW.indirect(eu(t)), ["X", "EU%d" % t, "EUh%d" % t, "EUi%d" % t], ["G0"])
-        act(T.G01[:, 256:512], XW.indirect(eu(t - 1)), F.Copy, ["X", "EU%d" % (t - 1)], ["G1"])
-        hb = T.PH[:, 0:32, :]
-        for k in range(8):
-            mm(hb, sel("hn", k), T.G01[:, k:512:8], False, False, ["SELhn", "G0", "G1"], ["P:H"])
-        mm(hb, idm(0), T.M9[:], False, False, ["ID0", "M9"], ["P:H"])
-        mm(hb, idm(16), T.M9[:], False, False, ["ID16", "M9"], ["P:H"])
-        mm(hb, idm(0), T.HP[:], False, False, ["ID0", "HP0", "HP1"], ["P:H"])
-        for k in range(8):
-            mm(hb, sel("h", k), T.G01[:, k:512:8], False, k == 7, ["SELh", "G0", "G1"], ["P:H"])
-        if t == 0:
-            kaps()
-            late_scalar()
-        red(T.OFF[:], hb, A.max, ["P:H"], ["OFF"])
-        if not last:
-            ts(T.FO[:], T.OFF[:], 256.0, A.is_ge, ["OFF"], ["FO"])
-            mm(T.PK0[:, 0:32], T.ONES[:], T.FO[:], True, True, ["ONES", "FO"], ["P:K0"])
-        if t == 0:
-            late_vector()
-        for h in (0, 1):
-            mm(rbank[h][0][:, 0:16 * nblk[h]], idm(0), T.C1024[:, 0:16 * nblk[h]], True, False, ["ID0", "C1024"], [rbank[h][1]])
-        need("v", "arr%d" % t, arrivals(t))
-        need("s", "arr%d" % t, arrivals(t))
-        tk = ["T%down" % t] + ["T%de%d" % (t, u) for u in range(t)]
-        if t == 0:
-            cp(T.T0[:, 256:384], T.TH[:, 256:384], [], ["T0far"])
-            act(T.T0[:, 384:512], T.TH[:, 384:512], F.Copy, [], ["T0farb"])
-            tk += ["T0far", "T0farb"]
-        tt(T.GP[:], Tt[:, 0:512].indirect(T.OFF[:, 0:16]), T.DM[:], A.mult, tk + ["OFF", "DM"], ["GP"])
-        act(T.GQ[:], Tt[:, 0:512].indirect(T.OFF[:, 16:32]), F.Copy, tk + ["OFF"], ["GQ"], bias=-2048.0)
+        tk = ["T%down" % t] + ["T%de%d" % (t, u) for u in range(t)] + (["T0far", "T0farb"] if t == 0 else [])
         ek = ("EU%d" % (t + 1), "EUh%d" % (t + 1), "EUi%d" % (t + 1))
+        widened = []
+
+        def ga(h):
+            cp(T.G01[:, 256 * h:256 * h + 128], XW.indirect(eu(t)[:, thin[h]]), ["X", "EU%d" % t, "EUh%d" % t, "EUi%d" % t], ["GA%d" % h])
+
+        def gb(h):
+            act(T.G01[:, 256 * h + 128:256 * h + 256], XW.indirect(eu(t - 1)[:, thin[h]]), F.Copy, ["X", "EU%d" % (t - 1)], ["GB%d" % h])
+
+        def first(k):
+            if t == 0:
+                (late_scalar, late_vector, kaps)[k]()
+
+        def arrive():
+            need("v", "arr%d" % t, arrivals(t))
+            need("s", "arr%d" % t, arrivals(t))
+            if t == 0 and not widened:
+                widened.append(1)
+                cp(T.T0[:, 256:384], T.TH[:, 256:384], [], ["T0far"])
+                act(T.T0[:, 384:512], T.TH[:, 384:512], F.Copy, [], ["T0farb"])
+
+        def gp_(h):
+            arrive()
+            tt(T.GP[:, wide[h]], Tt[:, 0:512].indirect(T.OFF[:, 16 * h:16 * h + 8]), T.DM32[:], A.mult,
+               tk + ["OFF%d" % h, "DM32"], ["GP%d" % h])
+
+        def gq_(h):
+            arrive()
+            act(T.GQ[:, wide[h]], Tt[:, 0:512].indirect(T.OFF[:, 16 * h + 8:16 * h + 16]), F.Copy,
+                tk + ["OFF%d" % h], ["GQ%d" % h], bias=-2048.0)
+
+        def flags():
+            if not last:
+                ts(T.FO[:], T.OFF[:], 256.0, A.is_ge, ["OFF0", "OFF1"], ["FO"])
+                mm(T.PK0[:, 0:32], T.ONES[:], T.FO[:], True, True, ["ONES", "FO"], ["P:K0"])
 
         def count(k):
             if last:
                 return
             if k == 0:
-                red(cf(AN), T.PK0[:, 0:32], A.add, ["P:K0"], ["an"])
+                op("s", lambda: S.activation(T.FS[:], T.PK0[:, 0:32], F.Copy, bias=-15.5 / 1024, accum_out=cf(AN)),
+                   ["P:K0"], ["an", "FS"])
             elif k == 1:
-                cp(ci(8), cf(AN), ["an"], ["ai"])
-            elif k == 2:
-                ts(ci(9), ci(8), 63, A.bitwise_and, ["ai"], ["aj"])
+                act(ci(8), cf(AN), F.Copy, ["an"], ["ai"], scale=1.0 / 64, bias=16 - 31.0 / 64)
             else:
-                act(cf(AC + t + 1), ci(9), F.Copy, ["aj"], ["ac%d" % (t + 1)], bias=AOFF)
+                act(cf(AC + t + 1), ci(8), F.Identity, ["ai", "an"], ["ac%d" % (t + 1)], scale=-64.0, bias=cf(AN))
 
-        def floor_pq():
-            ts(T.FI[:], T.PQ[:], 1.0 / 32, A.mult, ["PQ", "ac%d" % t], ["FI"], cf(AC + t), A.add)
+        def ftile(h):
+            act(T.RR[:, blk[h]], T.FI[:].indirect(T.TQ[:, 0:nblk[h]]), F.Identity, ["FI", "TQ", "ac%d" % t], ["RR%d" % h],
+                bias=cf(AC + t))
 
         def elist(h):
             if not last:
@@ -566,11 +594,27 @@ def rank_program(g, core, T, topo):
         def estore():
             dmas("y", "ye%d" % t, [(T.yr[RO - 1 - t:128:16, :], T.EB[0:128:16, :], ["EB0", "EB1", "EB2"], ["yr"])])
 
-        def next_open():
+        def next_open(h):
             if not last:
-                hash_open()
+                hash_open(h)
 
-        twin_open(2); count(0); take_p(); cpart("P",0); take_q(); plist(); xp(1); xp(0); product(); qlist(); floor_pq(); ysum(1); ysum(0); cpart("Q",0); rr(0); csum(0); yand(1); yand(0); cand(0); cpart("P",1); cpart("Q",1); dense_open(2); rr(1); csum(1); cu(0); cand(1); ytile(0); dense_open(1); yneg(2,1); yneg(2,0); dense_open(0); ytile(1); sgather(4,6); xadd(4,6,1); sgather(0,2); vgather(2,3); cu(1); vgather(6,8); sabs(6,8); pabs(4,6,1); xadd(0,2,0); quad_open(); dense(1); new_open(2); vgather(3,4); sabs(2,4); vgather(10,12); pabs(0,2,0); dense(0); sabs(10,12); vgather(8,10); sabs(8,10); dense(2); vgather(12,14); sabs(12,14); quad(12); quad(13); vgather(14,15); vgather(15,16); count(1); quad(15,"qn"); fold(0); fold(1); sabs(14,15); quad(14); vrelu(15,16); put(0); put(3); put(1); put(2); pdiff(4, 6, 1); pdiff(0, 2, 0); count(2); count(3); quad(15,"q2",True); least(2); least(0); least(1); new_open(1); column(2); column(0); column(1); dlist(2); dlist(1); xe(2); colist(2); colist(0); colist(1); choose(2); choose(0); hold(2); choose(1); twin_open(0); twin_open(1); spread(2); xe_sum(2); xe(1); dlist(0); spread(0); hold(0); spread(1); twins(2, 2); twins(2, 0); xe_sum(1); twins(2, 1); twins(2, 3); hold(1); elist(0); newval(2); xe(0); erow(2); publish(); newval(1); twins(0, 3); twins(0, 4); twins(0, 2); twins(0, 5); twins(1, 2); twins(0, 0); new_open(0); twins(1, 0); twins(1, 1); twins(1, 3); pick(2); twins(0, 6); twins(0, 1); twins(0, 7); scatter(12, 4); pick(1); xe_sum(0); next_open(); newval(0); erow(0); erow(1); elist(1); estore(); elist(2); pick(0); scatter(8, 4); scatter(0, 8)
+        ga(1); gb(1); ga(0); gb(0); ages(1); ages(0); first(0); first(2); alist(1); alist(0); first(1); r_open(0); r_open(1)
+        dense_open(2); gp_(1); gq_(1); gp_(0); take_p(1); take_q(1); flags(); take_p(0); cpart("P", 0); gq_(0); plist(1); xp(1)
+        take_q(0); cpart("Q", 0); qlist(1); plist(0); product(); ftile(0); qlist(0); ftile(1); count(0); count(1); count(2)
+        vxp(0); ysum(1); ysum(0); csum(0); yand(1); yand(0); ytile(0); ytile(1); cand(0); cu(0); cpart("P", 1); cpart("Q", 1)
+        csum(1); vgather(3, 4); cand(1); quad_open(); yneg(2, 0); sgather(4, 6); sgather(0, 2); vgather(6, 8); sabs(6, 8)
+        yneg(2, 1); xadd(4, 6, 1); pabs(4, 6, 1); dense_open(1); xadd(0, 2, 0); dense_open(0); dense(1); cu(1); vgather(2, 3)
+        sabs(2, 4); pabs(0, 2, 0); dense(0); vgather(10, 12); sabs(10, 12); vgather(8, 10); sabs(8, 10); dense(2)
+        vgather(12, 14); sabs(12, 14); quad(13); vgather(14, 15); quad(12); vgather(15, 16); quad(15, "qn"); fold(0); fold(1)
+        sabs(14, 15); quad(14); vrelu(15, 16); quad(15, "q2", True); put(1); put(3); put(0); put(2)
+        least(2); least(1); least(0); twin_open(2); column(2); column(1); column(0); colist(2); colist(1); colist(0)
+        choose(2); choose(1); hold(2); pdiff(0, 2, 0); pdiff(4, 6, 1); new_open(1); new_open(2); twin_open(0); twin_open(1)
+        spread(2); choose(0); hold(1); dlist(2); xe(2); xe_sum(2); dlist(1); xe(1); spread(1); spread(0)
+        twins(2, 0); twins(2, 2); twins(2, 1); twins(2, 3); hold(0); twins(1, 3); xe_sum(1); twins(1, 1); twins(1, 0)
+        twins(1, 2); twins(0, 4); twins(1, 4); dlist(0); newval(2); publish(); elist(0); twins(0, 1); twins(1, 5); xe(0)
+        newval(1); erow(2); erow(1); pick(2); twins(0, 0); twins(0, 3); twins(0, 2); twins(0, 5); scatter(12, 4); pick(1)
+        new_open(0); xe_sum(0); next_open(1); next_open(0); newval(0); erow(0); estore(); pick(0); scatter(6, 6)
+        elist(2); elist(1); scatter(0, 6)
 
     dmas("y", "yxa", [(T.yx[0:64, :], T.X[0:64, 0:2048], ["X"], ["yxa"])])
     dmas("s", "yxb", [(T.yx[64:128, :], T.X[64:128, 0:2048], ["X"], ["yxb"])])

from concourse.bass import DstId, RemoteDMATransfer
from concourse.mybir import AluOpType as A, AxisListType, ActivationFunctionType as F

N, RO = 8, 4
CH = ((0, 6), (6, 12), (12, 16))
KS = (6, 6, 4)
CA = 8
QB = 12
BF, H, FL, I32, U16 = "bfloat16", "float16", "float32", "int32", "uint16"


def _sb(n, d):
    return ("sbuf", [128, n], d)


SCRATCH = {
    "X": _sb(2048 + 256, BF), "RI": _sb(288, I32), "WI": _sb(1, I32), "KI": _sb(1, I32),
    "RF": _sb(256, FL), "TR": _sb(544, I32), "TL": _sb(16, U16), "TH": _sb(512, H),
    "T0": _sb(560, FL), "T1": _sb(560, FL), "T2": _sb(560, FL), "T3": _sb(560, FL),
    "CI": _sb(16, I32), "CF": _sb(32, FL), "AGE": _sb(16, I32),
    "JL": _sb(256, BF), "IG": _sb(256, BF), "H2": _sb(64, BF), "J": _sb(192, BF), "J4": _sb(128, BF),
    "SEL": _sb(6 * 144, BF), "ONES": _sb(128, BF), "C1024": _sb(192, BF), "C248": _sb(64, BF), "MG": _sb(128, BF), "M9": _sb(64, BF),
    "DM": _sb(256, BF), "NDM": _sb(256, BF), "DM32": _sb(128, BF), "HK": _sb(128, BF), "HL": _sb(256, BF),
    "BON": _sb(128, BF), "B4K": _sb(128, BF),
    "ID": _sb(18 * 128, BF), "KM": _sb(2048, H), "KD": _sb(16, H),
    "HP": _sb(128, H), "HQ": _sb(64, BF), "HC": _sb(128, BF), "KB": _sb(64, BF), "KT": _sb(256, BF), "KL": _sb(128, BF),
    "NBG": ("sbuf", [128, 8, 17], H), "TQ": _sb(16, U16),
    "EU": _sb(96, U16), "G01": _sb(512, BF), "OFF": _sb(32, U16), "FO": _sb(32, BF), "FS": _sb(32, FL),
    "GP": _sb(256, H), "SP": _sb(256, H), "GQ": _sb(256, H), "SQ": _sb(256, H),
    "OP": _sb(16, U16), "OQ": _sb(16, U16), "FI": _sb(16, FL),
    "XP": _sb(256, BF), "YS": _sb(256, I32), "YI": _sb(256, I32), "Y": _sb(512, BF),
    "RR": _sb(256, I32), "CR": _sb(256, I32), "C32": _sb(256, I32), "CU": _sb(256, U16),
    "D": _sb(4096, BF), "AB": _sb(4096, BF),
    "R0": _sb(64, FL), "R1": _sb(64, FL), "LB": _sb(256, FL), "SC": _sb(256, I32),
    "MA": _sb(16, I32), "OM": _sb(16, U16), "OD": _sb(16, U16),
    "GE": _sb(256, H), "SE": _sb(256, H), "EQ": _sb(256 * 8, BF), "OS": _sb(16, U16),
    "XE": _sb(256, H), "NX": _sb(256, BF), "EB": _sb(256, FL),
}
for _n in ("PC0", "PC1", "PK0"):
    SCRATCH[_n] = ("psum", [128, 512], FL)
for _n in ("PH", "PK1"):
    SCRATCH[_n] = ("psum", [128, 128, 4], FL)
for _n in ("PD0", "PD1", "PY"):
    SCRATCH[_n] = ("psum", [128, 16, 32], FL)

SEMAPHORES = (["v", "s", "p", "gp", "sent", "lr", "lx", "lw", "lk", "cp", "yr0", "yxa", "yxb"]
              + ["arr%d" % k for k in range(RO)] + ["ce%d" % k for k in range(RO)] + ["ye%d" % k for k in range(RO)])

MAGIC = 12582912.0


def rank_program(g, core, T, topo):
    rank = T.rank_of(core)
    if rank is None:
        return
    Q = {"v": g.vector, "s": g.scalar, "p": g.tensor, "gp": g, "y": g.sync}
    cnt = {}
    waited = {}
    lastw = {}
    readers = {}

    def need(q, sem, val):
        if waited.get((q, sem), 0) < val:
            Q[q].wait_ge(T.sem[sem], val)
            waited[(q, sem)] = val

    def deps(q, r, w):
        for k in r:
            t = lastw.get(k)
            if t and not (t[0] == q and (q == "p" or not t[3])):
                need(q, t[1], t[2])
        for k in w:
            t = lastw.get(k)
            if t and not (t[0] == q and (q == "p" or not t[3])):
                need(q, t[1], t[2])
            for t in readers.get(k, []):
                if not (t[0] == q == "p"):
                    need(q, t[1], t[2])

    def note(q, sem, val, r, w):
        for k in r:
            if k[:2] == "P:":
                lastw[k] = (q, sem, val, False)
            else:
                readers.setdefault(k, []).append((q, sem, val))
        for k in w:
            lastw[k] = (q, sem, val, True)
            readers[k] = []

    def op(q, fn, r, w):
        deps(q, r, w)
        cnt[q] = cnt.get(q, 0) + 1
        fn().then_inc(T.sem[q], 1)
        note(q, q, cnt[q], r, w)

    def dmas(q, sem, items):
        for o, i, r, w in items:
            deps(q, r, w)
        for o, i, r, w in items:
            Q[q].dma_start(o, i).then_inc(T.sem[sem], 16)
        cnt[sem] = cnt.get(sem, 0) + 16 * len(items)
        for o, i, r, w in items:
            note("dma", sem, cnt[sem], r, w)

    V, S, P = g.vector, g.scalar, g.tensor

    def cp(o, i, r, w):
        op("v", lambda: V.tensor_copy(o, i), r, w)

    def ts(o, i, s1, o1, r, w, s2=None, o2=None):
        if o2 is None:
            op("v", lambda: V.tensor_scalar(o, i, s1, None, o1), r, w)
        else:
            op("v", lambda: V.tensor_scalar(o, i, s1, s2, o1, o2), r, w)

    def tt(o, a, b, o1, r, w):
        op("v", lambda: V.tensor_tensor(o, a, b, o1), r, w)

    def scan(o, d0, d1, init, o0, o1, r, w):
        op("v", lambda: V.tensor_tensor_scan(o, d0, d1, init, o0, o1), r, w)

    def red(o, i, how, r, w):
        op("v", lambda: V.tensor_reduce(o, i, AxisListType.X, how), r, w)

    def ms(o, c, w):
        op("v", lambda: V.memset(o, c), [], w)

    def act(o, i, f, r, w, bias=0.0, scale=1.0):
        op("s", lambda: S.activation(o, i, f, bias=bias, scale=scale), r, w)

    def mm(o, l, x, st, sp, r, w):
        op("p", lambda: P.matmul(o, l, x, st, sp), r, w)

    def iota(o, pat, base, cm, w, small=True):
        if small:
            op("gp", lambda: g.iota(o, pat, base, cm, allow_small_or_imprecise_dtypes=True), [], w)
        else:
            op("gp", lambda: g.iota(o, pat, base, cm), [], w)

    TT = [T.T0, T.T1, T.T2, T.T3]
    XW = T.X[:, 0:2048]

    def ci(k):
        return T.CI[:, k:k + 1]

    def cf(k):
        return T.CF[:, k:k + 1]

    def cols(bank, a, b):
        return bank[:, a // 4:b // 4, :] if bank.name in ("PH", "PK1") else bank[:, a:b]

    def idm(k):
        return T.ID[:, 128 * k:128 * (k + 1)]

    SELS = {"d": (0, 16, 256.0), "q2": (1, 4, 512.0), "qn": (2, 4, -256.0), "h": (3, 4, None), "q": (4, 4, 256.0),
            "hn": (5, 4, None)}

    def sel(which, k):
        a, n, _ = SELS[which]
        return T.SEL[:, 144 * a + n - 1 - k:144 * a + n - 1 - k + 128]

    def make_sel(which, factor=None, r=()):
        a, n, c = SELS[which]
        ts(T.SEL[:, 144 * a + n - 1:144 * a + 128:n], T.IG[:, 0:128:n], cf(GF), A.is_equal, ["IG", "gf"] + list(r),
           ["SEL" + which], c if factor is None else factor, A.mult)

    def peer(s):
        return T.cores[(rank - 1 - s) % N]

    def send(items, r):
        for k in r:
            t = lastw[k]
            need("gp", t[1], t[2])
        trs, tot = [], 0
        for j, (s, src, dst) in enumerate(items):
            d = peer(s)
            eng = topo.engines(core, d)
            n = share(len(items), len(eng))
            mask = 0
            for e in eng[j * n:(j + 1) * n]:
                mask += 1 << e
            rid, pid = topo.addr(d, core)
            trs.append(RemoteDMATransfer(dst_ids=[DstId(rid=rid, pnc=pid)], dma_engine_mask=mask,
                                         remote_sem=T.sem["arr%d" % s], src=src, dst=dst))
            tot += n
        g.remote_dma_fused(trs, local_sem=T.sem["sent"])
        cnt["sent"] = cnt.get("sent", 0) + tot

    def share(k, n):
        m = 1
        while 2 * m * k <= n:
            m *= 2
        return m

    def arrivals(s):
        n = len(topo.engines(T.cores[(rank + 1 + s) % N], core))
        if s == 0:
            return share(1, n)
        return share(RO - 1, n) + share(1, n) + sum(share(RO - 2 - t, n) for t in range(s - 1))

    dmas("y", "lr", [(T.RI[:, 16:272], T.ring[:], [], ["RI"])])
    dmas("y", "lw", [(T.WI[:], T.wt[:], [], ["WI"])])
    dmas("y", "lk", [(T.KI[:], T.kap[:], [], ["KI"])])
    dmas("y", "lx", [(XW, T.x[:], [], ["X"])])

    iota(ci(0), [[0, 1]], 0, 1, ["q"], small=False)
    iota(T.AGE[:], [[1, 16]], 0, 0, ["AGE"], small=False)
    iota(T.JL[:], [[0, 16], [1, 16]], 0, 0, ["JL"])
    iota(T.IG[:], [[1, 16], [0, 16]], 0, 0, ["IG"])
    iota(T.H2[:], [[0, 16], [1, 4]], 0, 0, ["H2"])
    for k in (0, 1):
        iota(T.HC[:, 64 * k:64 * k + 64], [[0, 2], [1, 8], [0, 4]], 8 * k, 0, ["HC%d" % k])
    iota(T.KT[0:32, :], [[0, 16], [1, 4], [0, 4]], 0, 0, ["KTa"])
    iota(T.J4[:], [[0, 8], [1, 4], [0, 4]], 0, 0, ["J4"])
    GF, PF, B1, B2, W16, W16N, P4, QF, KF, AN, AC = 0, 1, 3, 4, 5, 6, 7, 9, 10, 11, 12
    QQ, S1, S2, S3, S4 = 20, 21, 22, 23, 24
    ms(T.SEL[:], 0.0, ["SEL" + k for k in SELS])
    act(T.LB[:], T.SEL[:, 0:256], F.Copy, ["SELd", "SELq2"], ["LB0", "LB1", "LB2", "LB3"], bias=67108864.0)
    for buf, key, c in ((T.ONES[:], "ONES", 1.0), (T.C1024[:], "C1024", 1024.0), (T.MG[:], "MG", MAGIC), (T.C248[:], "C248", 248.0),
                        (T.M9[:], "M9", MAGIC * 512)):
        act(buf, T.SEL[:, 0:buf.shape[1]], F.Copy, ["SELd", "SELq2"], [key], bias=c)
    ts(ci(1), ci(0), 4, A.arith_shift_right, ["q"], ["g32"])
    ts(ci(2), ci(0), 15, A.bitwise_and, ["q"], ["p32"])
    ms(T.RI[:, 0:16], 0, ["RIa"])
    ms(T.RI[:, 272:288], 0, ["RIb"])
    tt(ci(4), ci(0), ci(1), A.add, ["q", "g32"], ["t32"])
    cp(cf(PF), ci(2), ["p32"], ["pf"])
    ms(cf(AC), -1024.0 - 15.5 / 32, ["ac0"])
    ts(ci(5), ci(4), 1, A.bitwise_and, ["t32"], ["b0"])
    cp(cf(GF), ci(1), ["g32"], ["gf"])
    ts(cf(B1), cf(PF), 16.0, A.mult, ["pf"], ["b1"])
    ts(ci(6), ci(2), 2, A.arith_shift_right, ["p32"], ["p4i"])
    ts(cf(B2), ci(5), 272.0, A.mult, ["b0", "b1"], ["b2"], cf(B1), A.add)
    ts(T.TL[:], T.AGE[:], cf(B2), A.add, ["AGE", "b2"], ["TL"])
    op("v", lambda: V.transpose(T.TR[:, 0:256], T.RI[:, 16:272]), ["RI"], ["TRa"])
    op("v", lambda: V.transpose(T.TR[:, 256:544], T.RI[:]), ["RI", "RIa", "RIb"], ["TRb"])
    ts(T.DM[:], T.JL[:, 0:256], cf(PF), A.is_equal, ["JL", "pf"], ["DM"])
    ts(T.BON[:], T.IG[:, 0:128], cf(GF), A.is_equal, ["IG", "gf"], ["BON"])
    cp(T.TH[:, 0:128], T.TR[:].indirect(T.TL[:, 0:8]), ["TRa", "TRb", "TL"], ["TH"])
    act(T.TH[:, 128:256], T.TR[:].indirect(T.TL[:, 8:16]), F.Copy, ["TRa", "TRb", "TL"], ["THb"])
    send([(0, T.TH[:, 0:256], T.TH[:, 256:512])], ["TH", "THb"])
    act(T.T0[:, 0:256], T.TR[:].indirect(T.TL[:]), F.Copy, ["TRa", "TRb", "TL"], ["T0own"])
    iota(T.J[:], [[1, 192]], 0, 0, ["J"])
    need("gp", "gp", cnt["gp"])
    iota(T.KT[32:64, :], [[-1, 16], [0, 16]], 15, 0, ["KTb"])
    need("gp", "gp", cnt["gp"])
    iota(T.KT[64:96, :], [[1, 16], [0, 4], [16, 4]], 16 * QB, 0, ["KTc"])
    need("gp", "arr0", arrivals(0))
    send([(s, T.T0[:, 0:256], TT[s][:, 256 + 16 * s:512 + 16 * s]) for s in range(1, RO)], ["T0own"])
    need("y", "arr0", arrivals(0))
    dmas("y", "cp", [(TT[s][:, 16 * s:256], T.T0[:, 0:256 - 16 * s], ["T0own"], ["T%down" % s]) for s in range(1, RO)])

    cp(cf(P4), ci(6), ["p4i"], ["p4"])
    ts(cf(W16), T.WI[:], 16.0, A.mult, ["WI"], ["w16"])
    ts(cf(W16N), T.WI[:], -16.0, A.mult, ["WI"], ["w16n"])
    tt(idm(0), T.DM[:, 0:128], T.BON[:], A.mult, ["DM", "BON"], ["ID0"])
    ts(cf(QF), cf(PF), -1.0, A.add, ["pf"], ["qf"])
    ts(cf(S3), cf(PF), 2.0, A.mult, ["pf"], ["s3"], 2048.0, A.add)
    ts(T.HQ[:], T.H2[:], cf(P4), A.not_equal, ["H2", "p4"], ["HQ"], -1024.0, A.mult)
    cp(T.EU[:, 64:96], T.TH[:, 0:32], ["TH"], ["EU0", "EU-1"])
    make_sel("h", cf(W16), ["w16"])
    make_sel("hn", cf(W16N), ["w16n"])
    act(idm(16), idm(0), F.Copy, ["ID0"], ["ID16"], scale=-1.0)
    for k in (0, 1):
        tt(T.HP[:, 64 * k:64 * k + 64], T.HQ[:], T.HC[:, 64 * k:64 * k + 64], A.add, ["HQ", "HC%d" % k], ["HP%d" % k])
    cp(cf(KF), T.KI[:], ["KI"], ["kf"])
    ts(T.HK[:], T.JL[:, 0:128], 15.0, A.is_equal, ["JL"], ["HK"], 4096.0, A.mult)
    ts(T.HL[:, 0:128], T.JL[:, 0:128], cf(QF), A.is_equal, ["JL", "qf"], ["HL"], 2048.0, A.mult)
    ts(T.KD[:], T.DM[:, 0:16], cf(KF), A.mult, ["DM", "kf"], ["KD"], 32.0, A.mult)
    mm(T.PK0[:, 0:16], T.BON[:], T.KD[:], True, True, ["BON", "KD"], ["P:K0"])
    ts(T.HL[:, 128:256], T.JL[:, 0:128], cf(PF), A.is_equal, ["JL", "pf"], ["HM"], -2048.0, A.mult)
    mm(T.PY[:, 0:4, :], idm(0), T.HK[:], True, False, ["ID0", "HK"], ["P:Y"])
    mm(T.PY[:, 0:4, :], idm(0), T.HL[:, 0:128], False, False, ["ID0", "HL"], ["P:Y"])
    mm(T.PY[:, 0:4, :], idm(0), T.HL[:, 128:256], False, True, ["ID0", "HM"], ["P:Y"])

    def late_scalar():
        act(T.NDM[:], T.DM[:], F.Copy, ["DM"], ["NDM"], scale=-1.0, bias=1.0)
        act(T.DM32[:], T.DM[:, 0:128], F.Copy, ["DM"], ["DM32"], scale=1.0 / 32)
        act(T.HK[:], T.PY[:, 0:4, :], F.Copy, ["P:Y"], ["HK"])
        for m in range(1, 16):
            act(idm(m), idm(0), F.Copy, ["ID0"], ["ID%d" % m], scale=float(2 * m + 1))
        act(idm(17), idm(0), F.Copy, ["ID0"], ["ID17"], scale=0.5)
        act(T.KB[:], T.JL[:, 0:64], F.Copy, ["JL"], ["KB"], scale=-1048576.0, bias=15728640.0)
        act(T.B4K[:], T.BON[:], F.Copy, ["BON"], ["B4K"], scale=4096.0)
        act(T.NBG[:, :, 0:16], T.DM[:, 0:128], F.Copy, ["DM"], ["NBG"], scale=-36864.0, bias=32768.0)
        act(T.RF[:], T.RI[:, 16:272], F.Copy, ["RI"], ["RFa"])
        dmas("y", "yr0", [(T.yr[4:128, :], T.RF[0:124, 0:256], ["RFa"], ["yr"])])

    def kaps():
        for m in range(16):
            ts(T.KM[:, 128 * m:128 * (m + 1)], idm(0), T.PK0[:, m:m + 1], A.mult, ["ID0", "P:K0"], ["KM%d" % m])

    def late_vector():
        for k in ("d", "q2", "qn", "q"):
            make_sel(k)
        ts(T.NBG[:, :, 16], T.IG[:, 0:128:16], 32.0, A.mult, ["IG", "s3"], ["NBGb"], cf(S3), A.add)
        cp(cf(QQ), ci(0), ["q"], ["qq"])
        ts(cf(S1), ci(0), 32.0, A.is_equal, ["q"], ["s1"], 1048576.0, A.mult)
        ts(T.TQ[:], T.JL[:, 0:256:16], cf(PF), A.add, ["JL", "pf"], ["TQ"])
        ts(T.KT[0:32, :], T.KT[0:32, :], T.CF[0:32, QQ:QQ + 1], A.not_equal, ["KTa", "qq"], ["KTa"], 33554432.0, A.mult)
        ts(cf(S2), ci(0), 64.0, A.is_equal, ["q", "s1"], ["s2"], cf(S1), A.add)
        ts(T.KL[:], T.J4[:], cf(QQ), A.is_equal, ["J4", "qq", "s2"], ["KL"], cf(S2), A.add)

    def eu(k):
        return T.EU[:, 64 - 16 * k:80 - 16 * k]

    wide = (slice(0, 128), slice(128, 256))
    thin = (slice(0, 8), slice(8, 16))
    ends = (slice(15, 128, 16), slice(143, 256, 16))
    P16, Q16 = T.SP[:, 15:256:16], T.SQ[:, 15:256:16]
    hbank = ((T.PH, "P:H"), (T.PK1, "P:K1"))
    rbank = ((T.PC0, "P:C0"), (T.PC1, "P:C1"))
    blk = (slice(0, 16 * CA), slice(16 * CA, 256))
    nblk = (CA, 16 - CA)

    def hash_open(h):
        mm(hbank[h][0][:, 0:16, :], idm(0), T.C248[:], True, False, ["ID0", "C248"], [hbank[h][1]])

    def ages(h):
        hb, key = hbank[h][0][:, 0:16, :], hbank[h][1]
        gk = ["GA%d" % h, "GB%d" % h]
        for k in range(4):
            mm(hb, sel("hn", k), T.G01[:, 256 * h + k:256 * h + 256:4], False, False, ["SELhn"] + gk, [key])
        mm(hb, idm(0), T.M9[:], False, False, ["ID0", "M9"], [key])
        mm(hb, idm(16), T.M9[:], False, False, ["ID16", "M9"], [key])
        mm(hb, idm(0), T.HP[:, 64 * h:64 * h + 64], False, False, ["ID0", "HP%d" % h], [key])
        for k in range(4):
            mm(hb, sel("h", k), T.G01[:, 256 * h + k:256 * h + 256:4], False, k == 3, ["SELh"] + gk, [key])

    def alist(h):
        red(T.OFF[:, 16 * h:16 * h + 16], hbank[h][0][:, 0:16, :], A.max, [hbank[h][1]], ["OFF%d" % h])

    def take_p(h):
        scan(T.SP[:, wide[h]], T.NDM[:, 0:128], T.GP[:, wide[h]], 0.0, A.mult, A.add, ["NDM", "GP%d" % h], ["SP%d" % h])

    def take_q(h):
        scan(T.SQ[:, wide[h]], T.GQ[:, wide[h]], T.HK[:], 0.0, A.min, A.add, ["HK", "GQ%d" % h], ["SQ%d" % h])

    def plist(h):
        ts(T.OP[:, thin[h]], T.SP[:, ends[h]], 32.0, A.mult, ["SP%d" % h], ["OP%d" % h])

    def qlist(h):
        cp(T.OQ[:, thin[h]], T.SQ[:, ends[h]], ["SQ%d" % h], ["OQ%d" % h])

    def product():
        tt(T.FI[:], P16, Q16, A.mult, ["SP0", "SP1", "SQ0", "SQ1"], ["FI"])

    def r_open(h):
        mm(rbank[h][0][:, 0:16 * nblk[h]], idm(0), T.C1024[:, 0:16 * nblk[h]], True, False, ["ID0", "C1024"], [rbank[h][1]])

    def cpart(which, h):
        bank, key = rbank[h]
        for m in range(CA * h, CA if h == 0 else 16):
            o = bank[:, 16 * (m - CA * h):16 * (m - CA * h) + 16]
            if which == "P":
                mm(o, T.KM[:, 128 * m:128 * (m + 1)], P16, False, False, ["KM%d" % m, "SP0", "SP1"], [key])
            else:
                mm(o, idm(m), Q16, False, m in (CA - 1, 15), ["ID%d" % m, "SQ0", "SQ1"], [key])

    def xp(h):
        act(T.XP[:, wide[h]], XW.indirect(T.OP[:, thin[h]]), F.Copy, ["X", "OP%d" % h], ["XP%d" % h])

    def vxp(h):
        cp(T.XP[:, wide[h]], XW.indirect(T.OP[:, thin[h]]), ["X", "OP%d" % h], ["XP%d" % h])

    def ysum(h):
        tt(T.YS[:, wide[h]], XW.indirect(T.OQ[:, thin[h]]), T.XP[:, wide[h]], A.add, ["X", "OQ%d" % h, "XP%d" % h], ["YS%d" % h])

    def yand(h):
        ts(T.YI[:, wide[h]], T.YS[:, wide[h]], 255, A.bitwise_and, ["YS%d" % h], ["YI%d" % h])

    def ytile(j):
        act(T.Y[:, 256 * j:256 * j + 256], T.YI[:], F.Copy, ["YI0", "YI1"], ["Y" + "ab"[j]])

    def csum(h):
        tt(T.CR[:, blk[h]], rbank[h][0][:, 0:16 * nblk[h]], T.RR[:, blk[h]], A.add, [rbank[h][1], "RR%d" % h], ["CR%d" % h])

    def cand(h):
        ts(T.C32[:, blk[h]], T.CR[:, blk[h]], 2047, A.bitwise_and, ["CR%d" % h], ["C32" + "ab"[h]])

    def cu(h):
        cp(T.CU[:, blk[h]], T.C32[:, blk[h]], ["C32" + "ab"[h]], ["CU" + "ab"[h]])

    kbank = ((T.PK0, "P:K0"), (T.PK1, "P:K1"), (T.PH, "P:H"))
    dbank = ((T.PD0, "P:D0"), (T.PD1, "P:D1"))

    def dk(a, b):
        return ["D%d" % m for m in range(a, b)]

    def ak(a, b):
        return ["AB%d" % m for m in range(a, b)]

    def cuk(a, b):
        return (["CUa"] if a < CA else []) + (["CUb"] if b > CA else [])

    def vgather(a, b):
        y, yk = (T.YI[:], ["YI0", "YI1"]) if b - a == 1 else (T.Y[:], ["Ya", "Yb"])
        tt(T.D[:, 256 * a:256 * b], XW.indirect(T.CU[:, 16 * a:16 * b]), y, A.subtract, ["X"] + yk + cuk(a, b), dk(a, b))

    def vrelu(a, b):
        ts(T.AB[:, 256 * a:256 * b], T.D[:, 256 * a:256 * b], 0.0, A.max, dk(a, b), ak(a, b))

    def sabs(a, b):
        act(T.AB[:, 256 * a:256 * b], T.D[:, 256 * a:256 * b], F.Abs, dk(a, b), ak(a, b))

    def sgather(a, b):
        act(T.D[:, 256 * a:256 * b], XW.indirect(T.CU[:, 16 * a:16 * b]), F.Copy, ["X"] + cuk(a, b), dk(a, b))

    def yneg(n, j):
        for k in range(n):
            mm(dbank[j][0][:, 8 * k:8 * k + 8, :], idm(16), T.Y[:, 0:256], k == 0, False, ["ID16", "Ya"], [dbank[j][1]])

    def xadd(a, b, j):
        mm(dbank[j][0][:, 0:8 * (b - a), :], idm(0), T.D[:, 256 * a:256 * b], False, True, ["ID0"] + dk(a, b), [dbank[j][1]])

    def pabs(a, b, j):
        act(T.AB[:, 256 * a:256 * b], dbank[j][0][:, 0:8 * (b - a), :], F.Abs, [dbank[j][1]], ak(a, b))

    def pdiff(a, b, j):
        act(T.D[:, 256 * a:256 * b], dbank[j][0][:, 0:8 * (b - a), :], F.Copy, [dbank[j][1]], dk(a, b))

    def dense_open(j):
        bank, key = kbank[j]
        mm(cols(bank, 0, 64), idm(0), T.KB[:], True, False, ["ID0", "KB"], [key])
        mm(cols(bank, 0, 64), idm(0), T.J[:, 64 * j:64 * j + 64], False, False, ["ID0", "J"], [key])

    def dense(j):
        bank, key = kbank[j]
        for p in range(16):
            mm(cols(bank, 0, 64), sel("d", p), T.AB[:, 1024 * j + p:1024 * (j + 1):16], False, p == 15,
               ["SELd"] + ak(4 * j, 4 * j + 4), [key])

    def quad_open():
        mm(T.PC0[:, 0:256], T.KL[0:96, :], T.KT[0:96, :], True, False, ["KL", "KTa", "KTb", "KTc"], ["P:C0"])

    def quad(m, which="q", stop=False):
        src, rk = (T.D, dk(m, m + 1)) if which == "qn" else (T.AB, ak(m, m + 1))
        for k in range(4):
            mm(T.PC0[:, m - QB:256:4], sel(which, k), src[:, 256 * m + k:256 * m + 256:4], False,
               stop and k == 3, ["SEL" + which] + rk, ["P:C0"])

    def fold(j):
        if j == 0:
            act(T.R0[:], T.PK0[:, 0:64], F.Copy, ["P:K0"], ["R0"])
        else:
            tt(T.R1[:], T.PK1[:, 0:16, :], T.R0[:], A.min, ["P:K1", "R0"], ["R1"])

    def put(k):
        tt(T.LB[:, k:256:16], cols(T.PH, 16 * k, 16 * k + 16), T.R1[:, 16 * k:16 * k + 16], A.min, ["P:H", "R1"], ["LB%d" % k])

    e1 = kbank
    cb = ((T.PD1, "P:D1"), (T.PD0, "P:D0"), (T.PY, "P:Y"))
    nb2 = ((T.PC1, "P:C1"), (T.PC0, "P:C0"), (T.PC1, "P:C1"))
    cn = [b - a for a, b in CH]
    cw = [slice(16 * a, 16 * b) for a, b in CH]
    ct = [slice(a, b) for a, b in CH]
    ce = [slice(16 * a + 15, 16 * b, 16) for a, b in CH]

    def new_open(h):
        mm(nb2[h][0][:, 0:16 * cn[h]], idm(0), T.Y[:, cw[h]], True, False, ["ID0", "Ya"], [nb2[h][1]])

    def twin_open(h):
        mm(cb[h][0][:, 0:cn[h], 0:17], idm(0), T.NBG[:, 0:cn[h], :], True, False, ["ID0", "NBG", "NBGb"], [cb[h][1]])

    def least(h):
        w = cw[h]
        scan(T.SC[:, w], T.LB[:, w], T.PC0[:, w], 67108864.0, A.min, A.min, ["LB0", "LB1", "LB2", "LB3", "P:C0"], ["SC%d" % h])

    def column(h):
        ts(T.MA[:, ct[h]], T.SC[:, ce[h]], 255, A.bitwise_and, ["SC%d" % h], ["MA%d" % h])

    def colist(h):
        cp(T.OM[:, ct[h]], T.MA[:, ct[h]], ["MA%d" % h], ["OM%d" % h])

    def dlist(h):
        act(T.OD[:, ct[h]], T.MA[:, ct[h]], F.Identity, ["MA%d" % h, "pf"], ["OD%d" % h], scale=16.0, bias=cf(PF))

    def choose(h):
        tt(T.GE[:, cw[h]], T.C32[:].indirect(T.OM[:, ct[h]]), T.DM[:, 0:16 * cn[h]], A.mult,
           ["C32a", "C32b", "OM%d" % h, "DM"], ["GE%d" % h])

    def spread(h):
        ge, gk = T.GE[:, cw[h]], "GE%d" % h
        mm(cols(e1[h][0], 0, 16 * cn[h]), T.BON[:], ge, True, True, ["BON", gk], [e1[h][1]])
        mm(cb[h][0][:, 0:cn[h], 0:16], T.BON[:], ge, False, False, ["BON", gk], [cb[h][1]])

    def hold(h):
        scan(T.SE[:, cw[h]], T.NDM[:, 0:16 * cn[h]], T.GE[:, cw[h]], -1.0, A.mult, A.add, ["NDM", "GE%d" % h], ["SE%d" % h])

    def twins(h, k):
        lo, hi = 16 * (CH[h][0] + k), 16 * CH[h][1]
        bank, key = e1[h]
        eq = T.EQ[:, 256 * k + lo:256 * k + hi]
        tt(eq, cols(bank, 16 * k, 16 * cn[h]), T.SE[:, lo - 16 * k:hi - 16 * k], A.is_equal, [key, "SE%d" % h], ["EQ%d%d" % (h, k)])
        mm(cb[h][0][:, k:cn[h], 0:16], T.B4K[:], eq, False, k == KS[h] - 1, ["B4K", "EQ%d%d" % (h, k)], [cb[h][1]])

    def xe(h):
        act(T.XE[:, cw[h]], T.D[:].indirect(T.OD[:, ct[h]]), F.Copy, dk(0, 16) + ["OD%d" % h], ["XE%d" % h], bias=-0.5)

    def xe_sum(h):
        bank, key = nb2[h]
        n = 16 * cn[h]
        mm(bank[:, 0:n], idm(17), T.XE[:, cw[h]], False, False, ["ID17", "XE%d" % h], [key])
        mm(bank[:, 0:n], idm(0), T.MG[:, 0:n], False, False, ["ID0", "MG"], [key])
        mm(bank[:, 0:n], idm(16), T.MG[:, 0:n], False, True, ["ID16", "MG"], [key])

    def newval(h):
        act(T.NX[:, cw[h]], nb2[h][0][:, 0:16 * cn[h]], F.Copy, [nb2[h][1]], ["NX%d" % h])

    def pick(h):
        red(T.OS[:, ct[h]], cb[h][0][:, 0:cn[h], 0:17], A.min, [cb[h][1]], ["OS%d" % h])

    def scatter(c, n):
        h = [a <= c < b for a, b in CH].index(True)
        cp(T.X[:].indirect(T.OS[:, c:c + n]), T.NX[:, 16 * c:16 * (c + n)], ["OS%d" % h, "NX%d" % h], ["X"])

    def erow(h):
        act(T.EB[:, cw[h]], cols(e1[h][0], 0, 16 * cn[h]), F.Copy, [e1[h][1]], ["EB%d" % h])

    hash_open(1)
    hash_open(0)
    for t in range(RO):
        Tt = TT[t]
        last = t == RO - 1
        tk = ["T%down" % t] + ["T%de%d" % (t, u) for u in range(t)] + (["T0far", "T0farb"] if t == 0 else [])
        ek = ("EU%d" % (t + 1), "EUh%d" % (t + 1), "EUi%d" % (t + 1))
        widened = []

        def ga(h):
            cp(T.G01[:, 256 * h:256 * h + 128], XW.indirect(eu(t)[:, thin[h]]), ["X", "EU%d" % t, "EUh%d" % t, "EUi%d" % t], ["GA%d" % h])

        def gb(h):
            act(T.G01[:, 256 * h + 128:256 * h + 256], XW.indirect(eu(t - 1)[:, thin[h]]), F.Copy, ["X", "EU%d" % (t - 1)], ["GB%d" % h])

        def first(k):
            if t == 0:
                (late_scalar, late_vector, kaps)[k]()

        def arrive():
            need("v", "arr%d" % t, arrivals(t))
            need("s", "arr%d" % t, arrivals(t))
            if t == 0 and not widened:
                widened.append(1)
                cp(T.T0[:, 256:384], T.TH[:, 256:384], [], ["T0far"])
                act(T.T0[:, 384:512], T.TH[:, 384:512], F.Copy, [], ["T0farb"])

        def gp_(h):
            arrive()
            tt(T.GP[:, wide[h]], Tt[:, 0:512].indirect(T.OFF[:, 16 * h:16 * h + 8]), T.DM32[:], A.mult,
               tk + ["OFF%d" % h, "DM32"], ["GP%d" % h])

        def gq_(h):
            arrive()
            act(T.GQ[:, wide[h]], Tt[:, 0:512].indirect(T.OFF[:, 16 * h + 8:16 * h + 16]), F.Copy,
                tk + ["OFF%d" % h], ["GQ%d" % h], bias=-2048.0)

        def flags():
            if not last:
                ts(T.FO[:], T.OFF[:], 256.0, A.is_ge, ["OFF0", "OFF1"], ["FO"])
                mm(T.PK0[:, 0:32], T.ONES[:], T.FO[:], True, True, ["ONES", "FO"], ["P:K0"])

        def count(k):
            if last:
                return
            if k == 0:
                op("s", lambda: S.activation(T.FS[:], T.PK0[:, 0:32], F.Copy, bias=-15.5 / 1024, accum_out=cf(AN)),
                   ["P:K0"], ["an", "FS"])
            elif k == 1:
                act(ci(8), cf(AN), F.Copy, ["an"], ["ai"], scale=1.0 / 64, bias=16 - 31.0 / 64)
            else:
                act(cf(AC + t + 1), ci(8), F.Identity, ["ai", "an"], ["ac%d" % (t + 1)], scale=-64.0, bias=cf(AN))

        def ftile(h):
            act(T.RR[:, blk[h]], T.FI[:].indirect(T.TQ[:, 0:nblk[h]]), F.Identity, ["FI", "TQ", "ac%d" % t], ["RR%d" % h],
                bias=cf(AC + t))

        def elist(h):
            if not last:
                act(eu(t + 1)[:, ct[h]], T.SE[:, ce[h]], F.Copy, ["SE%d" % h], [ek[h]])

        def publish():
            if last:
                return
            k1 = "T%de%d" % (t + 1, t)
            act(TT[t + 1][:, 0:16], T.SE[:, 15:256:16], F.Copy, ["SE0", "SE1", "SE2"], [k1])
            src = TT[t + 1][:, 0:16]
            far = [(s, src, TT[s][:, 256 + 16 * (s - 1 - t):272 + 16 * (s - 1 - t)]) for s in range(t + 1, RO)]
            send(far[:1], [k1])
            if t + 2 < RO:
                send(far[1:], [k1])
                dmas("y", "ce%d" % t, [(TT[s][:, 16 * (s - 1 - t):16 * (s - t)], src, [k1], ["T%de%d" % (s, t)])
                                       for s in range(t + 2, RO)])

        def estore():
            dmas("y", "ye%d" % t, [(T.yr[RO - 1 - t:128:16, :], T.EB[0:128:16, :], ["EB0", "EB1", "EB2"], ["yr"])])

        def next_open(h):
            if not last:
                hash_open(h)

        ga(1); gb(1); ga(0); gb(0); ages(1); ages(0); first(0); first(2); alist(1); alist(0); first(1); r_open(0); r_open(1)
        dense_open(2); gp_(1); gq_(1); gp_(0); take_p(1); take_q(1); flags(); take_p(0); cpart("P", 0); gq_(0); plist(1); xp(1)
        take_q(0); cpart("Q", 0); qlist(1); plist(0); product(); ftile(0); qlist(0); ftile(1); count(0); count(1); count(2)
        vxp(0); ysum(1); ysum(0); csum(0); yand(1); yand(0); ytile(0); ytile(1); cand(0); cu(0); cpart("P", 1); cpart("Q", 1)
        csum(1); vgather(3, 4); cand(1); quad_open(); yneg(2, 0); sgather(4, 6); sgather(0, 2); vgather(6, 8); sabs(6, 8)
        yneg(2, 1); xadd(4, 6, 1); pabs(4, 6, 1); dense_open(1); xadd(0, 2, 0); dense_open(0); dense(1); cu(1); vgather(2, 3)
        sabs(2, 4); pabs(0, 2, 0); dense(0); vgather(10, 12); sabs(10, 12); vgather(8, 10); sabs(8, 10); dense(2)
        vgather(12, 14); sabs(12, 14); quad(13); vgather(14, 15); quad(12); vgather(15, 16); quad(15, "qn"); fold(0); fold(1)
        sabs(14, 15); quad(14); vrelu(15, 16); quad(15, "q2", True); put(1); put(3); put(0); put(2)
        least(2); least(1); least(0); twin_open(2); column(2); column(1); column(0); colist(2); colist(1); colist(0)
        choose(2); choose(1); hold(2); pdiff(0, 2, 0); pdiff(4, 6, 1); new_open(1); new_open(2); twin_open(0); twin_open(1)
        spread(2); choose(0); hold(1); dlist(2); xe(2); xe_sum(2); dlist(1); xe(1); spread(1); spread(0)
        twins(2, 0); twins(2, 2); twins(2, 1); twins(2, 3); hold(0); twins(1, 3); xe_sum(1); twins(1, 1); twins(1, 0)
        twins(1, 2); twins(0, 4); twins(1, 4); dlist(0); newval(2); publish(); elist(0); twins(0, 1); twins(1, 5); xe(0)
        newval(1); erow(2); erow(1); pick(2); twins(0, 0); twins(0, 3); twins(0, 2); twins(0, 5); scatter(12, 4); pick(1)
        new_open(0); xe_sum(0); next_open(1); next_open(0); newval(0); erow(0); estore(); pick(0); scatter(6, 6)
        elist(2); elist(1); scatter(0, 6)

    dmas("y", "yxa", [(T.yx[0:64, :], T.X[0:64, 0:2048], ["X"], ["yxa"])])
    dmas("s", "yxb", [(T.yx[64:128, :], T.X[64:128, 0:2048], ["X"], ["yxb"])])
    for sem in sorted(cnt):
        need("gp", sem, cnt[sem])
